import numpy as np
import ml_dtypes


def mxq(x, axis, fmt="e4m3"):
    dtype, down = {"e4m3": (ml_dtypes.float8_e4m3fn, 7), "e5m2": (ml_dtypes.float8_e5m2, 14)}[fmt]
    v = np.moveaxis(np.asarray(x, np.float32).astype(ml_dtypes.bfloat16).astype(np.float64), axis, -1)
    blocks = v.reshape(v.shape[:-1] + (-1, 32))
    amax = np.abs(blocks).max(-1, keepdims=True)
    byte = np.maximum(np.where(amax > 0, np.frexp(amax)[1] - 1 + 127, 0) - down, 1)
    scale = np.exp2(byte - 127.0)
    codes = (blocks / scale).astype(np.float32).astype(dtype).astype(np.float64)
    return np.moveaxis((codes * scale).reshape(v.shape), -1, axis)


WIDE = False


def mx_kscale(k):
    if not WIDE:
        return np.ones(k)
    levels = np.array([10, -10, 5, -5, 0])
    if k % 512:
        return np.exp2(np.random.permutation(np.resize(levels, k // 32))).repeat(32)
    a = np.empty((k // 512, 16))
    for p in range(k // 512):
        a[p, :8] = np.random.permutation(np.resize(levels, 8))
        for g in range(8):
            far = levels[np.abs(levels - a[p, g]) >= 10]
            a[p, g + 8] = far[np.random.randint(len(far))]
    return np.exp2(a.ravel()).repeat(32)


def f64(x):
    return np.asarray(x).astype(np.float64)


def striped(idx):
    return np.tile(idx.reshape(-1, 16).T, (8, 1)).astype(np.uint16)


def unstriped(offs):
    return offs[:16].T.reshape(-1).astype(np.int64)


E2M1 = np.array([0.0, 0.5, 1.0, 1.5, 2.0, 3.0, 4.0, 6.0, -0.0, -0.5, -1.0, -1.5, -2.0, -3.0, -4.0, -6.0])


def pack_weight(w, fmt):
    k, n = w.shape
    w = f64(np.asarray(w, np.float32).astype(ml_dtypes.bfloat16)).reshape(k // 32, 32, n)
    amax = np.abs(w).max(1)
    if fmt == "e4m3":
        byte = np.frexp(amax)[1] - 1 + 127 - 7
    else:
        mant, ex = np.frexp(amax / 6.0)
        byte = np.where(mant > 0.5, ex, ex - 1) + 127
    byte = np.clip(np.where(amax > 0, byte, 1), 1, 254)
    scaled = (w * np.exp2(127.0 - byte)[:, None, :]).reshape(k, n).astype(np.float32)
    by_word = np.ascontiguousarray(scaled.reshape(k // 512, 128, 4, n).transpose(0, 1, 3, 2))
    if fmt == "e4m3":
        words = by_word.astype(ml_dtypes.float8_e4m3fn).view(np.uint8)
    else:
        c = by_word.astype(ml_dtypes.float4_e2m1fn).view(np.uint8) & 0xF
        words = (c[..., 0::2] | (c[..., 1::2] << 4)).reshape(k // 512, 128, 2 * n)
    return np.ascontiguousarray(words), np.ascontiguousarray(byte.astype(np.uint8).reshape(k // 512, 16, n))


def unpack_weight(words, scales, fmt):
    g, _, n = scales.shape
    words = np.ascontiguousarray(words).reshape(g, 128, n, -1)
    if fmt == "e4m3":
        vals = words.view(ml_dtypes.float8_e4m3fn).astype(np.float64)
    else:
        nib = np.empty((g, 128, n, 4), np.uint8)
        nib[..., 0::2] = words & 0xF
        nib[..., 1::2] = words >> 4
        vals = E2M1[nib]
    vals = vals * np.repeat(np.exp2(scales.astype(np.float64) - 127.0), 8, axis=1)[..., None]
    return vals.transpose(0, 1, 3, 2).reshape(g * 512, n)


def silu(v):
    return v / (1.0 + np.exp(-np.maximum(v, -700.0)))


K, T, E, C = 512, 768, 12, 128


def deal():
    first = np.random.permutation(np.repeat(np.arange(E), T // E))
    second = (first + 1 + np.random.permutation(np.repeat(np.arange(E - 1), -(-T // (E - 1)))[:T])) % E
    while np.bincount(second, minlength=E).max() != T // E:
        load = np.bincount(second, minlength=E); hi, lo = int(load.argmax()), int(load.argmin())
        t = np.flatnonzero((second == hi) & (first != lo))[0]; second[t] = lo
    slot_token = np.empty(E * C, np.int64); pos = np.empty((2, T), np.int64); fill = np.zeros(E, np.int64)
    place = np.stack([np.random.permutation(C) for _ in range(E)])
    for r, deal in enumerate((first, second)):
        for t in np.random.permutation(T):
            e = deal[t]; j = e * C + place[e, fill[e]]; fill[e] += 1; slot_token[j] = t; pos[r, t] = j
    g = np.random.uniform(0.2, 0.8, T)
    return slot_token, pos, np.stack([g, 1.0 - g])


def by_expert(wq, xq):
    return np.concatenate([wq[e].T @ xq[:, e * C:(e + 1) * C] for e in range(E)], axis=1)


def setup_inputs():
    n = np.random.standard_normal
    s = mx_kscale(K)
    slots1, pos1, g1 = deal()
    slots2, pos2, g2 = deal()
    x = pack_weight(n((K, T)) * s[:, None], "e4m3")
    w = [pack_weight(m, "e2m1") for m in n((E, K, K)) / np.sqrt(K) / s[None, :, None] * s]
    return {
        "x_words": x[0],
        "x_scales": x[1],
        "w_words": np.stack([m[0] for m in w]),
        "w_scales": np.stack([m[1] for m in w]),
        "gate1": (np.stack([np.tile(r, (128, 1)) for r in g1])).astype(np.float32),
        "gate2": (np.stack([np.tile(r, (128, 1)) for r in g2])).astype(np.float32),
        "offs": striped(slots1),
        "pos1": striped(pos1[0]),
        "pos2": striped(pos1[1]),
        "offs2": striped(slots2),
        "pos3": striped(pos2[0]),
        "pos4": striped(pos2[1]),
    }


def reference(x_words, x_scales, w_words, w_scales, gate1, gate2, offs, pos1, pos2, offs2, pos3, pos4):
    w = np.stack([unpack_weight(w_words[e], w_scales[e], "e2m1") for e in range(E)])
    idx, idx2 = unstriped(offs), unstriped(offs2)
    y = silu(by_expert(w, unpack_weight(x_words, x_scales, "e4m3")[:, idx]))
    c = sum(f64(gate1[r, :1]) * y[:, unstriped(p)] for r, p in enumerate((pos1, pos2)))
    z = silu(by_expert(w, mxq(c[:, idx2], 0, "e4m3")))
    out = sum(f64(gate2[r, :1]) * z[:, unstriped(p)] for r, p in enumerate((pos3, pos4)))
    return out

@@ -1,0 +1,192 @@
+from contextlib import ExitStack
+
+import concourse.mybir as mybir
+from concourse.masks import make_identity
+
+K, T, E, C = 512, 768, 12, 128
+S = E * C
+P = 128
+FLOPS = 2 * 2 * K * K * S
+
+F32 = mybir.dt.float32
+BF16 = mybir.dt.bfloat16
+I32 = mybir.dt.int32
+U32 = mybir.dt.uint32
+U16 = mybir.dt.uint16
+U8 = mybir.dt.uint8
+FP8X4 = mybir.dt.float8_e4m3fn_x4
+FP4X4 = mybir.dt.float4_e2m1fn_x4
+MULT = mybir.AluOpType.mult
+ADD = mybir.AluOpType.add
+SILU = mybir.ActivationFunctionType.Silu
+
+G1 = (512, 512, 384, 128)
+C1 = (384, 256, 128)
+G2 = ((512, False), (512, False), (256, False), (256, True))
+FIN = ((0, 0, 384, True), (0, 384, 768, True), (1, 0, 384, True), (1, 384, 768, True), (2, 0, 384, True), (2, 384, 768, True), (3, 0, 384, False), (3, 384, 768, False))
+WOVEN_AT = (0, 4096, 8192, 4096)
+PLANES_AT = (12288, 16384, 0)
+
+
+def starts(widths):
+    return [sum(widths[:i]) for i in range(len(widths))]
+
+
+def tile_moe_uni_silu_kernel(
+    tc, x_words, x_scales, w_words, w_scales, gate1, gate2, offs, pos1, pos2, offs2, pos3, pos4, out
+):
+    nc = tc.nc
+    with ExitStack() as ctx:
+        keep = ctx.enter_context(tc.tile_pool(name="keep", bufs=1))
+        ring = ctx.enter_context(tc.tile_pool(name="ring", bufs=3))
+        mid = ctx.enter_context(tc.tile_pool(name="mid", bufs=1))
+        ps_mm = ctx.enter_context(tc.psum_pool(name="ps_mm", bufs=4))
+        ps_t1 = ctx.enter_context(tc.psum_pool(name="ps_t1", bufs=2))
+        ps_t2 = ctx.enter_context(tc.psum_pool(name="ps_t2", bufs=2))
+
+        def load_list(src, name):
+            t = keep.tile([P, src.shape[1]], U16, name=name)
+            nc.sync.dma_start(t[:], src)
+            return t
+
+        def part(lst, a, n):
+            return lst[:, a // 16 : (a + n) // 16]
+
+        xs = keep.tile([P, T], U8, name="xs", align_bytes=64)
+        ws = keep.tile([P, E, K], U8, name="ws", align_bytes=64)
+        nc.vector.memset(xs[:].bitcast(I32), 0)
+        nc.vector.memset(ws[:].rearrange("p e n -> p (e n)").bitcast(I32), 0)
+        ident = keep.tile([P, P], F32, name="ident")
+        make_identity(nc, ident[:])
+
+        xw = keep.tile([P, T], I32, name="xw", align_bytes=64)
+        nc.sync.dma_start(xw[:], x_words[0].rearrange("p t d -> p (t d)").bitcast(I32))
+        l_offs = load_list(offs, "l_offs")
+        for r in range(4):
+            nc.sync.dma_start(xs[r:P:32, :].bitcast(I32), x_scales[0, r:16:4, :].bitcast(I32))
+        ww = []
+        for g in range(2):
+            t = keep.tile([P, 6, 2 * K], U8, name=f"ww{g}", align_bytes=64)
+            nc.sync.dma_start(
+                t[:].bitcast(I32), w_words[6 * g : 6 * g + 6, 0].rearrange("e p n -> p e n").bitcast(I32)
+            )
+            ww.append(t)
+        for r in range(4):
+            nc.sync.dma_start(
+                ws[r:P:32, :, :].bitcast(I32),
+                w_scales[:, 0, r:16:4, :].rearrange("e q n -> q e n").bitcast(I32),
+            )
+        l_pos1 = load_list(pos1, "l_pos1")
+        l_pos2 = load_list(pos2, "l_pos2")
+        gates = []
+        for i, gsrc in enumerate((gate1[0], gate1[1])):
+            t = keep.tile([P, T], F32, name=f"gate{i}")
+            nc.sync.dma_start(t[:], gsrc)
+            gates.append(t)
+        l_offs2 = load_list(offs2, "l_offs2")
+        l_pos3 = load_list(pos3, "l_pos3")
+        l_pos4 = load_list(pos4, "l_pos4")
+        for i, gsrc in enumerate((gate2[0], gate2[1])):
+            t = keep.tile([P, T], F32, name=f"gate{2 + i}")
+            nc.sync.dma_start(t[:], gsrc)
+            gates.append(t)
+
+        def experts(chunks, name, early):
+            planes = [keep.tile([P, S], F32, name=f"{name}{b}") for b in range(4)]
+            order = [(b, 0) for b in range(early)]
+            order = order + [(b, i) for b in range(4) for i in range(len(chunks)) if (b, i) not in order]
+            for b, i in order:
+                s0, n, words, scales = chunks[i]
+                acc = ps_mm.tile([P, 512], F32, name="acc")
+                for j in range(n // C):
+                    e = s0 // C + j
+                    nc.tensor.matmul_mx(
+                        out=acc[:, j * C : (j + 1) * C],
+                        lhsT=ww[e // 6][:, e % 6, 256 * b : 256 * (b + 1)].bitcast(FP4X4),
+                        lhsT_scale=ws[:, e, P * b : P * (b + 1)],
+                        rhs=words[:, j * C : (j + 1) * C].bitcast(FP8X4),
+                        rhs_scale=scales[:, j * C : (j + 1) * C],
+                        start=True,
+                        stop=True,
+                    )
+                nc.scalar.activation(planes[b][:, s0 : s0 + n], acc[:, 0:n], SILU)
+            return planes
+
+        def gated(y, lst, gate, t0, n, name):
+            a = ring.tile([P, 512], F32, name=name)
+            nc.vector.tensor_tensor(a[:, 0:n], y[:].indirect(part(lst, t0, n)), gate[:, t0 : t0 + n], MULT)
+            return a
+
+        def sum_turned(a1, a2, n):
+            bank = ps_t1.tile([P, 512], F32, name="t1")
+            for j in range(n // P):
+                cols = slice(j * P, (j + 1) * P)
+                nc.tensor.matmul(bank[:, cols], a1[:, cols], ident[:], start=True, stop=False, is_transpose=True)
+                nc.tensor.matmul(bank[:, cols], a2[:, cols], ident[:], start=False, stop=True, is_transpose=True)
+            return bank
+
+        chunks = []
+        for i, (s0, n) in enumerate(zip(starts(G1), G1)):
+            gw = keep.tile([P, n], U32, name=f"gw{i}", align_bytes=64)
+            gs = keep.tile([P, n], U8, name=f"gs{i}", align_bytes=64)
+            nc.vector.tensor_copy(gw[:], xw[:].bitcast(U32).indirect(part(l_offs, s0, n)))
+            nc.vector.tensor_copy(gs[:], xs[:].indirect(part(l_offs, s0, n)))
+            chunks.append((s0, n, gw, gs))
+        y = experts(chunks, "y", 4)
+
+        cw = [keep.tile([P, T], F32, name=f"cw{u}", align_bytes=64) for u in range(2)]
+        for i, (t0, n) in enumerate(zip(starts(C1), C1)):
+            nb = n // P
+            ct = keep.tile([P, nb, 2, 256], BF16, name=f"ct{i}", align_bytes=64)
+            for b in range(4):
+                a1 = gated(y[b], l_pos1, gates[0], t0, n, "a1")
+                a2 = gated(y[b], l_pos2, gates[1], t0, n, "a2")
+                bank = sum_turned(a1, a2, n)
+                nc.scalar.copy(
+                    ct[:, :, :, 64 * b : 64 * (b + 1)].rearrange("p k u (m e) -> p k u m e", e=2),
+                    bank[:, 0:n].rearrange("p (k m u e) -> p k u m e", m=32, u=2, e=2),
+                )
+            ctw = ct[:].bitcast(F32)
+            for u in range(2):
+                bank = ps_t2.tile([P, 512], F32, name="t2")
+                for j in range(nb):
+                    nc.tensor.transpose(bank[:, j * P : (j + 1) * P], ctw[:, j, u, :], ident[:])
+                nc.scalar.copy(cw[u][:, t0 : t0 + n], bank[:, 0:n])
+
+        chunks = []
+        widths = [w for w, st in G2]
+        for i, (s0, (n, stepped)) in enumerate(zip(starts(widths), G2)):
+            woven = mid.tile([P, n, 2], U32, name=f"woven{i}", align_bytes=64, offset=WOVEN_AT[i])
+            if stepped:
+                for u in range(2):
+                    nc.vector.tensor_copy(woven[:, :, u], cw[u][:].bitcast(U32).indirect(part(l_offs2, s0, n)))
+            else:
+                pl = mid.tile([P, 2, n], U32, name=f"pl{i}", align_bytes=64, offset=PLANES_AT[i])
+                for u in range(2):
+                    nc.vector.tensor_copy(pl[:, u, :], cw[u][:].bitcast(U32).indirect(part(l_offs2, s0, n)))
+                nc.scalar.copy(woven[:], pl[:].rearrange("p u n -> p n u"))
+            qw = keep.tile([P, n], U32, name=f"qw{i}", align_bytes=64)
+            qs = keep.tile([P, n], U8, name=f"qs{i}", align_bytes=64)
+            nc.vector.quantize_mx(
+                out=qw[:].bitcast(FP8X4), scales=qs[:], in_=woven[:].rearrange("p n u -> p (n u)").bitcast(BF16)
+            )
+            chunks.append((s0, n, qw, qs))
+        z = experts(chunks, "z", 2)
+
+        for b, t0, t1, on_pe in FIN:
+            n = t1 - t0
+            a1 = gated(z[b], l_pos3, gates[2], t0, n, "a1")
+            a2 = gated(z[b], l_pos4, gates[3], t0, n, "a2")
+            res = ring.tile([P, 512], F32, name="res")
+            if on_pe:
+                bank = sum_turned(a1, a2, n)
+                st = ring.tile([P, 512], F32, name="st")
+                nc.scalar.copy(st[:, 0:n], bank[:, 0:n])
+                bank2 = ps_t2.tile([P, 512], F32, name="t2")
+                for j in range(n // P):
+                    cols = slice(j * P, (j + 1) * P)
+                    nc.tensor.transpose(bank2[:, cols], st[:, cols], ident[:])
+                nc.scalar.copy(res[:, 0:n], bank2[:, 0:n])
+            else:
+                nc.vector.tensor_tensor(res[:, 0:n], a1[:, 0:n], a2[:, 0:n], ADD)
+            nc.sync.dma_start(out[b * P : (b + 1) * P, t0:t1], res[:, 0:n])

@@ -21,9 +21,9 @@ ADD = mybir.AluOpType.add
 SILU = mybir.ActivationFunctionType.Silu
 
 G1 = (512, 512, 384, 128)
-C1 = (384, 256, 128)
+C1 = (512, 128, 128)
 G2 = ((512, False), (512, False), (256, False), (256, True))
-FIN = ((0, 0, 384, True), (0, 384, 768, True), (1, 0, 384, True), (1, 384, 768, True), (2, 0, 384, True), (2, 384, 768, True), (3, 0, 384, False), (3, 384, 768, False))
+FIN = ((0, 0, 384, True), (0, 384, 768, True), (1, 0, 384, True), (1, 384, 768, True), (2, 0, 384, True), (2, 384, 768, False), (3, 0, 384, False), (3, 384, 768, False))
 WOVEN_AT = (0, 4096, 8192, 4096)
 PLANES_AT = (12288, 16384, 0)
 
@@ -38,7 +38,7 @@ def tile_moe_uni_silu_kernel(
     nc = tc.nc
     with ExitStack() as ctx:
         keep = ctx.enter_context(tc.tile_pool(name="keep", bufs=1))
-        ring = ctx.enter_context(tc.tile_pool(name="ring", bufs=3))
+        ring = ctx.enter_context(tc.tile_pool(name="ring", bufs=6))
         mid = ctx.enter_context(tc.tile_pool(name="mid", bufs=1))
         ps_mm = ctx.enter_context(tc.psum_pool(name="ps_mm", bufs=4))
         ps_t1 = ctx.enter_context(tc.psum_pool(name="ps_t1", bufs=2))
@@ -64,18 +64,18 @@ def tile_moe_uni_silu_kernel(
         l_offs = load_list(offs, "l_offs")
         for r in range(4):
             nc.sync.dma_start(xs[r:P:32, :].bitcast(I32), x_scales[0, r:16:4, :].bitcast(I32))
-        ww = []
-        for g in range(2):
-            t = keep.tile([P, 6, 2 * K], U8, name=f"ww{g}", align_bytes=64)
-            nc.sync.dma_start(
-                t[:].bitcast(I32), w_words[6 * g : 6 * g + 6, 0].rearrange("e p n -> p e n").bitcast(I32)
-            )
-            ww.append(t)
         for r in range(4):
             nc.sync.dma_start(
                 ws[r:P:32, :, :].bitcast(I32),
                 w_scales[:, 0, r:16:4, :].rearrange("e q n -> q e n").bitcast(I32),
             )
+        ww = []
+        for g in range(3):
+            t = keep.tile([P, 4, 2 * K], U8, name=f"ww{g}", align_bytes=64)
+            nc.sync.dma_start(
+                t[:].bitcast(I32), w_words[4 * g : 4 * g + 4, 0].rearrange("e p n -> p e n").bitcast(I32)
+            )
+            ww.append(t)
         l_pos1 = load_list(pos1, "l_pos1")
         l_pos2 = load_list(pos2, "l_pos2")
         gates = []
@@ -93,7 +93,7 @@ def tile_moe_uni_silu_kernel(
 
         def experts(chunks, name, early):
             planes = [keep.tile([P, S], F32, name=f"{name}{b}") for b in range(4)]
-            order = [(b, 0) for b in range(early)]
+            order = [(b, i) for i, nb in enumerate(early) for b in range(nb)]
             order = order + [(b, i) for b in range(4) for i in range(len(chunks)) if (b, i) not in order]
             for b, i in order:
                 s0, n, words, scales = chunks[i]
@@ -102,7 +102,7 @@ def tile_moe_uni_silu_kernel(
                     e = s0 // C + j
                     nc.tensor.matmul_mx(
                         out=acc[:, j * C : (j + 1) * C],
-                        lhsT=ww[e // 6][:, e % 6, 256 * b : 256 * (b + 1)].bitcast(FP4X4),
+                        lhsT=ww[e // 4][:, e % 4, 256 * b : 256 * (b + 1)].bitcast(FP4X4),
                         lhsT_scale=ws[:, e, P * b : P * (b + 1)],
                         rhs=words[:, j * C : (j + 1) * C].bitcast(FP8X4),
                         rhs_scale=scales[:, j * C : (j + 1) * C],
@@ -132,7 +132,7 @@ def tile_moe_uni_silu_kernel(
             nc.vector.tensor_copy(gw[:], xw[:].bitcast(U32).indirect(part(l_offs, s0, n)))
             nc.vector.tensor_copy(gs[:], xs[:].indirect(part(l_offs, s0, n)))
             chunks.append((s0, n, gw, gs))
-        y = experts(chunks, "y", 4)
+        y = experts(chunks, "y", (4, 2))
 
         cw = [keep.tile([P, T], F32, name=f"cw{u}", align_bytes=64) for u in range(2)]
         for i, (t0, n) in enumerate(zip(starts(C1), C1)):
@@ -171,7 +171,7 @@ def tile_moe_uni_silu_kernel(
                 out=qw[:].bitcast(FP8X4), scales=qs[:], in_=woven[:].rearrange("p n u -> p (n u)").bitcast(BF16)
             )
             chunks.append((s0, n, qw, qs))
-        z = experts(chunks, "z", 2)
+        z = experts(chunks, "z", (3,))
 
         for b, t0, t1, on_pe in FIN:
             n = t1 - t0

@@ -23,7 +23,7 @@ SILU = mybir.ActivationFunctionType.Silu
 G1 = (512, 512, 384, 128)
 C1 = (512, 128, 128)
 G2 = ((512, False), (512, False), (256, False), (256, True))
-FIN = ((0, 0, 384, True), (0, 384, 768, True), (1, 0, 384, True), (1, 384, 768, True), (2, 0, 384, True), (2, 384, 768, False), (3, 0, 384, False), (3, 384, 768, False))
+FIN = ((0, 0, 384, True), (0, 384, 768, True), (1, 0, 384, True), (1, 384, 768, True), (2, 0, 384, True), (2, 384, 768, False), (3, 0, 640, False), (3, 640, 768, False))
 WOVEN_AT = (0, 4096, 8192, 4096)
 PLANES_AT = (12288, 16384, 0)
 
@@ -40,9 +40,7 @@ def tile_moe_uni_silu_kernel(
         keep = ctx.enter_context(tc.tile_pool(name="keep", bufs=1))
         ring = ctx.enter_context(tc.tile_pool(name="ring", bufs=6))
         mid = ctx.enter_context(tc.tile_pool(name="mid", bufs=1))
-        ps_mm = ctx.enter_context(tc.psum_pool(name="ps_mm", bufs=4))
-        ps_t1 = ctx.enter_context(tc.psum_pool(name="ps_t1", bufs=2))
-        ps_t2 = ctx.enter_context(tc.psum_pool(name="ps_t2", bufs=2))
+        psum = ctx.enter_context(tc.psum_pool(name="psum", bufs=8))
 
         def load_list(src, name):
             t = keep.tile([P, src.shape[1]], U16, name=name)
@@ -61,9 +59,9 @@ def tile_moe_uni_silu_kernel(
 
         xw = keep.tile([P, T], I32, name="xw", align_bytes=64)
         nc.sync.dma_start(xw[:], x_words[0].rearrange("p t d -> p (t d)").bitcast(I32))
-        l_offs = load_list(offs, "l_offs")
         for r in range(4):
             nc.sync.dma_start(xs[r:P:32, :].bitcast(I32), x_scales[0, r:16:4, :].bitcast(I32))
+        l_offs = load_list(offs, "l_offs")
         for r in range(4):
             nc.sync.dma_start(
                 ws[r:P:32, :, :].bitcast(I32),
@@ -97,7 +95,7 @@ def tile_moe_uni_silu_kernel(
             order = order + [(b, i) for b in range(4) for i in range(len(chunks)) if (b, i) not in order]
             for b, i in order:
                 s0, n, words, scales = chunks[i]
-                acc = ps_mm.tile([P, 512], F32, name="acc")
+                acc = psum.tile([P, 512], F32, name="bank")
                 for j in range(n // C):
                     e = s0 // C + j
                     nc.tensor.matmul_mx(
@@ -113,12 +111,12 @@ def tile_moe_uni_silu_kernel(
             return planes
 
         def gated(y, lst, gate, t0, n, name):
-            a = ring.tile([P, 512], F32, name=name)
+            a = ring.tile([P, 640], F32, name=name)
             nc.vector.tensor_tensor(a[:, 0:n], y[:].indirect(part(lst, t0, n)), gate[:, t0 : t0 + n], MULT)
             return a
 
         def sum_turned(a1, a2, n):
-            bank = ps_t1.tile([P, 512], F32, name="t1")
+            bank = psum.tile([P, 512], F32, name="bank")
             for j in range(n // P):
                 cols = slice(j * P, (j + 1) * P)
                 nc.tensor.matmul(bank[:, cols], a1[:, cols], ident[:], start=True, stop=False, is_transpose=True)
@@ -148,7 +146,7 @@ def tile_moe_uni_silu_kernel(
                 )
             ctw = ct[:].bitcast(F32)
             for u in range(2):
-                bank = ps_t2.tile([P, 512], F32, name="t2")
+                bank = psum.tile([P, 512], F32, name="bank")
                 for j in range(nb):
                     nc.tensor.transpose(bank[:, j * P : (j + 1) * P], ctw[:, j, u, :], ident[:])
                 nc.scalar.copy(cw[u][:, t0 : t0 + n], bank[:, 0:n])
@@ -171,18 +169,18 @@ def tile_moe_uni_silu_kernel(
                 out=qw[:].bitcast(FP8X4), scales=qs[:], in_=woven[:].rearrange("p n u -> p (n u)").bitcast(BF16)
             )
             chunks.append((s0, n, qw, qs))
-        z = experts(chunks, "z", (3,))
+        z = experts(chunks, "z", (4,))
 
         for b, t0, t1, on_pe in FIN:
             n = t1 - t0
             a1 = gated(z[b], l_pos3, gates[2], t0, n, "a1")
             a2 = gated(z[b], l_pos4, gates[3], t0, n, "a2")
-            res = ring.tile([P, 512], F32, name="res")
+            res = ring.tile([P, 640], F32, name="res")
             if on_pe:
                 bank = sum_turned(a1, a2, n)
                 st = ring.tile([P, 512], F32, name="st")
                 nc.scalar.copy(st[:, 0:n], bank[:, 0:n])
-                bank2 = ps_t2.tile([P, 512], F32, name="t2")
+                bank2 = psum.tile([P, 512], F32, name="bank")
                 for j in range(n // P):
                     cols = slice(j * P, (j + 1) * P)
                     nc.tensor.transpose(bank2[:, cols], st[:, cols], ident[:])

@@ -6,6 +6,7 @@ from concourse.masks import make_identity
 K, T, E, C = 512, 768, 12, 128
 S = E * C
 P = 128
+NB = T // P
 FLOPS = 2 * 2 * K * K * S
 
 F32 = mybir.dt.float32
@@ -19,13 +20,18 @@ FP4X4 = mybir.dt.float4_e2m1fn_x4
 MULT = mybir.AluOpType.mult
 ADD = mybir.AluOpType.add
 SILU = mybir.ActivationFunctionType.Silu
+COPY = mybir.ActivationFunctionType.Copy
 
+TINY = 2.0**-60
+BANK = 2048
 G1 = (512, 512, 384, 128)
-C1 = (512, 128, 128)
+EARLY1 = ((0, 0, 4), (1, 0, 4), (0, 4, 4), (0, 8, 3), (0, 11, 1))
+EARLY2 = ((0, 0, 4), (1, 0, 4), (2, 0, 4), (0, 4, 4), (1, 4, 4), (0, 8, 2), (0, 10, 2))
 G2 = ((512, False), (512, False), (256, False), (256, True))
-FIN = ((0, 0, 384, True), (0, 384, 768, True), (1, 0, 384, True), (1, 384, 768, True), (2, 0, 384, True), (2, 384, 768, False), (3, 0, 640, False), (3, 640, 768, False))
 WOVEN_AT = (0, 4096, 8192, 4096)
 PLANES_AT = (12288, 16384, 0)
+A_SLOTS = 3
+PE_GROUPS = 5
 
 
 def starts(widths):
@@ -38,9 +44,15 @@ def tile_moe_uni_silu_kernel(
     nc = tc.nc
     with ExitStack() as ctx:
         keep = ctx.enter_context(tc.tile_pool(name="keep", bufs=1))
-        ring = ctx.enter_context(tc.tile_pool(name="ring", bufs=6))
+        first = ctx.enter_context(tc.tile_pool(name="first", bufs=1))
+        early = ctx.enter_context(tc.tile_pool(name="early", bufs=1))
         mid = ctx.enter_context(tc.tile_pool(name="mid", bufs=1))
-        psum = ctx.enter_context(tc.psum_pool(name="psum", bufs=8))
+        psum = ctx.enter_context(tc.psum_pool(name="psum", bufs=1))
+        made = []
+
+        def bank_tile(k, shape):
+            made.append(k)
+            return psum.tile(shape, F32, name=f"bank{len(made)}", offset=BANK * k)
 
         def load_list(src, name):
             t = keep.tile([P, src.shape[1]], U16, name=name)
@@ -50,18 +62,34 @@ def tile_moe_uni_silu_kernel(
         def part(lst, a, n):
             return lst[:, a // 16 : (a + n) // 16]
 
+        def spread(rcol, step, at):
+            ratio = keep.tile([P, T], F32, name=f"ratio{step}")
+            for h in range(2):
+                bank = bank_tile(at + h, [P, 384])
+                for j in range(3):
+                    nc.tensor.transpose(
+                        bank[:, j * P : (j + 1) * P], rcol[:, j, step, h : h + 1].to_broadcast([P, P]), ident[:]
+                    )
+                nc.scalar.copy(ratio[:, 384 * h : 384 * (h + 1)], bank[:])
+            return ratio
+
         xs = keep.tile([P, T], U8, name="xs", align_bytes=64)
         ws = keep.tile([P, E, K], U8, name="ws", align_bytes=64)
         nc.vector.memset(xs[:].bitcast(I32), 0)
         nc.vector.memset(ws[:].rearrange("p e n -> p (e n)").bitcast(I32), 0)
+        rows = keep.tile([P, T // 2], F32, name="rows")
+        nc.gpsimd.memset(rows[:], 0.0)
         ident = keep.tile([P, P], F32, name="ident")
         make_identity(nc, ident[:])
 
-        xw = keep.tile([P, T], I32, name="xw", align_bytes=64)
-        nc.sync.dma_start(xw[:], x_words[0].rearrange("p t d -> p (t d)").bitcast(I32))
+        l_offs = load_list(offs, "l_offs")
         for r in range(4):
             nc.sync.dma_start(xs[r:P:32, :].bitcast(I32), x_scales[0, r:16:4, :].bitcast(I32))
-        l_offs = load_list(offs, "l_offs")
+        xw = keep.tile([P, T], I32, name="xw", align_bytes=64)
+        nc.sync.dma_start(xw[:], x_words[0].rearrange("p t d -> p (t d)").bitcast(I32))
+        for step, gate in enumerate((gate1, gate2)):
+            flat = gate.rearrange("r p (h t) -> (r p h) t", h=2)
+            nc.sync.dma_start(rows[4 * step : 4 * step + 4, :], flat[2 * P - 2 : 2 * P + 2, :])
         for r in range(4):
             nc.sync.dma_start(
                 ws[r:P:32, :, :].bitcast(I32),
@@ -76,115 +104,178 @@ def tile_moe_uni_silu_kernel(
             ww.append(t)
         l_pos1 = load_list(pos1, "l_pos1")
         l_pos2 = load_list(pos2, "l_pos2")
-        gates = []
-        for i, gsrc in enumerate((gate1[0], gate1[1])):
-            t = keep.tile([P, T], F32, name=f"gate{i}")
-            nc.sync.dma_start(t[:], gsrc)
-            gates.append(t)
         l_offs2 = load_list(offs2, "l_offs2")
         l_pos3 = load_list(pos3, "l_pos3")
         l_pos4 = load_list(pos4, "l_pos4")
-        for i, gsrc in enumerate((gate2[0], gate2[1])):
-            t = keep.tile([P, T], F32, name=f"gate{2 + i}")
-            nc.sync.dma_start(t[:], gsrc)
-            gates.append(t)
+        groups2 = [(pair, t0, 256) for pair in range(2) for t0 in (0, 256, 512)]
+        groups2 = groups2[:4] + [(1, 256, P), (1, 384, 256), (1, 640, P)]
+        q2_from = groups2[PE_GROUPS][1]
+        q2 = keep.tile([P, T - q2_from], F32, name="q2")
+        nc.sync.dma_start(q2[:], gate2[1][:, q2_from:T])
 
-        def experts(chunks, name, early):
+        bank = bank_tile(0, [P, 3, P])
+        for j in range(3):
+            nc.tensor.transpose(bank[:, j, :], rows[:, j * P : (j + 1) * P], ident[:])
+        later = early.tile([P, 5 * (S - G1[0]) // 4], F32, name="later", align_bytes=64, offset=5 * G1[0])
+        den = later[:, 0 : 2 * NB].rearrange("p (j s h) -> p j s h", j=3, s=2)
+        nc.scalar.activation(den, bank[:, :, 0:8].rearrange("p j (s r h) -> p j s r h", s=2, r=2)[:, :, :, 1, :], COPY, bias=TINY)
+        cols = keep.tile([P, 3, 2, 2, 2], F32, name="cols")
+        nc.scalar.activation(cols[:].rearrange("p j s r h -> p j (s r h)"), bank[:, :, 0:8], COPY, bias=TINY)
+        rec = keep.tile([P, 3, 2, 2], F32, name="rec")
+        nc.vector.reciprocal(rec[:].rearrange("p j s h -> p (j s h)"), later[:, 0 : 2 * NB])
+        rcol = keep.tile([P, 3, 2, 2], F32, name="rcol")
+        nc.gpsimd.tensor_tensor(rcol[:], cols[:, :, :, 0, :], rec[:], MULT)
+
+        def factor(step, j):
+            return cols[:, j % 3, step, 1, j // 3 : j // 3 + 1]
+
+        def experts(operands, name, first_banks, at, between):
             planes = [keep.tile([P, S], F32, name=f"{name}{b}") for b in range(4)]
-            order = [(b, i) for i, nb in enumerate(early) for b in range(nb)]
-            order = order + [(b, i) for b in range(4) for i in range(len(chunks)) if (b, i) not in order]
-            for b, i in order:
-                s0, n, words, scales = chunks[i]
-                acc = psum.tile([P, 512], F32, name="bank")
-                for j in range(n // C):
-                    e = s0 // C + j
+            done = [(b, e) for b, e0, ne in first_banks for e in range(e0, e0 + ne)]
+            order = list(first_banks) + [(b, e0, 4) for b in range(4) for e0 in range(0, E, 4) if (b, e0) not in done]
+            for i, (b, e0, ne) in enumerate(order):
+                acc = bank_tile((at + i) % 8, [P, ne * C])
+                for j in range(ne):
+                    e = e0 + j
+                    words, scales = operands[e]
                     nc.tensor.matmul_mx(
                         out=acc[:, j * C : (j + 1) * C],
                         lhsT=ww[e // 4][:, e % 4, 256 * b : 256 * (b + 1)].bitcast(FP4X4),
                         lhsT_scale=ws[:, e, P * b : P * (b + 1)],
-                        rhs=words[:, j * C : (j + 1) * C].bitcast(FP8X4),
-                        rhs_scale=scales[:, j * C : (j + 1) * C],
+                        rhs=words.bitcast(FP8X4),
+                        rhs_scale=scales,
                         start=True,
                         stop=True,
                     )
-                nc.scalar.activation(planes[b][:, s0 : s0 + n], acc[:, 0:n], SILU)
-            return planes
+                nc.scalar.activation(planes[b][:, e0 * C : (e0 + ne) * C], acc[:], SILU)
+                if i == 1:
+                    between()
+            return planes, (at + len(order)) % 8
 
-        def gated(y, lst, gate, t0, n, name):
-            a = ring.tile([P, 640], F32, name=name)
-            nc.vector.tensor_tensor(a[:, 0:n], y[:].indirect(part(lst, t0, n)), gate[:, t0 : t0 + n], MULT)
-            return a
+        def combine(y, lst_a, lst_b, ratio, pieces, name, after):
+            sums = [keep.tile([P, T], F32, name=f"{name}{b}") for b in range(4)]
+            held = {}
+            for i in range(len(pieces) + 1):
+                if i < len(pieces):
+                    b, t0, n = pieces[i]
+                    a = first.tile([P, 256], F32, name=f"{name}_a{i}", offset=1024 * (i % A_SLOTS))
+                    nc.vector.tensor_tensor(a[:, 0:n], y[b][:].indirect(part(lst_a, t0, n)), ratio[:, t0 : t0 + n], MULT)
+                    held[i] = a
+                if i > 0:
+                    b, t0, n = pieces[i - 1]
+                    nc.vector.tensor_tensor(
+                        sums[b][:, t0 : t0 + n], y[b][:].indirect(part(lst_b, t0, n)), held[i - 1][:, 0:n], ADD
+                    )
+                    after(i - 1, sums)
 
-        def sum_turned(a1, a2, n):
-            bank = psum.tile([P, 512], F32, name="bank")
-            for j in range(n // P):
-                cols = slice(j * P, (j + 1) * P)
-                nc.tensor.matmul(bank[:, cols], a1[:, cols], ident[:], start=True, stop=False, is_transpose=True)
-                nc.tensor.matmul(bank[:, cols], a2[:, cols], ident[:], start=False, stop=True, is_transpose=True)
-            return bank
-
-        chunks = []
+        operands = []
         for i, (s0, n) in enumerate(zip(starts(G1), G1)):
-            gw = keep.tile([P, n], U32, name=f"gw{i}", align_bytes=64)
-            gs = keep.tile([P, n], U8, name=f"gs{i}", align_bytes=64)
-            nc.vector.tensor_copy(gw[:], xw[:].bitcast(U32).indirect(part(l_offs, s0, n)))
+            gs = early.tile([P, n], U8, name=f"gs{i}", align_bytes=64, offset=5 * s0)
+            gw = early.tile([P, n], U32, name=f"gw{i}", align_bytes=64, offset=5 * s0 + n)
             nc.vector.tensor_copy(gs[:], xs[:].indirect(part(l_offs, s0, n)))
-            chunks.append((s0, n, gw, gs))
-        y = experts(chunks, "y", (4, 2))
+            nc.vector.tensor_copy(gw[:], xw[:].bitcast(U32).indirect(part(l_offs, s0, n)))
+            operands.extend((gw[:, j : j + C], gs[:, j : j + C]) for j in range(0, n, C))
+        ratios = []
+        y, at = experts(operands, "y", EARLY1, 1, lambda: ratios.append(spread(rcol, 0, 1)))
+        ratio1 = ratios[0]
+        ratio2 = spread(rcol, 1, at)
+        free = [(at + 2 + k) % 8 for k in range(8)]
 
-        cw = [keep.tile([P, T], F32, name=f"cw{u}", align_bytes=64) for u in range(2)]
-        for i, (t0, n) in enumerate(zip(starts(C1), C1)):
+        pieces = [(b, t0, 256) for b in range(4) for t0 in (0, 256)]
+        pieces = pieces + [(b, 512, 256) for b in range(3)] + [(3, 512, P), (3, 640, P)]
+        ct = [keep.tile([P, 2, 256], BF16, name=f"ct{j}", align_bytes=64) for j in range(NB)]
+        cw = keep.tile([P, 2, T], F32, name="cw", align_bytes=64)
+        banks = {}
+        turn_at = {(0, 0): 0, (256, 0): 1, (0, 2): 2, (256, 2): 3, (512, 0): 2, (512, 2): 3, (512, 3): 4, (640, 3): 5}
+        back_at = {0: 4, 256: 5, 512: 0, 640: 1}
+
+        def after1(i, sums):
+            b, t0, n = pieces[i]
+            g0 = b if t0 >= 512 and b >= 2 else b - b % 2
+            if (t0, g0) not in banks:
+                banks[(t0, g0)] = bank_tile(free[turn_at[(t0, g0)]], [P, 2, 256])
+            bank = banks[(t0, g0)]
             nb = n // P
-            ct = keep.tile([P, nb, 2, 256], BF16, name=f"ct{i}", align_bytes=64)
-            for b in range(4):
-                a1 = gated(y[b], l_pos1, gates[0], t0, n, "a1")
-                a2 = gated(y[b], l_pos2, gates[1], t0, n, "a2")
-                bank = sum_turned(a1, a2, n)
-                nc.scalar.copy(
-                    ct[:, :, :, 64 * b : 64 * (b + 1)].rearrange("p k u (m e) -> p k u m e", e=2),
-                    bank[:, 0:n].rearrange("p (k m u e) -> p k u m e", m=32, u=2, e=2),
+            for j in range(nb):
+                col = (b - g0) * P
+                nc.tensor.transpose(bank[:, j, col : col + P], sums[b][:, t0 + j * P : t0 + (j + 1) * P], ident[:])
+            if b == 0 or (b == 2 and t0 < 512):
+                return
+            width = P * (b - g0 + 1)
+            for j in range(nb):
+                nc.scalar.activation(
+                    ct[t0 // P + j][:, :, 64 * g0 : 64 * g0 + width // 2].rearrange("p u (m e) -> p u m e", e=2),
+                    bank[:, j, 0:width].rearrange("p (m u e) -> p u m e", u=2, e=2),
+                    COPY,
+                    scale=factor(0, t0 // P + j),
                 )
-            ctw = ct[:].bitcast(F32)
-            for u in range(2):
-                bank = psum.tile([P, 512], F32, name="bank")
+            if b == 3:
+                back = bank_tile(free[back_at[t0]], [P, 2, n])
                 for j in range(nb):
-                    nc.tensor.transpose(bank[:, j * P : (j + 1) * P], ctw[:, j, u, :], ident[:])
-                nc.scalar.copy(cw[u][:, t0 : t0 + n], bank[:, 0:n])
+                    for u in range(2):
+                        nc.tensor.transpose(
+                            back[:, u, j * P : (j + 1) * P], ct[t0 // P + j][:].bitcast(F32)[:, u, :], ident[:]
+                        )
+                nc.scalar.copy(cw[:, :, t0 : t0 + n], back[:])
 
-        chunks = []
+        combine(y, l_pos1, l_pos2, ratio1, pieces, "c", after1)
+
+        operands = []
         widths = [w for w, st in G2]
         for i, (s0, (n, stepped)) in enumerate(zip(starts(widths), G2)):
             woven = mid.tile([P, n, 2], U32, name=f"woven{i}", align_bytes=64, offset=WOVEN_AT[i])
             if stepped:
                 for u in range(2):
-                    nc.vector.tensor_copy(woven[:, :, u], cw[u][:].bitcast(U32).indirect(part(l_offs2, s0, n)))
+                    nc.vector.tensor_copy(woven[:, :, u], cw[:, u, :].bitcast(U32).indirect(part(l_offs2, s0, n)))
             else:
                 pl = mid.tile([P, 2, n], U32, name=f"pl{i}", align_bytes=64, offset=PLANES_AT[i])
                 for u in range(2):
-                    nc.vector.tensor_copy(pl[:, u, :], cw[u][:].bitcast(U32).indirect(part(l_offs2, s0, n)))
+                    nc.vector.tensor_copy(pl[:, u, :], cw[:, u, :].bitcast(U32).indirect(part(l_offs2, s0, n)))
                 nc.scalar.copy(woven[:], pl[:].rearrange("p u n -> p n u"))
             qw = keep.tile([P, n], U32, name=f"qw{i}", align_bytes=64)
             qs = keep.tile([P, n], U8, name=f"qs{i}", align_bytes=64)
             nc.vector.quantize_mx(
                 out=qw[:].bitcast(FP8X4), scales=qs[:], in_=woven[:].rearrange("p n u -> p (n u)").bitcast(BF16)
             )
-            chunks.append((s0, n, qw, qs))
-        z = experts(chunks, "z", (4,))
+            operands.extend((qw[:, j : j + C], qs[:, j : j + C]) for j in range(0, n, C))
+        z, at = experts(operands, "z", EARLY2, free[2], lambda: None)
+        free = [(at + k) % 8 for k in range(8)]
 
-        for b, t0, t1, on_pe in FIN:
-            n = t1 - t0
-            a1 = gated(z[b], l_pos3, gates[2], t0, n, "a1")
-            a2 = gated(z[b], l_pos4, gates[3], t0, n, "a2")
-            res = ring.tile([P, 640], F32, name="res")
-            if on_pe:
-                bank = sum_turned(a1, a2, n)
-                st = ring.tile([P, 512], F32, name="st")
-                nc.scalar.copy(st[:, 0:n], bank[:, 0:n])
-                bank2 = psum.tile([P, 512], F32, name="bank")
-                for j in range(n // P):
-                    cols = slice(j * P, (j + 1) * P)
-                    nc.tensor.transpose(bank2[:, cols], st[:, cols], ident[:])
-                nc.scalar.copy(res[:, 0:n], bank2[:, 0:n])
-            else:
-                nc.vector.tensor_tensor(res[:, 0:n], a1[:, 0:n], a2[:, 0:n], ADD)
-            nc.sync.dma_start(out[b * P : (b + 1) * P, t0:t1], res[:, 0:n])
+        pieces2 = [(2 * pair + h, t0, n) for pair, t0, n in groups2 for h in range(2)]
+
+        def after2(i, sums):
+            b, t0, n = pieces2[i]
+            g = i // 2
+            if g >= PE_GROUPS:
+                res = keep.tile([P, n], F32, name=f"res{i}")
+                nc.vector.scalar_tensor_tensor(
+                    res[:], q2[:, t0 - q2_from : t0 - q2_from + n], TINY, sums[b][:, t0 : t0 + n], ADD, MULT
+                )
+                nc.sync.dma_start(out[b * P : (b + 1) * P, t0 : t0 + n], res[:])
+                return
+            nb = n // P
+            if b % 2 == 0:
+                banks[g] = bank_tile(free[g % 2], [P, nb, 2, P])
+            for j in range(nb):
+                nc.tensor.transpose(banks[g][:, j, b % 2, :], sums[b][:, t0 + j * P : t0 + (j + 1) * P], ident[:])
+            if b % 2 == 0:
+                return
+            st = keep.tile([P, nb, 2, P], F32, name=f"st{g}")
+            for j in range(nb):
+                nc.scalar.activation(
+                    st[:, j].rearrange("p h f -> p (h f)"),
+                    banks[g][:, j].rearrange("p h f -> p (h f)"),
+                    COPY,
+                    scale=factor(1, t0 // P + j),
+                )
+            back = bank_tile(free[2 + g % 2], [P, 2, nb, P])
+            for j in range(nb):
+                for h in range(2):
+                    nc.tensor.transpose(back[:, h, j, :], st[:, j, h, :], ident[:])
+            res = keep.tile([P, 2, n], F32, name=f"res{i}")
+            nc.scalar.copy(res[:].rearrange("p h t -> p (h t)"), back[:].rearrange("p h j t -> p (h j t)"))
+            nc.scalar.dma_start(
+                out[(b - 1) * P : (b + 1) * P, t0 : t0 + n].rearrange("(h p) t -> p h t", h=2), res[:]
+            )
+
+        combine(z, l_pos3, l_pos4, ratio2, pieces2, "o", after2)

@@ -26,12 +26,13 @@ TINY = 2.0**-60
 BANK = 2048
 G1 = (512, 512, 384, 128)
 EARLY1 = ((0, 0, 4), (1, 0, 4), (0, 4, 4), (0, 8, 3), (0, 11, 1))
-EARLY2 = ((0, 0, 4), (1, 0, 4), (2, 0, 4), (0, 4, 4), (1, 4, 4), (0, 8, 2), (0, 10, 2))
-G2 = ((512, False), (512, False), (256, False), (256, True))
+EARLY2 = ((0, 0, 4), (1, 0, 4), (0, 4, 4), (1, 4, 4), (0, 8, 3), (0, 11, 1))
+G2 = ((512, False), (512, False), (384, False), (128, True))
 WOVEN_AT = (0, 4096, 8192, 4096)
 PLANES_AT = (12288, 16384, 0)
+QUANT = {512: (512,), 384: (256, 128), 128: (128,)}
 A_SLOTS = 3
-PE_GROUPS = 5
+TAIL = ((0, 384), (384, 256), (640, 128))
 
 
 def starts(widths):
@@ -75,7 +76,7 @@ def tile_moe_uni_silu_kernel(
 
         xs = keep.tile([P, T], U8, name="xs", align_bytes=64)
         ws = keep.tile([P, E, K], U8, name="ws", align_bytes=64)
-        nc.vector.memset(xs[:].bitcast(I32), 0)
+        nc.gpsimd.memset(xs[:].bitcast(I32), 0)
         nc.vector.memset(ws[:].rearrange("p e n -> p (e n)").bitcast(I32), 0)
         rows = keep.tile([P, T // 2], F32, name="rows")
         nc.gpsimd.memset(rows[:], 0.0)
@@ -107,9 +108,7 @@ def tile_moe_uni_silu_kernel(
         l_offs2 = load_list(offs2, "l_offs2")
         l_pos3 = load_list(pos3, "l_pos3")
         l_pos4 = load_list(pos4, "l_pos4")
-        groups2 = [(pair, t0, 256) for pair in range(2) for t0 in (0, 256, 512)]
-        groups2 = groups2[:4] + [(1, 256, P), (1, 384, 256), (1, 640, P)]
-        q2_from = groups2[PE_GROUPS][1]
+        q2_from = TAIL[1][0]
         q2 = keep.tile([P, T - q2_from], F32, name="q2")
         nc.sync.dma_start(q2[:], gate2[1][:, q2_from:T])
 
@@ -158,7 +157,7 @@ def tile_moe_uni_silu_kernel(
             for i in range(len(pieces) + 1):
                 if i < len(pieces):
                     b, t0, n = pieces[i]
-                    a = first.tile([P, 256], F32, name=f"{name}_a{i}", offset=1024 * (i % A_SLOTS))
+                    a = first.tile([P, T], F32, name=f"{name}_a{i}", offset=4 * T * (i % A_SLOTS))
                     nc.vector.tensor_tensor(a[:, 0:n], y[b][:].indirect(part(lst_a, t0, n)), ratio[:, t0 : t0 + n], MULT)
                     held[i] = a
                 if i > 0:
@@ -170,53 +169,59 @@ def tile_moe_uni_silu_kernel(
 
         operands = []
         for i, (s0, n) in enumerate(zip(starts(G1), G1)):
-            gs = early.tile([P, n], U8, name=f"gs{i}", align_bytes=64, offset=5 * s0)
-            gw = early.tile([P, n], U32, name=f"gw{i}", align_bytes=64, offset=5 * s0 + n)
-            nc.vector.tensor_copy(gs[:], xs[:].indirect(part(l_offs, s0, n)))
+            if s0 % 512 == 0:
+                gs = early.tile([P, 512], U8, name=f"gs{i}", align_bytes=64, offset=5 * s0)
+                nc.vector.tensor_copy(gs[:], xs[:].indirect(part(l_offs, s0, 512)))
+            gw = early.tile([P, n], U32, name=f"gw{i}", align_bytes=64, offset=4 * s0 + 512 * (s0 // 512 + 1))
             nc.vector.tensor_copy(gw[:], xw[:].bitcast(U32).indirect(part(l_offs, s0, n)))
-            operands.extend((gw[:, j : j + C], gs[:, j : j + C]) for j in range(0, n, C))
+            operands.extend((gw[:, j : j + C], gs[:, (s0 + j) % 512 : (s0 + j) % 512 + C]) for j in range(0, n, C))
         ratios = []
         y, at = experts(operands, "y", EARLY1, 1, lambda: ratios.append(spread(rcol, 0, 1)))
         ratio1 = ratios[0]
         ratio2 = spread(rcol, 1, at)
         free = [(at + 2 + k) % 8 for k in range(8)]
 
-        pieces = [(b, t0, 256) for b in range(4) for t0 in (0, 256)]
-        pieces = pieces + [(b, 512, 256) for b in range(3)] + [(3, 512, P), (3, 640, P)]
+        pieces = [(0, 0, T), (1, 0, T)] + [(b, t0, n) for t0, n in TAIL for b in (2, 3)]
         ct = [keep.tile([P, 2, 256], BF16, name=f"ct{j}", align_bytes=64) for j in range(NB)]
         cw = keep.tile([P, 2, T], F32, name="cw", align_bytes=64)
         banks = {}
-        turn_at = {(0, 0): 0, (256, 0): 1, (0, 2): 2, (256, 2): 3, (512, 0): 2, (512, 2): 3, (512, 3): 4, (640, 3): 5}
-        back_at = {0: 4, 256: 5, 512: 0, 640: 1}
+
+        def turn(sums, b, t0, n, step, slot_of):
+            for j in range(t0 // P, (t0 + n) // P):
+                key = (step, b // 2, t0, slot_of(j))
+                if key not in banks:
+                    banks[key] = bank_tile(free[slot_of(j)], [P, 2, 2, P])
+                nc.tensor.transpose(banks[key][:, j % 2, b % 2, :], sums[b][:, j * P : (j + 1) * P], ident[:])
+
+        slot1 = ((0, 0, 1, 1, 2, 2), (3, 3, 4, 3, 3, 4))
+        back_at = {0: (5, 6), 384: (0,), 640: (1,)}
 
         def after1(i, sums):
             b, t0, n = pieces[i]
-            g0 = b if t0 >= 512 and b >= 2 else b - b % 2
-            if (t0, g0) not in banks:
-                banks[(t0, g0)] = bank_tile(free[turn_at[(t0, g0)]], [P, 2, 256])
-            bank = banks[(t0, g0)]
-            nb = n // P
-            for j in range(nb):
-                col = (b - g0) * P
-                nc.tensor.transpose(bank[:, j, col : col + P], sums[b][:, t0 + j * P : t0 + (j + 1) * P], ident[:])
-            if b == 0 or (b == 2 and t0 < 512):
+            pair = b // 2
+            turn(sums, b, t0, n, 0, lambda j: slot1[pair][j])
+            if b % 2 == 0:
                 return
-            width = P * (b - g0 + 1)
-            for j in range(nb):
-                nc.scalar.activation(
-                    ct[t0 // P + j][:, :, 64 * g0 : 64 * g0 + width // 2].rearrange("p u (m e) -> p u m e", e=2),
-                    bank[:, j, 0:width].rearrange("p (m u e) -> p u m e", u=2, e=2),
-                    COPY,
-                    scale=factor(0, t0 // P + j),
-                )
-            if b == 3:
-                back = bank_tile(free[back_at[t0]], [P, 2, n])
-                for j in range(nb):
+            blocks = range(t0 // P, (t0 + n) // P)
+            for j in blocks:
+                dst = ct[j][:, :, P * pair : P * (pair + 1)].rearrange("p u (m e) -> p u m e", e=2)
+                src = banks[(0, pair, t0, slot1[pair][j])][:, j % 2].rearrange("p h (m u e) -> p u (h m) e", u=2, e=2)
+                if i == len(pieces) - 1:
+                    nc.vector.tensor_scalar(dst, src, factor(0, j), None, MULT)
+                else:
+                    nc.scalar.activation(dst, src, COPY, scale=factor(0, j))
+            if pair == 0:
+                return
+            for k, at2 in enumerate(back_at[t0]):
+                some = blocks[2 * k : 2 * k + 2]
+                back = bank_tile(free[at2], [P, 2, len(some) * P])
+                for m, j in enumerate(some):
                     for u in range(2):
-                        nc.tensor.transpose(
-                            back[:, u, j * P : (j + 1) * P], ct[t0 // P + j][:].bitcast(F32)[:, u, :], ident[:]
-                        )
-                nc.scalar.copy(cw[:, :, t0 : t0 + n], back[:])
+                        nc.tensor.transpose(back[:, u, m * P : (m + 1) * P], ct[j][:].bitcast(F32)[:, u, :], ident[:])
+                if i == len(pieces) - 1:
+                    nc.vector.tensor_copy(cw[:, :, some[0] * P : (some[-1] + 1) * P], back[:])
+                else:
+                    nc.scalar.copy(cw[:, :, some[0] * P : (some[-1] + 1) * P], back[:])
 
         combine(y, l_pos1, l_pos2, ratio1, pieces, "c", after1)
 
@@ -234,48 +239,42 @@ def tile_moe_uni_silu_kernel(
                 nc.scalar.copy(woven[:], pl[:].rearrange("p u n -> p n u"))
             qw = keep.tile([P, n], U32, name=f"qw{i}", align_bytes=64)
             qs = keep.tile([P, n], U8, name=f"qs{i}", align_bytes=64)
-            nc.vector.quantize_mx(
-                out=qw[:].bitcast(FP8X4), scales=qs[:], in_=woven[:].rearrange("p n u -> p (n u)").bitcast(BF16)
-            )
+            for q0, qn in zip(starts(QUANT[n]), QUANT[n]):
+                nc.vector.quantize_mx(
+                    out=qw[:, q0 : q0 + qn].bitcast(FP8X4),
+                    scales=qs[:, q0 : q0 + qn],
+                    in_=woven[:, q0 : q0 + qn, :].rearrange("p n u -> p (n u)").bitcast(BF16),
+                )
             operands.extend((qw[:, j : j + C], qs[:, j : j + C]) for j in range(0, n, C))
         z, at = experts(operands, "z", EARLY2, free[2], lambda: None)
         free = [(at + k) % 8 for k in range(8)]
 
-        pieces2 = [(2 * pair + h, t0, n) for pair, t0, n in groups2 for h in range(2)]
+        pieces2 = pieces
+        back2_at = ((2, 3), (4, 5), (2,), (3,))
 
         def after2(i, sums):
             b, t0, n = pieces2[i]
-            g = i // 2
-            if g >= PE_GROUPS:
+            pair = b // 2
+            if pair == 1 and t0 >= q2_from:
                 res = keep.tile([P, n], F32, name=f"res{i}")
                 nc.vector.scalar_tensor_tensor(
                     res[:], q2[:, t0 - q2_from : t0 - q2_from + n], TINY, sums[b][:, t0 : t0 + n], ADD, MULT
                 )
                 nc.sync.dma_start(out[b * P : (b + 1) * P, t0 : t0 + n], res[:])
                 return
-            nb = n // P
-            if b % 2 == 0:
-                banks[g] = bank_tile(free[g % 2], [P, nb, 2, P])
-            for j in range(nb):
-                nc.tensor.transpose(banks[g][:, j, b % 2, :], sums[b][:, t0 + j * P : t0 + (j + 1) * P], ident[:])
-            if b % 2 == 0:
-                return
-            st = keep.tile([P, nb, 2, P], F32, name=f"st{g}")
-            for j in range(nb):
-                nc.scalar.activation(
-                    st[:, j].rearrange("p h f -> p (h f)"),
-                    banks[g][:, j].rearrange("p h f -> p (h f)"),
-                    COPY,
-                    scale=factor(1, t0 // P + j),
-                )
-            back = bank_tile(free[2 + g % 2], [P, 2, nb, P])
-            for j in range(nb):
-                for h in range(2):
-                    nc.tensor.transpose(back[:, h, j, :], st[:, j, h, :], ident[:])
-            res = keep.tile([P, 2, n], F32, name=f"res{i}")
-            nc.scalar.copy(res[:].rearrange("p h t -> p (h t)"), back[:].rearrange("p h j t -> p (h j t)"))
-            nc.scalar.dma_start(
-                out[(b - 1) * P : (b + 1) * P, t0 : t0 + n].rearrange("(h p) t -> p h t", h=2), res[:]
-            )
+            res = keep.tile([P, n], F32, name=f"res{i}")
+            for k, at2 in enumerate(back2_at[b]):
+                there = bank_tile(free[k], [P, 3, P])
+                for m in range(3):
+                    j = 3 * k + m
+                    nc.tensor.transpose(there[:, m, :], sums[b][:, j * P : (j + 1) * P], ident[:])
+                st = keep.tile([P, 3, P], F32, name=f"st{b}{k}")
+                for m in range(3):
+                    nc.scalar.activation(st[:, m, :], there[:, m, :], COPY, scale=factor(1, 3 * k + m))
+                back = bank_tile(free[at2], [P, 3, P])
+                for m in range(3):
+                    nc.tensor.transpose(back[:, m, :], st[:, m, :], ident[:])
+                nc.scalar.copy(res[:, 384 * k : 384 * (k + 1)], back[:].rearrange("p j t -> p (j t)"))
+            nc.scalar.dma_start(out[b * P : (b + 1) * P, t0 : t0 + n], res[:])
 
         combine(z, l_pos3, l_pos4, ratio2, pieces2, "o", after2)

@@ -25,7 +25,7 @@ COPY = mybir.ActivationFunctionType.Copy
 TINY = 2.0**-60
 BANK = 2048
 G1 = (512, 512, 384, 128)
-EARLY1 = ((0, 0, 4), (1, 0, 4), (0, 4, 4), (0, 8, 3), (0, 11, 1))
+EARLY1 = ((0, 0, 4), (0, 4, 4), (1, 0, 4), (0, 8, 3), (0, 11, 1))
 EARLY2 = ((0, 0, 4), (1, 0, 4), (0, 4, 4), (1, 4, 4), (0, 8, 3), (0, 11, 1))
 G2 = ((512, False), (512, False), (384, False), (128, True))
 WOVEN_AT = (0, 4096, 8192, 4096)
@@ -83,14 +83,16 @@ def tile_moe_uni_silu_kernel(
         ident = keep.tile([P, P], F32, name="ident")
         make_identity(nc, ident[:])
 
+        warm = keep.tile([P, 1], F32, name="warm")
+        nc.scalar.activation(warm[:], ident[:, 0:1], SILU)
         l_offs = load_list(offs, "l_offs")
         for r in range(4):
-            nc.sync.dma_start(xs[r:P:32, :].bitcast(I32), x_scales[0, r:16:4, :].bitcast(I32))
-        xw = keep.tile([P, T], I32, name="xw", align_bytes=64)
-        nc.sync.dma_start(xw[:], x_words[0].rearrange("p t d -> p (t d)").bitcast(I32))
+            (nc.sync if r < 2 else nc.scalar).dma_start(xs[r:P:32, :].bitcast(I32), x_scales[0, r:16:4, :].bitcast(I32))
         for step, gate in enumerate((gate1, gate2)):
             flat = gate.rearrange("r p (h t) -> (r p h) t", h=2)
             nc.sync.dma_start(rows[4 * step : 4 * step + 4, :], flat[2 * P - 2 : 2 * P + 2, :])
+        xw = keep.tile([P, T], I32, name="xw", align_bytes=64)
+        nc.sync.dma_start(xw[:], x_words[0].rearrange("p t d -> p (t d)").bitcast(I32))
         for r in range(4):
             nc.sync.dma_start(
                 ws[r:P:32, :, :].bitcast(I32),
@@ -108,14 +110,14 @@ def tile_moe_uni_silu_kernel(
         l_offs2 = load_list(offs2, "l_offs2")
         l_pos3 = load_list(pos3, "l_pos3")
         l_pos4 = load_list(pos4, "l_pos4")
-        q2_from = TAIL[1][0]
+        q2_from = 0
         q2 = keep.tile([P, T - q2_from], F32, name="q2")
         nc.sync.dma_start(q2[:], gate2[1][:, q2_from:T])
 
         bank = bank_tile(0, [P, 3, P])
         for j in range(3):
             nc.tensor.transpose(bank[:, j, :], rows[:, j * P : (j + 1) * P], ident[:])
-        later = early.tile([P, 5 * (S - G1[0]) // 4], F32, name="later", align_bytes=64, offset=5 * G1[0])
+        later = early.tile([P, (5 * S - 1024) // 4], F32, name="later", align_bytes=64, offset=1024)
         den = later[:, 0 : 2 * NB].rearrange("p (j s h) -> p j s h", j=3, s=2)
         nc.scalar.activation(den, bank[:, :, 0:8].rearrange("p j (s r h) -> p j s r h", s=2, r=2)[:, :, :, 1, :], COPY, bias=TINY)
         cols = keep.tile([P, 3, 2, 2, 2], F32, name="cols")
@@ -167,16 +169,23 @@ def tile_moe_uni_silu_kernel(
                     )
                     after(i - 1, sums)
 
-        operands = []
-        for i, (s0, n) in enumerate(zip(starts(G1), G1)):
-            if s0 % 512 == 0:
-                gs = early.tile([P, 512], U8, name=f"gs{i}", align_bytes=64, offset=5 * s0)
-                nc.vector.tensor_copy(gs[:], xs[:].indirect(part(l_offs, s0, 512)))
-            gw = early.tile([P, n], U32, name=f"gw{i}", align_bytes=64, offset=4 * s0 + 512 * (s0 // 512 + 1))
-            nc.vector.tensor_copy(gw[:], xw[:].bitcast(U32).indirect(part(l_offs, s0, n)))
-            operands.extend((gw[:, j : j + C], gs[:, (s0 + j) % 512 : (s0 + j) % 512 + C]) for j in range(0, n, C))
-        ratios = []
-        y, at = experts(operands, "y", EARLY1, 1, lambda: ratios.append(spread(rcol, 0, 1)))
+        gs = [early.tile([P, 512], U8, name=f"gs{i}", align_bytes=64, offset=512 * i) for i in range(3)]
+        gw = [
+            early.tile([P, n], U32, name=f"gw{i}", align_bytes=64, offset=S + 4 * s0)
+            for i, (s0, n) in enumerate(zip(starts(G1), G1))
+        ]
+        for kind, i in (("s", 0), ("s", 1), ("w", 0), ("w", 1), ("s", 2), ("w", 2), ("w", 3)):
+            if kind == "s":
+                nc.vector.tensor_copy(gs[i][:], xs[:].indirect(part(l_offs, 512 * i, 512)))
+            else:
+                nc.vector.tensor_copy(gw[i][:], xw[:].bitcast(U32).indirect(part(l_offs, starts(G1)[i], G1[i])))
+        operands = [
+            (gw[i][:, j : j + C], gs[(s0 + j) // 512][:, (s0 + j) % 512 : (s0 + j) % 512 + C])
+            for i, (s0, n) in enumerate(zip(starts(G1), G1))
+            for j in range(0, n, C)
+        ]
+        ratios = [spread(rcol, 0, 1)]
+        y, at = experts(operands, "y", EARLY1, 3, lambda: None)
         ratio1 = ratios[0]
         ratio2 = spread(rcol, 1, at)
         free = [(at + 2 + k) % 8 for k in range(8)]
@@ -249,13 +258,12 @@ def tile_moe_uni_silu_kernel(
         z, at = experts(operands, "z", EARLY2, free[2], lambda: None)
         free = [(at + k) % 8 for k in range(8)]
 
-        pieces2 = pieces
-        back2_at = ((2, 3), (4, 5), (2,), (3,))
+        pieces2 = [(b, 0, T) for b in range(3)] + [(3, t0, n) for t0, n in TAIL]
+        back2_at = ((2, 3), (4, 5), (2, 3))
 
         def after2(i, sums):
             b, t0, n = pieces2[i]
-            pair = b // 2
-            if pair == 1 and t0 >= q2_from:
+            if b == 3:
                 res = keep.tile([P, n], F32, name=f"res{i}")
                 nc.vector.scalar_tensor_tensor(
                     res[:], q2[:, t0 - q2_from : t0 - q2_from + n], TINY, sums[b][:, t0 : t0 + n], ADD, MULT
@@ -275,6 +283,6 @@ def tile_moe_uni_silu_kernel(
                 for m in range(3):
                     nc.tensor.transpose(back[:, m, :], st[:, m, :], ident[:])
                 nc.scalar.copy(res[:, 384 * k : 384 * (k + 1)], back[:].rearrange("p j t -> p (j t)"))
-            nc.scalar.dma_start(out[b * P : (b + 1) * P, t0 : t0 + n], res[:])
+                nc.scalar.dma_start(out[b * P : (b + 1) * P, 384 * k : 384 * (k + 1)], res[:, 384 * k : 384 * (k + 1)])
 
         combine(z, l_pos3, l_pos4, ratio2, pieces2, "o", after2)

@@ -26,7 +26,7 @@ TINY = 2.0**-60
 BANK = 2048
 G1 = (512, 512, 384, 128)
 EARLY1 = ((0, 0, 4), (0, 4, 4), (1, 0, 4), (0, 8, 3), (0, 11, 1))
-EARLY2 = ((0, 0, 4), (1, 0, 4), (0, 4, 4), (1, 4, 4), (0, 8, 3), (0, 11, 1))
+EARLY2 = ((0, 0, 4), (0, 4, 4), (0, 10, 2), (0, 8, 2))
 G2 = ((512, False), (512, False), (384, False), (128, True))
 WOVEN_AT = (0, 4096, 8192, 4096)
 PLANES_AT = (12288, 16384, 0)
@@ -153,21 +153,27 @@ def tile_moe_uni_silu_kernel(
                     between()
             return planes, (at + len(order)) % 8
 
-        def combine(y, lst_a, lst_b, ratio, pieces, name, after):
+        def combine(y, lst_a, lst_b, ratio, pieces, order, name, after):
             sums = [keep.tile([P, T], F32, name=f"{name}{b}") for b in range(4)]
             held = {}
-            for i in range(len(pieces) + 1):
-                if i < len(pieces):
-                    b, t0, n = pieces[i]
+            for kind, i in order:
+                b, t0, n = pieces[i]
+                if kind == "a":
                     a = first.tile([P, T], F32, name=f"{name}_a{i}", offset=4 * T * (i % A_SLOTS))
                     nc.vector.tensor_tensor(a[:, 0:n], y[b][:].indirect(part(lst_a, t0, n)), ratio[:, t0 : t0 + n], MULT)
                     held[i] = a
-                if i > 0:
-                    b, t0, n = pieces[i - 1]
+                if kind == "b":
                     nc.vector.tensor_tensor(
-                        sums[b][:, t0 : t0 + n], y[b][:].indirect(part(lst_b, t0, n)), held[i - 1][:, 0:n], ADD
+                        sums[b][:, t0 : t0 + n], y[b][:].indirect(part(lst_b, t0, n)), held[i][:, 0:n], ADD
                     )
-                    after(i - 1, sums)
+                if kind == "c":
+                    after(i, sums)
+
+        def lagged(count):
+            order = [("a", 0)]
+            for i in range(1, count):
+                order = order + [("a", i), ("b", i - 1), ("c", i - 1)]
+            return order + [("b", count - 1), ("c", count - 1)]
 
         gs = [early.tile([P, 512], U8, name=f"gs{i}", align_bytes=64, offset=512 * i) for i in range(3)]
         gw = [
@@ -193,6 +199,7 @@ def tile_moe_uni_silu_kernel(
         pieces = [(0, 0, T), (1, 0, T)] + [(b, t0, n) for t0, n in TAIL for b in (2, 3)]
         ct = [keep.tile([P, 2, 256], BF16, name=f"ct{j}", align_bytes=64) for j in range(NB)]
         cw = keep.tile([P, 2, T], F32, name="cw", align_bytes=64)
+        cp = keep.tile([P, 2, 2, T], BF16, name="cp", align_bytes=64)
         banks = {}
 
         def turn(sums, b, t0, n, step, slot_of):
@@ -203,6 +210,7 @@ def tile_moe_uni_silu_kernel(
                 nc.tensor.transpose(banks[key][:, j % 2, b % 2, :], sums[b][:, j * P : (j + 1) * P], ident[:])
 
         slot1 = ((0, 0, 1, 1, 2, 2), (3, 3, 4, 3, 3, 4))
+        backs = []
         back_at = {0: (5, 6), 384: (0,), 640: (1,)}
 
         def after1(i, sums):
@@ -231,34 +239,65 @@ def tile_moe_uni_silu_kernel(
                     nc.vector.tensor_copy(cw[:, :, some[0] * P : (some[-1] + 1) * P], back[:])
                 else:
                     nc.scalar.copy(cw[:, :, some[0] * P : (some[-1] + 1) * P], back[:])
+                backs.append((back, some[0] * P, len(some) * P))
 
-        combine(y, l_pos1, l_pos2, ratio1, pieces, "c", after1)
+        combine(y, l_pos1, l_pos2, ratio1, pieces, lagged(len(pieces)), "c", after1)
 
-        operands = []
-        widths = [w for w, st in G2]
-        for i, (s0, (n, stepped)) in enumerate(zip(starts(widths), G2)):
-            woven = mid.tile([P, n, 2], U32, name=f"woven{i}", align_bytes=64, offset=WOVEN_AT[i])
-            if stepped:
-                for u in range(2):
-                    nc.vector.tensor_copy(woven[:, :, u], cw[:, u, :].bitcast(U32).indirect(part(l_offs2, s0, n)))
+        for back, t0, n in backs:
+            if t0 < TAIL[1][0]:
+                src = cw[:].bitcast(BF16)[:, :, 2 * t0 : 2 * (t0 + n)].rearrange("p u (t e) -> p u e t", e=2)
+                nc.vector.tensor_copy(cp[:, :, :, t0 : t0 + n], src)
             else:
-                pl = mid.tile([P, 2, n], U32, name=f"pl{i}", align_bytes=64, offset=PLANES_AT[i])
-                for u in range(2):
-                    nc.vector.tensor_copy(pl[:, u, :], cw[:, u, :].bitcast(U32).indirect(part(l_offs2, s0, n)))
-                nc.scalar.copy(woven[:], pl[:].rearrange("p u n -> p n u"))
-            qw = keep.tile([P, n], U32, name=f"qw{i}", align_bytes=64)
-            qs = keep.tile([P, n], U8, name=f"qs{i}", align_bytes=64)
-            for q0, qn in zip(starts(QUANT[n]), QUANT[n]):
-                nc.vector.quantize_mx(
-                    out=qw[:, q0 : q0 + qn].bitcast(FP8X4),
-                    scales=qs[:, q0 : q0 + qn],
-                    in_=woven[:, q0 : q0 + qn, :].rearrange("p n u -> p (n u)").bitcast(BF16),
-                )
-            operands.extend((qw[:, j : j + C], qs[:, j : j + C]) for j in range(0, n, C))
-        z, at = experts(operands, "z", EARLY2, free[2], lambda: None)
-        free = [(at + k) % 8 for k in range(8)]
+                nc.scalar.copy(cp[:, :, :, t0 : t0 + n], back[:].bitcast(BF16).rearrange("p u (t e) -> p u e t", e=2))
 
-        pieces2 = [(b, 0, T) for b in range(3)] + [(3, t0, n) for t0, n in TAIL]
+        woven = [
+            mid.tile([P, n, 2], U32, name=f"woven{i}", align_bytes=64, offset=at2)
+            for i, (n, at2) in enumerate(((512, 0), (512, 4096), (256, 8192)))
+        ]
+        pl = [mid.tile([P, 2, 512], U32, name=f"pl{i}", align_bytes=64, offset=12288 + 4096 * i) for i in range(2)]
+        qw = keep.tile([P, S], U32, name="qw", align_bytes=64)
+        qs = keep.tile([P, S], U8, name="qs", align_bytes=64)
+
+        def pairs(dst, u, s0, n):
+            nc.vector.tensor_copy(dst, cw[:, u, :].bitcast(U32).indirect(part(l_offs2, s0, n)))
+
+        def single(t):
+            dst = woven[2][:].bitcast(BF16).rearrange("p n t -> p t n")[:, t, :]
+            nc.scalar.activation(dst, cp[:, t // 2, t % 2, :].indirect(part(l_offs2, 1024, 256)), COPY)
+
+        def weave(i, j0, n):
+            nc.scalar.copy(woven[i][:, j0 : j0 + n, :], pl[i][:, :, j0 : j0 + n].rearrange("p u n -> p n u"))
+
+        def quantise(src, s0, n):
+            nc.vector.quantize_mx(
+                out=qw[:, s0 : s0 + n].bitcast(FP8X4),
+                scales=qs[:, s0 : s0 + n],
+                in_=src.rearrange("p n u -> p (n u)").bitcast(BF16),
+            )
+
+        for i in range(2):
+            for u in range(2):
+                pairs(pl[i][:, u, :], u, 512 * i, 512)
+        single(0)
+        weave(0, 0, 512)
+        single(1)
+        weave(1, 0, 256)
+        single(2)
+        weave(1, 256, 256)
+        single(3)
+        quantise(woven[0][:], 0, 512)
+        quantise(woven[1][:, 0:256, :], 512, 256)
+        last = mid.tile([P, 256, 2], U32, name="last", align_bytes=64, offset=0)
+        for u in range(2):
+            pairs(last[:, :, u], u, 1280, 256)
+        quantise(woven[1][:, 256:512, :], 768, 256)
+        quantise(last[:], 1280, 256)
+        quantise(woven[2][:], 1024, 256)
+        operands = [(qw[:, e * C : (e + 1) * C], qs[:, e * C : (e + 1) * C]) for e in range(E)]
+        z, at = experts(operands, "z", EARLY2, free[2], lambda: None)
+        free = [(at - 5 + k) % 8 for k in range(8)]
+
+        pieces2 = [(0, 0, 384), (0, 384, 384), (1, 0, T), (2, 0, T)] + [(3, t0, n) for t0, n in TAIL]
         back2_at = ((2, 3), (4, 5), (2, 3))
 
         def after2(i, sums):
@@ -270,8 +309,9 @@ def tile_moe_uni_silu_kernel(
                 )
                 nc.sync.dma_start(out[b * P : (b + 1) * P, t0 : t0 + n], res[:])
                 return
-            res = keep.tile([P, n], F32, name=f"res{i}")
-            for k, at2 in enumerate(back2_at[b]):
+            res = keep.tile([P, T], F32, name=f"res{i}")
+            for k in range(t0 // 384, (t0 + n) // 384):
+                at2 = back2_at[b][k]
                 there = bank_tile(free[k], [P, 3, P])
                 for m in range(3):
                     j = 3 * k + m
@@ -285,4 +325,5 @@ def tile_moe_uni_silu_kernel(
                 nc.scalar.copy(res[:, 384 * k : 384 * (k + 1)], back[:].rearrange("p j t -> p (j t)"))
                 nc.scalar.dma_start(out[b * P : (b + 1) * P, 384 * k : 384 * (k + 1)], res[:, 384 * k : 384 * (k + 1)])
 
-        combine(z, l_pos3, l_pos4, ratio2, pieces2, "o", after2)
+        order2 = lagged(4) + [("a", 4), ("a", 5), ("b", 4), ("a", 6), ("c", 4), ("b", 5), ("b", 6), ("c", 5), ("c", 6)]
+        combine(z, l_pos3, l_pos4, ratio2, pieces2, order2, "o", after2)

@@ -26,7 +26,7 @@ TINY = 2.0**-60
 BANK = 2048
 G1 = (512, 512, 384, 128)
 EARLY1 = ((0, 0, 4), (0, 4, 4), (1, 0, 4), (0, 8, 3), (0, 11, 1))
-EARLY2 = ((0, 0, 4), (0, 4, 4), (0, 10, 2), (0, 8, 2))
+EARLY2 = ((0, 0, 4), (0, 4, 3), (0, 10, 2), (0, 7, 3))
 G2 = ((512, False), (512, False), (384, False), (128, True))
 WOVEN_AT = (0, 4096, 8192, 4096)
 PLANES_AT = (12288, 16384, 0)
@@ -250,50 +250,43 @@ def tile_moe_uni_silu_kernel(
             else:
                 nc.scalar.copy(cp[:, :, :, t0 : t0 + n], back[:].bitcast(BF16).rearrange("p u (t e) -> p u e t", e=2))
 
-        woven = [
-            mid.tile([P, n, 2], U32, name=f"woven{i}", align_bytes=64, offset=at2)
-            for i, (n, at2) in enumerate(((512, 0), (512, 4096), (256, 8192)))
-        ]
-        pl = [mid.tile([P, 2, 512], U32, name=f"pl{i}", align_bytes=64, offset=12288 + 4096 * i) for i in range(2)]
         qw = keep.tile([P, S], U32, name="qw", align_bytes=64)
         qs = keep.tile([P, S], U8, name="qs", align_bytes=64)
+        woven = [mid.tile([P, 512, 2], U32, name=f"woven{i}", align_bytes=64, offset=4096 * i) for i in range(2)]
+        shares = ((896, 256), (1152, P))
+        singles = [keep.tile([P, n, 4], BF16, name=f"singles{s0}", align_bytes=64) for s0, n in shares]
 
         def pairs(dst, u, s0, n):
             nc.vector.tensor_copy(dst, cw[:, u, :].bitcast(U32).indirect(part(l_offs2, s0, n)))
 
         def single(t):
-            dst = woven[2][:].bitcast(BF16).rearrange("p n t -> p t n")[:, t, :]
-            nc.scalar.activation(dst, cp[:, t // 2, t % 2, :].indirect(part(l_offs2, 1024, 256)), COPY)
+            for dst, (s0, n) in zip(singles, shares):
+                nc.scalar.activation(dst[:, :, t], cp[:, t // 2, t % 2, :].indirect(part(l_offs2, s0, n)), COPY)
 
-        def weave(i, j0, n):
-            nc.scalar.copy(woven[i][:, j0 : j0 + n, :], pl[i][:, :, j0 : j0 + n].rearrange("p u n -> p n u"))
+        def quantise(src, s0, n, words, w0):
+            nc.vector.quantize_mx(out=words[:, s0 - w0 : s0 - w0 + n].bitcast(FP8X4), scales=qs[:, s0 : s0 + n], in_=src)
 
-        def quantise(src, s0, n):
-            nc.vector.quantize_mx(
-                out=qw[:, s0 : s0 + n].bitcast(FP8X4),
-                scales=qs[:, s0 : s0 + n],
-                in_=src.rearrange("p n u -> p (n u)").bitcast(BF16),
-            )
-
-        for i in range(2):
+        for t in range(4):
+            single(t)
+        for i, (s0, n) in enumerate(((0, 512), (512, 384))):
+            pl = keep.tile([P, 2, n], U32, name=f"pl{s0}", align_bytes=64)
             for u in range(2):
-                pairs(pl[i][:, u, :], u, 512 * i, 512)
-        single(0)
-        weave(0, 0, 512)
-        single(1)
-        weave(1, 0, 256)
-        single(2)
-        weave(1, 256, 256)
-        single(3)
-        quantise(woven[0][:], 0, 512)
-        quantise(woven[1][:, 0:256, :], 512, 256)
+                pairs(pl[:, u, :], u, s0, n)
+            nc.gpsimd.tensor_copy(woven[i][:, 0:n, :], pl[:].rearrange("p u n -> p n u"))
+        quantise(woven[0][:].rearrange("p n u -> p (n u)").bitcast(BF16), 0, 512, qw, 0)
         last = mid.tile([P, 256, 2], U32, name="last", align_bytes=64, offset=0)
         for u in range(2):
             pairs(last[:, :, u], u, 1280, 256)
-        quantise(woven[1][:, 256:512, :], 768, 256)
-        quantise(last[:], 1280, 256)
-        quantise(woven[2][:], 1024, 256)
-        operands = [(qw[:, e * C : (e + 1) * C], qs[:, e * C : (e + 1) * C]) for e in range(E)]
+        for j0, n in ((0, 256), (256, P)):
+            quantise(woven[1][:, j0 : j0 + n, :].rearrange("p n u -> p (n u)").bitcast(BF16), 512 + j0, n, qw, 0)
+        quantise(last[:].rearrange("p n u -> p (n u)").bitcast(BF16), 1280, 256, qw, 0)
+        qw2 = mid.tile([P, 384], U32, name="qw2", align_bytes=64, offset=4096)
+        for src, (s0, n) in zip(singles, shares):
+            quantise(src[:].rearrange("p n t -> p (n t)"), s0, n, qw2, 896)
+        operands = [
+            (qw2[:, (e - 7) * C : (e - 6) * C] if 7 <= e < 10 else qw[:, e * C : (e + 1) * C], qs[:, e * C : (e + 1) * C])
+            for e in range(E)
+        ]
         z, at = experts(operands, "z", EARLY2, free[2], lambda: None)
         free = [(at - 5 + k) % 8 for k in range(8)]
 

@@ -26,7 +26,7 @@ TINY = 2.0**-60
 BANK = 2048
 G1 = (512, 512, 384, 128)
 EARLY1 = ((0, 0, 4), (0, 4, 4), (1, 0, 4), (0, 8, 3), (0, 11, 1))
-EARLY2 = ((0, 0, 4), (0, 4, 3), (0, 10, 2), (0, 7, 3))
+EARLY2 = ((0, 0, 4), (1, 0, 4), (2, 0, 4), (0, 4, 3), (0, 10, 2), (0, 7, 3))
 G2 = ((512, False), (512, False), (384, False), (128, True))
 WOVEN_AT = (0, 4096, 8192, 4096)
 PLANES_AT = (12288, 16384, 0)
@@ -153,13 +153,13 @@ def tile_moe_uni_silu_kernel(
                     between()
             return planes, (at + len(order)) % 8
 
-        def combine(y, lst_a, lst_b, ratio, pieces, order, name, after):
+        def combine(y, lst_a, lst_b, ratio, pieces, slots, order, name, after):
             sums = [keep.tile([P, T], F32, name=f"{name}{b}") for b in range(4)]
             held = {}
             for kind, i in order:
                 b, t0, n = pieces[i]
                 if kind == "a":
-                    a = first.tile([P, T], F32, name=f"{name}_a{i}", offset=4 * T * (i % A_SLOTS))
+                    a = first.tile([P, n], F32, name=f"{name}_a{i}", offset=4 * (T * slots[i] + t0))
                     nc.vector.tensor_tensor(a[:, 0:n], y[b][:].indirect(part(lst_a, t0, n)), ratio[:, t0 : t0 + n], MULT)
                     held[i] = a
                 if kind == "b":
@@ -241,7 +241,7 @@ def tile_moe_uni_silu_kernel(
                     nc.scalar.copy(cw[:, :, some[0] * P : (some[-1] + 1) * P], back[:])
                 backs.append((back, some[0] * P, len(some) * P))
 
-        combine(y, l_pos1, l_pos2, ratio1, pieces, lagged(len(pieces)), "c", after1)
+        combine(y, l_pos1, l_pos2, ratio1, pieces, (0, 1, 2, 0, 1, 2, 0, 1), lagged(len(pieces)), "c", after1)
 
         for back, t0, n in backs:
             if t0 < TAIL[1][0]:
@@ -252,7 +252,9 @@ def tile_moe_uni_silu_kernel(
 
         qw = keep.tile([P, S], U32, name="qw", align_bytes=64)
         qs = keep.tile([P, S], U8, name="qs", align_bytes=64)
-        woven = [mid.tile([P, 512, 2], U32, name=f"woven{i}", align_bytes=64, offset=4096 * i) for i in range(2)]
+        woven = [
+            mid.tile([P, n, 2], U32, name=f"woven{i}", align_bytes=64, offset=2048 * i) for i, n in enumerate((512, 384))
+        ]
         shares = ((896, 256), (1152, P))
         singles = [keep.tile([P, n, 4], BF16, name=f"singles{s0}", align_bytes=64) for s0, n in shares]
 
@@ -268,19 +270,22 @@ def tile_moe_uni_silu_kernel(
 
         for t in range(4):
             single(t)
-        for i, (s0, n) in enumerate(((0, 512), (512, 384))):
-            pl = keep.tile([P, 2, n], U32, name=f"pl{s0}", align_bytes=64)
-            for u in range(2):
-                pairs(pl[:, u, :], u, s0, n)
-            nc.gpsimd.tensor_copy(woven[i][:, 0:n, :], pl[:].rearrange("p u n -> p n u"))
+        pl = [keep.tile([P, 2, n], U32, name=f"pl{n}", align_bytes=64) for n in (512, 384)]
+        pairs(pl[0][:, 0, :], 0, 0, 512)
+        for j0 in (0, 256):
+            pairs(pl[0][:, 1, j0 : j0 + 256], 1, j0, 256)
+            nc.gpsimd.tensor_copy(woven[0][:, j0 : j0 + 256, :], pl[0][:, :, j0 : j0 + 256].rearrange("p u n -> p n u"))
+        for u in range(2):
+            pairs(pl[1][:, u, :], u, 512, 384)
         quantise(woven[0][:].rearrange("p n u -> p (n u)").bitcast(BF16), 0, 512, qw, 0)
+        nc.gpsimd.tensor_copy(woven[1][:], pl[1][:].rearrange("p u n -> p n u"))
         last = mid.tile([P, 256, 2], U32, name="last", align_bytes=64, offset=0)
         for u in range(2):
             pairs(last[:, :, u], u, 1280, 256)
         for j0, n in ((0, 256), (256, P)):
             quantise(woven[1][:, j0 : j0 + n, :].rearrange("p n u -> p (n u)").bitcast(BF16), 512 + j0, n, qw, 0)
         quantise(last[:].rearrange("p n u -> p (n u)").bitcast(BF16), 1280, 256, qw, 0)
-        qw2 = mid.tile([P, 384], U32, name="qw2", align_bytes=64, offset=4096)
+        qw2 = mid.tile([P, 384], U32, name="qw2", align_bytes=64, offset=3072)
         for src, (s0, n) in zip(singles, shares):
             quantise(src[:].rearrange("p n t -> p (n t)"), s0, n, qw2, 896)
         operands = [
@@ -290,7 +295,7 @@ def tile_moe_uni_silu_kernel(
         z, at = experts(operands, "z", EARLY2, free[2], lambda: None)
         free = [(at - 5 + k) % 8 for k in range(8)]
 
-        pieces2 = [(0, 0, 384), (0, 384, 384), (1, 0, T), (2, 0, T)] + [(3, t0, n) for t0, n in TAIL]
+        pieces2 = [(0, 0, 384), (0, 384, 384), (1, 0, T), (2, 0, T), (3, 640, P), (3, 0, 384), (3, 384, 256)]
         back2_at = ((2, 3), (4, 5), (2, 3))
 
         def after2(i, sums):
@@ -318,5 +323,6 @@ def tile_moe_uni_silu_kernel(
                 nc.scalar.copy(res[:, 384 * k : 384 * (k + 1)], back[:].rearrange("p j t -> p (j t)"))
                 nc.scalar.dma_start(out[b * P : (b + 1) * P, 384 * k : 384 * (k + 1)], res[:, 384 * k : 384 * (k + 1)])
 
-        order2 = lagged(4) + [("a", 4), ("a", 5), ("b", 4), ("a", 6), ("c", 4), ("b", 5), ("b", 6), ("c", 5), ("c", 6)]
-        combine(z, l_pos3, l_pos4, ratio2, pieces2, order2, "o", after2)
+        order2 = lagged(2)[:-2] + [("a", 2), ("b", 1), ("c", 1), ("b", 2), ("c", 2), ("a", 3), ("a", 4), ("b", 3)]
+        order2 = order2 + [("c", 3), ("b", 4), ("a", 5), ("a", 6), ("c", 4), ("b", 5), ("b", 6), ("c", 5), ("c", 6)]
+        combine(z, l_pos3, l_pos4, ratio2, pieces2, (0, 0, 1, 2, 0, 2, 2), order2, "o", after2)

@@ -295,7 +295,8 @@ def tile_moe_uni_silu_kernel(
         z, at = experts(operands, "z", EARLY2, free[2], lambda: None)
         free = [(at - 5 + k) % 8 for k in range(8)]
 
-        pieces2 = [(0, 0, 384), (0, 384, 384), (1, 0, T), (2, 0, T), (3, 640, P), (3, 0, 384), (3, 384, 256)]
+        pieces2 = [(0, 0, 384), (0, 384, 384), (1, 0, T), (2, 0, 384), (2, 384, 384)]
+        pieces2 = pieces2 + [(3, t0, n) for t0, n in TAIL]
         back2_at = ((2, 3), (4, 5), (2, 3))
 
         def after2(i, sums):
@@ -324,5 +325,6 @@ def tile_moe_uni_silu_kernel(
                 nc.scalar.dma_start(out[b * P : (b + 1) * P, 384 * k : 384 * (k + 1)], res[:, 384 * k : 384 * (k + 1)])
 
         order2 = lagged(2)[:-2] + [("a", 2), ("b", 1), ("c", 1), ("b", 2), ("c", 2), ("a", 3), ("a", 4), ("b", 3)]
-        order2 = order2 + [("c", 3), ("b", 4), ("a", 5), ("a", 6), ("c", 4), ("b", 5), ("b", 6), ("c", 5), ("c", 6)]
-        combine(z, l_pos3, l_pos4, ratio2, pieces2, (0, 0, 1, 2, 0, 2, 2), order2, "o", after2)
+        order2 = order2 + [("c", 3), ("b", 4), ("c", 4), ("a", 5), ("a", 6), ("b", 5), ("a", 7), ("c", 5), ("b", 6)]
+        order2 = order2 + [("b", 7), ("c", 6), ("c", 7)]
+        combine(z, l_pos3, l_pos4, ratio2, pieces2, (0, 0, 1, 2, 2, 2, 2, 2), order2, "o", after2)

@@ -25,7 +25,7 @@ COPY = mybir.ActivationFunctionType.Copy
 TINY = 2.0**-60
 BANK = 2048
 G1 = (512, 512, 384, 128)
-EARLY1 = ((0, 0, 4), (0, 4, 4), (1, 0, 4), (0, 8, 3), (0, 11, 1))
+EARLY1 = ((0, 0, 4), (0, 4, 4), (0, 8, 3), (0, 11, 1))
 EARLY2 = ((0, 0, 4), (1, 0, 4), (2, 0, 4), (0, 4, 3), (0, 10, 2), (0, 7, 3))
 G2 = ((512, False), (512, False), (384, False), (128, True))
 WOVEN_AT = (0, 4096, 8192, 4096)
@@ -75,9 +75,10 @@ def tile_moe_uni_silu_kernel(
             return ratio
 
         xs = keep.tile([P, T], U8, name="xs", align_bytes=64)
-        ws = keep.tile([P, E, K], U8, name="ws", align_bytes=64)
+        ws = [keep.tile([P, E, K // 2], U8, name=f"ws{h}", align_bytes=64) for h in range(2)]
         nc.gpsimd.memset(xs[:].bitcast(I32), 0)
-        nc.vector.memset(ws[:].rearrange("p e n -> p (e n)").bitcast(I32), 0)
+        for h in range(2):
+            nc.vector.memset(ws[h][:].rearrange("p e n -> p (e n)").bitcast(I32), 0)
         rows = keep.tile([P, T // 2], F32, name="rows")
         nc.gpsimd.memset(rows[:], 0.0)
         ident = keep.tile([P, P], F32, name="ident")
@@ -93,11 +94,15 @@ def tile_moe_uni_silu_kernel(
             nc.sync.dma_start(rows[4 * step : 4 * step + 4, :], flat[2 * P - 2 : 2 * P + 2, :])
         xw = keep.tile([P, T], I32, name="xw", align_bytes=64)
         nc.sync.dma_start(xw[:], x_words[0].rearrange("p t d -> p (t d)").bitcast(I32))
-        for r in range(4):
-            nc.sync.dma_start(
-                ws[r:P:32, :, :].bitcast(I32),
-                w_scales[:, 0, r:16:4, :].rearrange("e q n -> q e n").bitcast(I32),
-            )
+
+        def load_scales(h):
+            for r in range(4):
+                nc.sync.dma_start(
+                    ws[h][r:P:32, :, :].bitcast(I32),
+                    w_scales[:, 0, r:16:4, 256 * h : 256 * (h + 1)].rearrange("e q n -> q e n").bitcast(I32),
+                )
+
+        load_scales(0)
         ww = []
         for g in range(3):
             t = keep.tile([P, 4, 2 * K], U8, name=f"ww{g}", align_bytes=64)
@@ -105,6 +110,7 @@ def tile_moe_uni_silu_kernel(
                 t[:].bitcast(I32), w_words[4 * g : 4 * g + 4, 0].rearrange("e p n -> p e n").bitcast(I32)
             )
             ww.append(t)
+        load_scales(1)
         l_pos1 = load_list(pos1, "l_pos1")
         l_pos2 = load_list(pos2, "l_pos2")
         l_offs2 = load_list(offs2, "l_offs2")
@@ -142,7 +148,7 @@ def tile_moe_uni_silu_kernel(
                     nc.tensor.matmul_mx(
                         out=acc[:, j * C : (j + 1) * C],
                         lhsT=ww[e // 4][:, e % 4, 256 * b : 256 * (b + 1)].bitcast(FP4X4),
-                        lhsT_scale=ws[:, e, P * b : P * (b + 1)],
+                        lhsT_scale=ws[b // 2][:, e, P * (b % 2) : P * (b % 2 + 1)],
                         rhs=words.bitcast(FP8X4),
                         rhs_scale=scales,
                         start=True,
@@ -194,12 +200,12 @@ def tile_moe_uni_silu_kernel(
         y, at = experts(operands, "y", EARLY1, 3, lambda: None)
         ratio1 = ratios[0]
         ratio2 = spread(rcol, 1, at)
-        free = [(at + 2 + k) % 8 for k in range(8)]
+        free = [(at - 3 + k) % 8 for k in range(8)]
 
         pieces = [(0, 0, T), (1, 0, T)] + [(b, t0, n) for t0, n in TAIL for b in (2, 3)]
         ct = [keep.tile([P, 2, 256], BF16, name=f"ct{j}", align_bytes=64) for j in range(NB)]
         cw = keep.tile([P, 2, T], F32, name="cw", align_bytes=64)
-        cp = keep.tile([P, 2, 2, T], BF16, name="cp", align_bytes=64)
+        cp = first.tile([P, 2, 2, T], BF16, name="cp", align_bytes=64, offset=4 * T + 4 * TAIL[2][0])
         banks = {}
 
         def turn(sums, b, t0, n, step, slot_of):
@@ -209,9 +215,9 @@ def tile_moe_uni_silu_kernel(
                     banks[key] = bank_tile(free[slot_of(j)], [P, 2, 2, P])
                 nc.tensor.transpose(banks[key][:, j % 2, b % 2, :], sums[b][:, j * P : (j + 1) * P], ident[:])
 
-        slot1 = ((0, 0, 1, 1, 2, 2), (3, 3, 4, 3, 3, 4))
+        slot1 = ((0, 0, 1, 1, 2, 2), (3, 3, 4, 3, 4, 5))
         backs = []
-        back_at = {0: (5, 6), 384: (0,), 640: (1,)}
+        back_at = {0: ((5, (0, 1)), (6, (2,))), 384: ((2, (4,)), (0, (3,))), 640: ((1, (5,)),)}
 
         def after1(i, sums):
             b, t0, n = pieces[i]
@@ -223,19 +229,18 @@ def tile_moe_uni_silu_kernel(
             for j in blocks:
                 dst = ct[j][:, :, P * pair : P * (pair + 1)].rearrange("p u (m e) -> p u m e", e=2)
                 src = banks[(0, pair, t0, slot1[pair][j])][:, j % 2].rearrange("p h (m u e) -> p u (h m) e", u=2, e=2)
-                if i == len(pieces) - 1:
+                if pair == 1 and j >= 4:
                     nc.vector.tensor_scalar(dst, src, factor(0, j), None, MULT)
                 else:
                     nc.scalar.activation(dst, src, COPY, scale=factor(0, j))
             if pair == 0:
                 return
-            for k, at2 in enumerate(back_at[t0]):
-                some = blocks[2 * k : 2 * k + 2]
+            for at2, some in back_at[t0]:
                 back = bank_tile(free[at2], [P, 2, len(some) * P])
                 for m, j in enumerate(some):
                     for u in range(2):
                         nc.tensor.transpose(back[:, u, m * P : (m + 1) * P], ct[j][:].bitcast(F32)[:, u, :], ident[:])
-                if i == len(pieces) - 1:
+                if some[0] >= 4:
                     nc.vector.tensor_copy(cw[:, :, some[0] * P : (some[-1] + 1) * P], back[:])
                 else:
                     nc.scalar.copy(cw[:, :, some[0] * P : (some[-1] + 1) * P], back[:])
@@ -246,7 +251,7 @@ def tile_moe_uni_silu_kernel(
         for back, t0, n in backs:
             if t0 < TAIL[1][0]:
                 src = cw[:].bitcast(BF16)[:, :, 2 * t0 : 2 * (t0 + n)].rearrange("p u (t e) -> p u e t", e=2)
-                nc.vector.tensor_copy(cp[:, :, :, t0 : t0 + n], src)
+                nc.gpsimd.tensor_copy(cp[:, :, :, t0 : t0 + n], src)
             else:
                 nc.scalar.copy(cp[:, :, :, t0 : t0 + n], back[:].bitcast(BF16).rearrange("p u (t e) -> p u e t", e=2))
 

@@ -26,7 +26,7 @@ TINY = 2.0**-60
 BANK = 2048
 G1 = (512, 512, 384, 128)
 EARLY1 = ((0, 0, 4), (0, 4, 4), (0, 8, 3), (0, 11, 1))
-EARLY2 = ((0, 0, 4), (1, 0, 4), (2, 0, 4), (0, 4, 3), (0, 10, 2), (0, 7, 3))
+EARLY2 = ((0, 0, 4), (1, 0, 4), (2, 0, 4), (0, 4, 3), (0, 10, 2), (0, 8, 2), (0, 7, 1))
 G2 = ((512, False), (512, False), (384, False), (128, True))
 WOVEN_AT = (0, 4096, 8192, 4096)
 PLANES_AT = (12288, 16384, 0)
@@ -260,7 +260,7 @@ def tile_moe_uni_silu_kernel(
         woven = [
             mid.tile([P, n, 2], U32, name=f"woven{i}", align_bytes=64, offset=2048 * i) for i, n in enumerate((512, 384))
         ]
-        shares = ((896, 256), (1152, P))
+        shares = ((1024, 256), (896, P))
         singles = [keep.tile([P, n, 4], BF16, name=f"singles{s0}", align_bytes=64) for s0, n in shares]
 
         def pairs(dst, u, s0, n):

@@ -25,13 +25,8 @@ COPY = mybir.ActivationFunctionType.Copy
 TINY = 2.0**-60
 BANK = 2048
 G1 = (512, 512, 384, 128)
-EARLY1 = ((0, 0, 4), (0, 4, 4), (0, 8, 3), (0, 11, 1))
+EARLY1 = ((0, 0, 4), (1, 0, 4), (0, 4, 4), (1, 4, 4), (0, 8, 3), (0, 11, 1))
 EARLY2 = ((0, 0, 4), (1, 0, 4), (2, 0, 4), (0, 4, 3), (0, 10, 2), (0, 8, 2), (0, 7, 1))
-G2 = ((512, False), (512, False), (384, False), (128, True))
-WOVEN_AT = (0, 4096, 8192, 4096)
-PLANES_AT = (12288, 16384, 0)
-QUANT = {512: (512,), 384: (256, 128), 128: (128,)}
-A_SLOTS = 3
 TAIL = ((0, 384), (384, 256), (640, 128))
 
 
@@ -45,7 +40,6 @@ def tile_moe_uni_silu_kernel(
     nc = tc.nc
     with ExitStack() as ctx:
         keep = ctx.enter_context(tc.tile_pool(name="keep", bufs=1))
-        first = ctx.enter_context(tc.tile_pool(name="first", bufs=1))
         early = ctx.enter_context(tc.tile_pool(name="early", bufs=1))
         mid = ctx.enter_context(tc.tile_pool(name="mid", bufs=1))
         psum = ctx.enter_context(tc.psum_pool(name="psum", bufs=1))
@@ -136,12 +130,12 @@ def tile_moe_uni_silu_kernel(
         def factor(step, j):
             return cols[:, j % 3, step, 1, j // 3 : j // 3 + 1]
 
-        def experts(operands, name, first_banks, at, between):
+        def experts(operands, name, first_banks, banks, between):
             planes = [keep.tile([P, S], F32, name=f"{name}{b}") for b in range(4)]
             done = [(b, e) for b, e0, ne in first_banks for e in range(e0, e0 + ne)]
             order = list(first_banks) + [(b, e0, 4) for b in range(4) for e0 in range(0, E, 4) if (b, e0) not in done]
             for i, (b, e0, ne) in enumerate(order):
-                acc = bank_tile((at + i) % 8, [P, ne * C])
+                acc = bank_tile(banks[i], [P, ne * C])
                 for j in range(ne):
                     e = e0 + j
                     words, scales = operands[e]
@@ -155,31 +149,29 @@ def tile_moe_uni_silu_kernel(
                         stop=True,
                     )
                 nc.scalar.activation(planes[b][:, e0 * C : (e0 + ne) * C], acc[:], SILU)
-                if i == 1:
-                    between()
-            return planes, (at + len(order)) % 8
+                between(i, planes)
+            return planes
 
-        def combine(y, lst_a, lst_b, ratio, pieces, slots, order, name, after):
-            sums = [keep.tile([P, T], F32, name=f"{name}{b}") for b in range(4)]
-            held = {}
-            for kind, i in order:
-                b, t0, n = pieces[i]
-                if kind == "a":
-                    a = first.tile([P, n], F32, name=f"{name}_a{i}", offset=4 * (T * slots[i] + t0))
-                    nc.vector.tensor_tensor(a[:, 0:n], y[b][:].indirect(part(lst_a, t0, n)), ratio[:, t0 : t0 + n], MULT)
-                    held[i] = a
-                if kind == "b":
-                    nc.vector.tensor_tensor(
-                        sums[b][:, t0 : t0 + n], y[b][:].indirect(part(lst_b, t0, n)), held[i][:, 0:n], ADD
-                    )
-                if kind == "c":
-                    after(i, sums)
+        def gathered(name, n):
+            return keep.tile([P, n], F32, name=name)
 
-        def lagged(count):
-            order = [("a", 0)]
-            for i in range(1, count):
-                order = order + [("a", i), ("b", i - 1), ("c", i - 1)]
-            return order + [("b", count - 1), ("c", count - 1)]
+        def times_ratio(y, lst, ratio, t0, n, name):
+            a = gathered(name, n)
+            nc.vector.tensor_tensor(a[:], y[:].indirect(part(lst, t0, n)), ratio[:, t0 : t0 + n], MULT)
+            return a
+
+        def plus(y, lst, a, t0, n, name):
+            s = gathered(name, n)
+            nc.vector.tensor_tensor(s[:], y[:].indirect(part(lst, t0, n)), a, ADD)
+            return s
+
+        def plain(y, lst, t0, n, name):
+            b = gathered(name, n)
+            nc.scalar.activation(b[:], y[:].indirect(part(lst, t0, n)), COPY)
+            return b
+
+        def turn(dst, src, start, stop):
+            nc.tensor.matmul(dst, src, ident[:], start=start, stop=stop, is_transpose=True)
 
         gs = [early.tile([P, 512], U8, name=f"gs{i}", align_bytes=64, offset=512 * i) for i in range(3)]
         gw = [
@@ -196,59 +188,73 @@ def tile_moe_uni_silu_kernel(
             for i, (s0, n) in enumerate(zip(starts(G1), G1))
             for j in range(0, n, C)
         ]
-        ratios = [spread(rcol, 0, 1)]
-        y, at = experts(operands, "y", EARLY1, 3, lambda: None)
-        ratio1 = ratios[0]
-        ratio2 = spread(rcol, 1, at)
-        free = [(at - 3 + k) % 8 for k in range(8)]
+        ratio1 = spread(rcol, 0, 1)
+        ratio2 = spread(rcol, 1, 6)
+        y = experts(operands, "y", EARLY1, [(3 + i) % 8 for i in range(13)], lambda i, planes: None)
 
-        pieces = [(0, 0, T), (1, 0, T)] + [(b, t0, n) for t0, n in TAIL for b in (2, 3)]
         ct = [keep.tile([P, 2, 256], BF16, name=f"ct{j}", align_bytes=64) for j in range(NB)]
         cw = keep.tile([P, 2, T], F32, name="cw", align_bytes=64)
-        cp = first.tile([P, 2, 2, T], BF16, name="cp", align_bytes=64, offset=4 * T + 4 * TAIL[2][0])
-        banks = {}
+        cp = keep.tile([P, 2, 2, T], BF16, name="cp", align_bytes=64)
+        tok = [bank_tile(j, [P, 4, P]) for j in range(NB)]
 
-        def turn(sums, b, t0, n, step, slot_of):
-            for j in range(t0 // P, (t0 + n) // P):
-                key = (step, b // 2, t0, slot_of(j))
-                if key not in banks:
-                    banks[key] = bank_tile(free[slot_of(j)], [P, 2, 2, P])
-                nc.tensor.transpose(banks[key][:, j % 2, b % 2, :], sums[b][:, j * P : (j + 1) * P], ident[:])
+        def turn1(src, b, t0, n, start=False, stop=False):
+            for m in range(n // P):
+                turn(tok[t0 // P + m][:, b, :], src[:, m * P : (m + 1) * P], start, stop)
 
-        slot1 = ((0, 0, 1, 1, 2, 2), (3, 3, 4, 3, 4, 5))
-        backs = []
-        back_at = {0: ((5, (0, 1)), (6, (2,))), 384: ((2, (4,)), (0, (3,))), 640: ((1, (5,)),)}
+        def scale1(j, eng):
+            dst = ct[j][:].rearrange("p u (m e) -> p u m e", e=2)
+            src = tok[j][:].rearrange("p h (m u e) -> p u (h m) e", u=2, e=2)
+            if eng == "v":
+                nc.vector.tensor_scalar(dst, src, factor(0, j), None, MULT)
+            else:
+                nc.scalar.activation(dst, src, COPY, scale=factor(0, j))
 
-        def after1(i, sums):
-            b, t0, n = pieces[i]
-            pair = b // 2
-            turn(sums, b, t0, n, 0, lambda j: slot1[pair][j])
-            if b % 2 == 0:
-                return
-            blocks = range(t0 // P, (t0 + n) // P)
-            for j in blocks:
-                dst = ct[j][:, :, P * pair : P * (pair + 1)].rearrange("p u (m e) -> p u m e", e=2)
-                src = banks[(0, pair, t0, slot1[pair][j])][:, j % 2].rearrange("p h (m u e) -> p u (h m) e", u=2, e=2)
-                if pair == 1 and j >= 4:
-                    nc.vector.tensor_scalar(dst, src, factor(0, j), None, MULT)
-                else:
-                    nc.scalar.activation(dst, src, COPY, scale=factor(0, j))
-            if pair == 0:
-                return
-            for at2, some in back_at[t0]:
-                back = bank_tile(free[at2], [P, 2, len(some) * P])
-                for m, j in enumerate(some):
-                    for u in range(2):
-                        nc.tensor.transpose(back[:, u, m * P : (m + 1) * P], ct[j][:].bitcast(F32)[:, u, :], ident[:])
-                if some[0] >= 4:
-                    nc.vector.tensor_copy(cw[:, :, some[0] * P : (some[-1] + 1) * P], back[:])
-                else:
-                    nc.scalar.copy(cw[:, :, some[0] * P : (some[-1] + 1) * P], back[:])
-                backs.append((back, some[0] * P, len(some) * P))
+        def back1(some, at):
+            back = bank_tile(at, [P, 2, len(some) * P])
+            for m, j in enumerate(some):
+                for u in range(2):
+                    nc.tensor.transpose(back[:, u, m * P : (m + 1) * P], ct[j][:].bitcast(F32)[:, u, :], ident[:])
+            return back, some[0] * P, len(some) * P
 
-        combine(y, l_pos1, l_pos2, ratio1, pieces, (0, 1, 2, 0, 1, 2, 0, 1), lagged(len(pieces)), "c", after1)
+        def words1(back, t0, n, eng):
+            (nc.vector.tensor_copy if eng == "v" else nc.scalar.copy)(cw[:, :, t0 : t0 + n], back[:])
 
-        for back, t0, n in backs:
+        (t0, n0), (t1, n1), (t2, n2) = TAIL
+        a0 = times_ratio(y[0], l_pos1, ratio1, 0, T, "a0")
+        a1 = times_ratio(y[1], l_pos1, ratio1, 0, T, "a1")
+        turn1(a1, 1, 0, T, start=True)
+        turn1(plus(y[0], l_pos2, a0[:, t0 : t0 + n0], t0, n0, "s00"), 0, t0, n0)
+        for b in (1, 2, 3):
+            if b > 1:
+                turn1(times_ratio(y[b], l_pos1, ratio1, t0, n0, f"a{b}0"), b, t0, n0)
+            turn1(plain(y[b], l_pos2, t0, n0, f"b{b}0"), b, t0, n0, stop=b == 3)
+        turn1(plus(y[0], l_pos2, a0[:, t1 : t1 + n1], t1, n1, "s01"), 0, t1, n1)
+        turn1(plain(y[1], l_pos2, t1, n1, "b11"), 1, t1, n1)
+        a31 = times_ratio(y[3], l_pos1, ratio1, t1, n1, "a31")
+        turn1(plain(y[2], l_pos2, t1, n1, "b21"), 2, t1, n1)
+        turn1(times_ratio(y[2], l_pos1, ratio1, t1, n1, "a21"), 2, t1, n1)
+        for j in (0, 1):
+            scale1(j, "s")
+        back01 = back1((0, 1), 6)
+        scale1(2, "s")
+        back2 = back1((2,), 7)
+        turn1(plus(y[3], l_pos2, a31[:], t1, n1, "s31"), 3, t1, n1, stop=True)
+        a32 = times_ratio(y[3], l_pos1, ratio1, t2, n2, "a32")
+        turn1(plus(y[0], l_pos2, a0[:, t2 : t2 + n2], t2, n2, "s02"), 0, t2, n2)
+        for b in (1, 2):
+            turn1(plain(y[b], l_pos2, t2, n2, f"b{b}2"), b, t2, n2)
+        turn1(times_ratio(y[2], l_pos1, ratio1, t2, n2, "a22"), 2, t2, n2)
+        turn1(plus(y[3], l_pos2, a32[:], t2, n2, "s32"), 3, t2, n2, stop=True)
+        words1(*back01, "v")
+        words1(*back2, "v")
+        for j in (3, 4):
+            scale1(j, "s")
+        scale1(5, "v")
+        back34 = back1((3, 4), 0)
+        back5 = back1((5,), 1)
+        words1(*back34, "s")
+        words1(*back5, "v")
+        for back, t0, n in (back01, back2, back34, back5):
             if t0 < TAIL[1][0]:
                 src = cw[:].bitcast(BF16)[:, :, 2 * t0 : 2 * (t0 + n)].rearrange("p u (t e) -> p u e t", e=2)
                 nc.gpsimd.tensor_copy(cp[:, :, :, t0 : t0 + n], src)
@@ -297,39 +303,65 @@ def tile_moe_uni_silu_kernel(
             (qw2[:, (e - 7) * C : (e - 6) * C] if 7 <= e < 10 else qw[:, e * C : (e + 1) * C], qs[:, e * C : (e + 1) * C])
             for e in range(E)
         ]
-        z, at = experts(operands, "z", EARLY2, free[2], lambda: None)
-        free = [(at - 5 + k) % 8 for k in range(8)]
+        held = {}
 
-        pieces2 = [(0, 0, 384), (0, 384, 384), (1, 0, T), (2, 0, 384), (2, 384, 384)]
-        pieces2 = pieces2 + [(3, t0, n) for t0, n in TAIL]
-        back2_at = ((2, 3), (4, 5), (2, 3))
+        def between(i, planes):
+            if i == 8:
+                held[0] = plain(planes[0], l_pos4, 0, T, "d0")
 
-        def after2(i, sums):
-            b, t0, n = pieces2[i]
-            if b == 3:
-                res = keep.tile([P, n], F32, name=f"res{i}")
-                nc.vector.scalar_tensor_tensor(
-                    res[:], q2[:, t0 - q2_from : t0 - q2_from + n], TINY, sums[b][:, t0 : t0 + n], ADD, MULT
-                )
-                nc.sync.dma_start(out[b * P : (b + 1) * P, t0 : t0 + n], res[:])
-                return
-            res = keep.tile([P, T], F32, name=f"res{i}")
-            for k in range(t0 // 384, (t0 + n) // 384):
-                at2 = back2_at[b][k]
-                there = bank_tile(free[k], [P, 3, P])
+        z = experts(operands, "z", EARLY2, (2, 3, 4, 5, 6, 7, 0, 1, 2, 3, 0, 1, 2, 3), between)
+
+        H = T // 2
+
+        def there(src, banks, halves, start, stop):
+            for k in halves:
                 for m in range(3):
                     j = 3 * k + m
-                    nc.tensor.transpose(there[:, m, :], sums[b][:, j * P : (j + 1) * P], ident[:])
-                st = keep.tile([P, 3, P], F32, name=f"st{b}{k}")
-                for m in range(3):
-                    nc.scalar.activation(st[:, m, :], there[:, m, :], COPY, scale=factor(1, 3 * k + m))
-                back = bank_tile(free[at2], [P, 3, P])
-                for m in range(3):
-                    nc.tensor.transpose(back[:, m, :], st[:, m, :], ident[:])
-                nc.scalar.copy(res[:, 384 * k : 384 * (k + 1)], back[:].rearrange("p j t -> p (j t)"))
-                nc.scalar.dma_start(out[b * P : (b + 1) * P, 384 * k : 384 * (k + 1)], res[:, 384 * k : 384 * (k + 1)])
+                    turn(banks[k][:, m, :], src[:, j * P : (j + 1) * P], start and m == 0, stop and m == 2)
 
-        order2 = lagged(2)[:-2] + [("a", 2), ("b", 1), ("c", 1), ("b", 2), ("c", 2), ("a", 3), ("a", 4), ("b", 3)]
-        order2 = order2 + [("c", 3), ("b", 4), ("c", 4), ("a", 5), ("a", 6), ("b", 5), ("a", 7), ("c", 5), ("b", 6)]
-        order2 = order2 + [("b", 7), ("c", 6), ("c", 7)]
-        combine(z, l_pos3, l_pos4, ratio2, pieces2, (0, 0, 1, 2, 2, 2, 2, 2), order2, "o", after2)
+        def again(bank, at, name):
+            st = keep.tile([P, 3, P], F32, name=name)
+            nc.scalar.copy(st[:], bank[:])
+            back = bank_tile(at, [P, 3, P])
+            for m in range(3):
+                nc.tensor.transpose(back[:, m, :], st[:, m, :], ident[:])
+            return back[:].rearrange("p j t -> p (j t)")
+
+        def finish(src, b, t0, n):
+            res = keep.tile([P, n], F32, name=f"res{b}_{t0}")
+            nc.vector.scalar_tensor_tensor(res[:], q2[:, t0 : t0 + n], TINY, src, ADD, MULT)
+            nc.sync.dma_start(out[b * P : (b + 1) * P, t0 : t0 + n], res[:])
+
+        c0 = times_ratio(z[0], l_pos3, ratio2, 0, T, "c0")
+        tb0 = [bank_tile(4 + k, [P, 3, P]) for k in range(2)]
+        there(c0, tb0, (0, 1), True, False)
+        there(held[0], tb0, (0, 1), False, True)
+        c1 = times_ratio(z[1], l_pos3, ratio2, 0, T, "c1")
+        c2 = times_ratio(z[2], l_pos3, ratio2, 0, T, "c2")
+        bk0 = [again(tb0[k], 6 + k, f"st0{k}") for k in range(2)]
+        tb1 = [bank_tile(k, [P, 3, P]) for k in range(2)]
+        there(c1, tb1, (0, 1), True, False)
+        d1 = plain(z[1], l_pos4, 0, T, "d1")
+        there(d1, tb1, (0, 1), False, True)
+        s2 = plus(z[2], l_pos4, c2[:, H:T], H, H, "s2")
+        c3 = [times_ratio(z[3], l_pos3, ratio2, t0, n, f"c3{t0}") for t0, n in TAIL[:1]]
+        finish(s2[:], 2, H, H)
+        for k in range(2):
+            finish(bk0[k], 0, H * k, H)
+        tb2 = [bank_tile(2, [P, 3, P])]
+        there(c2, tb2, (0,), True, False)
+        bk1 = [again(tb1[k], 4 + k, f"st1{k}") for k in range(2)]
+        d2 = plain(z[2], l_pos4, 0, H, "d2")
+        there(d2, tb2, (0,), False, True)
+        bk2 = again(tb2[0], 3, "st2")
+        s3 = [plus(z[3], l_pos4, c3[0][:], *TAIL[0], "s30")]
+        c3.append(times_ratio(z[3], l_pos3, ratio2, *TAIL[1], "c31"))
+        finish(s3[0][:], 3, *TAIL[0])
+        for k in range(2):
+            finish(bk1[k], 1, H * k, H)
+        s3.append(plus(z[3], l_pos4, c3[1][:], *TAIL[1], "s31b"))
+        c3.append(times_ratio(z[3], l_pos3, ratio2, *TAIL[2], "c32"))
+        finish(bk2, 2, 0, H)
+        s3.append(plus(z[3], l_pos4, c3[2][:], *TAIL[2], "s32b"))
+        for k in (1, 2):
+            finish(s3[k][:], 3, *TAIL[k])

@@ -25,8 +25,10 @@ COPY = mybir.ActivationFunctionType.Copy
 TINY = 2.0**-60
 BANK = 2048
 G1 = (512, 512, 384, 128)
-EARLY1 = ((0, 0, 4), (1, 0, 4), (0, 4, 4), (1, 4, 4), (0, 8, 3), (0, 11, 1))
-EARLY2 = ((0, 0, 4), (1, 0, 4), (2, 0, 4), (0, 4, 3), (0, 10, 2), (0, 8, 2), (0, 7, 1))
+ORDER1 = ((0, 0, 4), (1, 0, 4), (0, 4, 4), (1, 4, 4), (0, 8, 3), (0, 11, 1), (1, 8, 4))
+ORDER1 = ORDER1 + tuple((b, e0, 4) for b in (2, 3) for e0 in (0, 4, 8))
+CHUNKS = ((0, 256), (256, 384), (896, 384), (1280, 256))
+SHARE = (640, 256)
 TAIL = ((0, 384), (384, 256), (640, 128))
 
 
@@ -42,6 +44,7 @@ def tile_moe_uni_silu_kernel(
         keep = ctx.enter_context(tc.tile_pool(name="keep", bufs=1))
         early = ctx.enter_context(tc.tile_pool(name="early", bufs=1))
         mid = ctx.enter_context(tc.tile_pool(name="mid", bufs=1))
+        ring = ctx.enter_context(tc.tile_pool(name="ring", bufs=1))
         psum = ctx.enter_context(tc.psum_pool(name="psum", bufs=1))
         made = []
 
@@ -110,9 +113,10 @@ def tile_moe_uni_silu_kernel(
         l_offs2 = load_list(offs2, "l_offs2")
         l_pos3 = load_list(pos3, "l_pos3")
         l_pos4 = load_list(pos4, "l_pos4")
-        q2_from = 0
-        q2 = keep.tile([P, T - q2_from], F32, name="q2")
-        nc.sync.dma_start(q2[:], gate2[1][:, q2_from:T])
+        q2 = keep.tile([P, T], F32, name="q2")
+        nc.sync.dma_start(q2[:], gate2[1])
+        q1 = keep.tile([P, T], F32, name="q1")
+        nc.sync.dma_start(q1[:], gate2[0])
 
         bank = bank_tile(0, [P, 3, P])
         for j in range(3):
@@ -130,43 +134,39 @@ def tile_moe_uni_silu_kernel(
         def factor(step, j):
             return cols[:, j % 3, step, 1, j // 3 : j // 3 + 1]
 
-        def experts(operands, name, first_banks, banks, between):
-            planes = [keep.tile([P, S], F32, name=f"{name}{b}") for b in range(4)]
-            done = [(b, e) for b, e0, ne in first_banks for e in range(e0, e0 + ne)]
-            order = list(first_banks) + [(b, e0, 4) for b in range(4) for e0 in range(0, E, 4) if (b, e0) not in done]
-            for i, (b, e0, ne) in enumerate(order):
-                acc = bank_tile(banks[i], [P, ne * C])
-                for j in range(ne):
-                    e = e0 + j
-                    words, scales = operands[e]
-                    nc.tensor.matmul_mx(
-                        out=acc[:, j * C : (j + 1) * C],
-                        lhsT=ww[e // 4][:, e % 4, 256 * b : 256 * (b + 1)].bitcast(FP4X4),
-                        lhsT_scale=ws[b // 2][:, e, P * (b % 2) : P * (b % 2 + 1)],
-                        rhs=words.bitcast(FP8X4),
-                        rhs_scale=scales,
-                        start=True,
-                        stop=True,
-                    )
-                nc.scalar.activation(planes[b][:, e0 * C : (e0 + ne) * C], acc[:], SILU)
-                between(i, planes)
-            return planes
+        def product(planes, operands, b, e0, ne, at):
+            acc = bank_tile(at, [P, ne * C])
+            for j in range(ne):
+                e = e0 + j
+                words, scales = operands[e]
+                nc.tensor.matmul_mx(
+                    out=acc[:, j * C : (j + 1) * C],
+                    lhsT=ww[e // 4][:, e % 4, 256 * b : 256 * (b + 1)].bitcast(FP4X4),
+                    lhsT_scale=ws[b // 2][:, e, P * (b % 2) : P * (b % 2 + 1)],
+                    rhs=words.bitcast(FP8X4),
+                    rhs_scale=scales,
+                    start=True,
+                    stop=True,
+                )
+            nc.scalar.activation(planes[b][:, e0 * C : (e0 + ne) * C], acc[:], SILU)
 
-        def gathered(name, n):
-            return keep.tile([P, n], F32, name=name)
+        def gathered(name, n, at):
+            if at is None:
+                return keep.tile([P, n], F32, name=name)
+            return ring.tile([P, n], F32, name=name, align_bytes=64, offset=at)
 
-        def times_ratio(y, lst, ratio, t0, n, name):
-            a = gathered(name, n)
+        def times_ratio(y, lst, ratio, t0, n, name, at=None):
+            a = gathered(name, n, at)
             nc.vector.tensor_tensor(a[:], y[:].indirect(part(lst, t0, n)), ratio[:, t0 : t0 + n], MULT)
             return a
 
-        def plus(y, lst, a, t0, n, name):
-            s = gathered(name, n)
+        def plus(y, lst, a, t0, n, name, at=None):
+            s = gathered(name, n, at)
             nc.vector.tensor_tensor(s[:], y[:].indirect(part(lst, t0, n)), a, ADD)
             return s
 
-        def plain(y, lst, t0, n, name):
-            b = gathered(name, n)
+        def plain(y, lst, t0, n, name, at=None):
+            b = gathered(name, n, at)
             nc.scalar.activation(b[:], y[:].indirect(part(lst, t0, n)), COPY)
             return b
 
@@ -189,12 +189,13 @@ def tile_moe_uni_silu_kernel(
             for j in range(0, n, C)
         ]
         ratio1 = spread(rcol, 0, 1)
-        ratio2 = spread(rcol, 1, 6)
-        y = experts(operands, "y", EARLY1, [(3 + i) % 8 for i in range(13)], lambda i, planes: None)
+        y = [keep.tile([P, S], F32, name=f"y{b}") for b in range(4)]
+        for i, (b, e0, ne) in enumerate(ORDER1):
+            product(y, operands, b, e0, ne, (3 + i) % 8)
 
-        ct = [keep.tile([P, 2, 256], BF16, name=f"ct{j}", align_bytes=64) for j in range(NB)]
-        cw = keep.tile([P, 2, T], F32, name="cw", align_bytes=64)
-        cp = keep.tile([P, 2, 2, T], BF16, name="cp", align_bytes=64)
+        ct = [ring.tile([P, 2, 256], BF16, name=f"ct{j}", align_bytes=64, offset=4608 + 1024 * j) for j in range(NB)]
+        cw = [keep.tile([P, T], F32, name=f"cw{u}", align_bytes=64) for u in range(2)]
+        cp = [keep.tile([P, 2, T], BF16, name=f"cp{u}", align_bytes=64) for u in range(2)]
         tok = [bank_tile(j, [P, 4, P]) for j in range(NB)]
 
         def turn1(src, b, t0, n, start=False, stop=False):
@@ -209,15 +210,16 @@ def tile_moe_uni_silu_kernel(
             else:
                 nc.scalar.activation(dst, src, COPY, scale=factor(0, j))
 
-        def back1(some, at):
-            back = bank_tile(at, [P, 2, len(some) * P])
-            for m, j in enumerate(some):
-                for u in range(2):
-                    nc.tensor.transpose(back[:, u, m * P : (m + 1) * P], ct[j][:].bitcast(F32)[:, u, :], ident[:])
-            return back, some[0] * P, len(some) * P
+        def back1(backs, t0, j):
+            for u in range(2):
+                m = j - t0 // P
+                nc.tensor.transpose(backs[u][:, m * P : (m + 1) * P], ct[j][:].bitcast(F32)[:, u, :], ident[:])
 
-        def words1(back, t0, n, eng):
-            (nc.vector.tensor_copy if eng == "v" else nc.scalar.copy)(cw[:, :, t0 : t0 + n], back[:])
+        def words1(backs, t0, n, u):
+            nc.vector.tensor_copy(cw[u][:, t0 : t0 + n], backs[u][:])
+
+        def part1(backs, t0, n, u):
+            nc.scalar.copy(cp[u][:, :, t0 : t0 + n], backs[u][:].bitcast(BF16).rearrange("p (t e) -> p e t", e=2))
 
         (t0, n0), (t1, n1), (t2, n2) = TAIL
         a0 = times_ratio(y[0], l_pos1, ratio1, 0, T, "a0")
@@ -226,142 +228,172 @@ def tile_moe_uni_silu_kernel(
         turn1(plus(y[0], l_pos2, a0[:, t0 : t0 + n0], t0, n0, "s00"), 0, t0, n0)
         for b in (1, 2, 3):
             if b > 1:
-                turn1(times_ratio(y[b], l_pos1, ratio1, t0, n0, f"a{b}0"), b, t0, n0)
-            turn1(plain(y[b], l_pos2, t0, n0, f"b{b}0"), b, t0, n0, stop=b == 3)
-        turn1(plus(y[0], l_pos2, a0[:, t1 : t1 + n1], t1, n1, "s01"), 0, t1, n1)
+                turn1(times_ratio(y[b], l_pos1, ratio1, t0, n0, f"a{b}0", 0 if b == 2 else None), b, t0, n0)
+            turn1(plain(y[b], l_pos2, t0, n0, f"b{b}0", 1536 * b if b < 3 else None), b, t0, n0, stop=b == 3)
+        turn1(plus(y[0], l_pos2, a0[:, t1 : t1 + n1], t1, n1, "s01", 0), 0, t1, n1)
         turn1(plain(y[1], l_pos2, t1, n1, "b11"), 1, t1, n1)
         a31 = times_ratio(y[3], l_pos1, ratio1, t1, n1, "a31")
         turn1(plain(y[2], l_pos2, t1, n1, "b21"), 2, t1, n1)
-        turn1(times_ratio(y[2], l_pos1, ratio1, t1, n1, "a21"), 2, t1, n1)
-        for j in (0, 1):
-            scale1(j, "s")
-        back01 = back1((0, 1), 6)
-        scale1(2, "s")
-        back2 = back1((2,), 7)
-        turn1(plus(y[3], l_pos2, a31[:], t1, n1, "s31"), 3, t1, n1, stop=True)
+        turn1(times_ratio(y[2], l_pos1, ratio1, t1, n1, "a21", 1536), 2, t1, n1)
         a32 = times_ratio(y[3], l_pos1, ratio1, t2, n2, "a32")
-        turn1(plus(y[0], l_pos2, a0[:, t2 : t2 + n2], t2, n2, "s02"), 0, t2, n2)
+        turn1(plus(y[0], l_pos2, a0[:, t2 : t2 + n2], t2, n2, "s02", 3072), 0, t2, n2)
+        turn1(times_ratio(y[2], l_pos1, ratio1, t2, n2, "a22", 3584), 2, t2, n2)
         for b in (1, 2):
             turn1(plain(y[b], l_pos2, t2, n2, f"b{b}2"), b, t2, n2)
-        turn1(times_ratio(y[2], l_pos1, ratio1, t2, n2, "a22"), 2, t2, n2)
-        turn1(plus(y[3], l_pos2, a32[:], t2, n2, "s32"), 3, t2, n2, stop=True)
-        words1(*back01, "v")
-        words1(*back2, "v")
-        for j in (3, 4):
-            scale1(j, "s")
+        backs0 = [bank_tile(6 + u, [P, n0]) for u in range(2)]
+        scale1(0, "s")
+        back1(backs0, t0, 0)
+        turn1(plus(y[3], l_pos2, a31[:], t1, n1, "s31", 4608), 3, t1, n1, stop=True)
+        scale1(1, "s")
+        back1(backs0, t0, 1)
+        turn1(plus(y[3], l_pos2, a32[:], t2, n2, "s32", 4608 + 1024), 3, t2, n2, stop=True)
+        scale1(2, "s")
+        back1(backs0, t0, 2)
+        backs1 = [bank_tile(u, [P, n1]) for u in range(2)]
         scale1(5, "v")
-        back34 = back1((3, 4), 0)
-        back5 = back1((5,), 1)
-        words1(*back34, "s")
-        words1(*back5, "v")
-        for back, t0, n in (back01, back2, back34, back5):
-            if t0 < TAIL[1][0]:
-                src = cw[:].bitcast(BF16)[:, :, 2 * t0 : 2 * (t0 + n)].rearrange("p u (t e) -> p u e t", e=2)
-                nc.gpsimd.tensor_copy(cp[:, :, :, t0 : t0 + n], src)
-            else:
-                nc.scalar.copy(cp[:, :, :, t0 : t0 + n], back[:].bitcast(BF16).rearrange("p u (t e) -> p u e t", e=2))
+        scale1(3, "s")
+        back1(backs1, t1, 3)
+        for u in range(2):
+            words1(backs0, t0, n0, u)
+            src = cw[u][:].bitcast(BF16)[:, 0 : 2 * n0].rearrange("p (t e) -> p e t", e=2)
+            nc.gpsimd.tensor_copy(cp[u][:, :, 0:n0], src)
+        backs2 = [bank_tile(2 + 3 * u, [P, n2]) for u in range(2)]
+        back1(backs2, t2, 5)
+        scale1(4, "s")
+        back1(backs1, t1, 4)
+        for u in range(2):
+            for piece in ((backs2, t2, n2), (backs1, t1, n1)):
+                words1(*piece, u)
+                part1(*piece, u)
 
         qw = keep.tile([P, S], U32, name="qw", align_bytes=64)
         qs = keep.tile([P, S], U8, name="qs", align_bytes=64)
-        woven = [
-            mid.tile([P, n, 2], U32, name=f"woven{i}", align_bytes=64, offset=2048 * i) for i, n in enumerate((512, 384))
-        ]
-        shares = ((1024, 256), (896, P))
-        singles = [keep.tile([P, n, 4], BF16, name=f"singles{s0}", align_bytes=64) for s0, n in shares]
+        woven = {}
 
-        def pairs(dst, u, s0, n):
-            nc.vector.tensor_copy(dst, cw[:, u, :].bitcast(U32).indirect(part(l_offs2, s0, n)))
+        def gather_pairs(k):
+            s0, n = CHUNKS[k]
+            pl = mid.tile([P, 2, n], U32, name=f"pl{k}", align_bytes=64, offset=3072 * (k % 2))
+            for u in range(2):
+                nc.vector.tensor_copy(pl[:, u, :], cw[u][:].bitcast(U32).indirect(part(l_offs2, s0, n)))
+            return pl
 
-        def single(t):
-            for dst, (s0, n) in zip(singles, shares):
-                nc.scalar.activation(dst[:, :, t], cp[:, t // 2, t % 2, :].indirect(part(l_offs2, s0, n)), COPY)
+        def weave(k, pl):
+            woven[k] = mid.tile([P, CHUNKS[k][1], 2], U32, name=f"woven{k}", align_bytes=64, offset=6144 if k else 8192)
+            nc.gpsimd.tensor_copy(woven[k][:], pl[:].rearrange("p u n -> p n u"))
 
-        def quantise(src, s0, n, words, w0):
-            nc.vector.quantize_mx(out=words[:, s0 - w0 : s0 - w0 + n].bitcast(FP8X4), scales=qs[:, s0 : s0 + n], in_=src)
+        def quantise(src, s0, n, words=None):
+            words = qw[:, s0 : s0 + n] if words is None else words
+            nc.vector.quantize_mx(out=words.bitcast(FP8X4), scales=qs[:, s0 : s0 + n], in_=src)
 
+        def quantise_woven(k):
+            quantise(woven[k][:].rearrange("p n u -> p (n u)").bitcast(BF16), *CHUNKS[k])
+
+        operands = [(qw[:, e * C : (e + 1) * C], qs[:, e * C : (e + 1) * C]) for e in range(E)]
+        z = [keep.tile([P, S], F32, name=f"z{b}") for b in range(4)]
+        turns = [3]
+
+        def product2(b, s0, n):
+            product(z, operands, b, s0 // C, n // C, turns[0] % 8)
+            turns[0] = turns[0] + 1
+
+        singles = mid.tile([P, SHARE[1], 4], BF16, name="singles", align_bytes=64, offset=10240)
         for t in range(4):
-            single(t)
-        pl = [keep.tile([P, 2, n], U32, name=f"pl{n}", align_bytes=64) for n in (512, 384)]
-        pairs(pl[0][:, 0, :], 0, 0, 512)
-        for j0 in (0, 256):
-            pairs(pl[0][:, 1, j0 : j0 + 256], 1, j0, 256)
-            nc.gpsimd.tensor_copy(woven[0][:, j0 : j0 + 256, :], pl[0][:, :, j0 : j0 + 256].rearrange("p u n -> p n u"))
+            nc.scalar.activation(singles[:, :, t], cp[t // 2][:, t % 2, :].indirect(part(l_offs2, *SHARE)), COPY)
+        weave(0, gather_pairs(0))
+        pl = gather_pairs(1)
+        quantise_woven(0)
+        weave(1, pl)
+        for b in range(4):
+            product2(b, *CHUNKS[0])
+        pl = gather_pairs(2)
+        qw2 = mid.tile([P, SHARE[1]], U32, name="qw2", align_bytes=64, offset=9216)
+        quantise(singles[:].rearrange("p n t -> p (n t)"), *SHARE, qw2[:])
+        for j in range(0, SHARE[1], C):
+            operands[(SHARE[0] + j) // C] = (qw2[:, j : j + C], qs[:, SHARE[0] + j : SHARE[0] + j + C])
+        quantise_woven(1)
+        weave(2, pl)
+        for b in range(4):
+            product2(b, *SHARE)
+        s0, n = CHUNKS[3]
+        woven[3] = mid.tile([P, n, 2], U32, name="woven3", align_bytes=64, offset=3072)
         for u in range(2):
-            pairs(pl[1][:, u, :], u, 512, 384)
-        quantise(woven[0][:].rearrange("p n u -> p (n u)").bitcast(BF16), 0, 512, qw, 0)
-        nc.gpsimd.tensor_copy(woven[1][:], pl[1][:].rearrange("p u n -> p n u"))
-        last = mid.tile([P, 256, 2], U32, name="last", align_bytes=64, offset=0)
-        for u in range(2):
-            pairs(last[:, :, u], u, 1280, 256)
-        for j0, n in ((0, 256), (256, P)):
-            quantise(woven[1][:, j0 : j0 + n, :].rearrange("p n u -> p (n u)").bitcast(BF16), 512 + j0, n, qw, 0)
-        quantise(last[:].rearrange("p n u -> p (n u)").bitcast(BF16), 1280, 256, qw, 0)
-        qw2 = mid.tile([P, 384], U32, name="qw2", align_bytes=64, offset=3072)
-        for src, (s0, n) in zip(singles, shares):
-            quantise(src[:].rearrange("p n t -> p (n t)"), s0, n, qw2, 896)
-        operands = [
-            (qw2[:, (e - 7) * C : (e - 6) * C] if 7 <= e < 10 else qw[:, e * C : (e + 1) * C], qs[:, e * C : (e + 1) * C])
-            for e in range(E)
-        ]
-        held = {}
-
-        def between(i, planes):
-            if i == 8:
-                held[0] = plain(planes[0], l_pos4, 0, T, "d0")
-
-        z = experts(operands, "z", EARLY2, (2, 3, 4, 5, 6, 7, 0, 1, 2, 3, 0, 1, 2, 3), between)
+            nc.vector.tensor_copy(woven[3][:, :, u], cw[u][:].bitcast(U32).indirect(part(l_offs2, s0, n)))
+        quantise_woven(2)
+        quantise_woven(3)
+        for b in range(3):
+            product2(b, *CHUNKS[1])
+        for k in (2, 3):
+            product2(0, *CHUNKS[k])
+        for k in (2, 3):
+            product2(1, *CHUNKS[k])
+        d0 = plain(z[0], l_pos4, 0, T, "d0", 3072)
+        product2(2, *CHUNKS[2])
 
         H = T // 2
+        halves = ((0, H), (H, H))
 
-        def there(src, banks, halves, start, stop):
-            for k in halves:
-                for m in range(3):
-                    j = 3 * k + m
-                    turn(banks[k][:, m, :], src[:, j * P : (j + 1) * P], start and m == 0, stop and m == 2)
+        def there(src, at, t0, n):
+            bank = bank_tile(at % 8, [P, n])
+            for m in range(n // P):
+                nc.tensor.transpose(bank[:, m * P : (m + 1) * P], src[:, t0 + m * P : t0 + (m + 1) * P], ident[:])
+            return bank
 
-        def again(bank, at, name):
-            st = keep.tile([P, 3, P], F32, name=name)
-            nc.scalar.copy(st[:], bank[:])
-            back = bank_tile(at, [P, 3, P])
-            for m in range(3):
-                nc.tensor.transpose(back[:, m, :], st[:, m, :], ident[:])
-            return back[:].rearrange("p j t -> p (j t)")
+        def again(bank, at, t0, n, name, place=None):
+            st = gathered(name, n, place)
+            back = bank_tile(at % 8, [P, n])
+            for m in range(n // P):
+                cut = slice(m * P, (m + 1) * P)
+                nc.scalar.activation(st[:, cut], bank[:, cut], COPY, scale=factor(1, t0 // P + m))
+            for m in range(n // P):
+                cut = slice(m * P, (m + 1) * P)
+                nc.tensor.transpose(back[:, cut], st[:, cut], ident[:])
+            return back
 
-        def finish(src, b, t0, n):
+        def finish(back, first, b, t0, n, origin=0):
             res = keep.tile([P, n], F32, name=f"res{b}_{t0}")
-            nc.vector.scalar_tensor_tensor(res[:], q2[:, t0 : t0 + n], TINY, src, ADD, MULT)
+            nc.vector.tensor_tensor(res[:], back[:], first[:, t0 - origin : t0 - origin + n], ADD)
             nc.sync.dma_start(out[b * P : (b + 1) * P, t0 : t0 + n], res[:])
 
-        c0 = times_ratio(z[0], l_pos3, ratio2, 0, T, "c0")
-        tb0 = [bank_tile(4 + k, [P, 3, P]) for k in range(2)]
-        there(c0, tb0, (0, 1), True, False)
-        there(held[0], tb0, (0, 1), False, True)
-        c1 = times_ratio(z[1], l_pos3, ratio2, 0, T, "c1")
-        c2 = times_ratio(z[2], l_pos3, ratio2, 0, T, "c2")
-        bk0 = [again(tb0[k], 6 + k, f"st0{k}") for k in range(2)]
-        tb1 = [bank_tile(k, [P, 3, P]) for k in range(2)]
-        there(c1, tb1, (0, 1), True, False)
-        d1 = plain(z[1], l_pos4, 0, T, "d1")
-        there(d1, tb1, (0, 1), False, True)
-        s2 = plus(z[2], l_pos4, c2[:, H:T], H, H, "s2")
-        c3 = [times_ratio(z[3], l_pos3, ratio2, t0, n, f"c3{t0}") for t0, n in TAIL[:1]]
-        finish(s2[:], 2, H, H)
+        def added(k, place):
+            t0, n = halves[k]
+            e = times_ratio(z[1], l_pos4, q2, t0, n, f"e1{k}", place)
+            res = keep.tile([P, n], F32, name=f"res1{k}")
+            nc.gpsimd.tensor_tensor(res[:], c1[:, t0 : t0 + n], e[:], ADD)
+            return lambda: nc.sync.dma_start(out[P : 2 * P, t0 : t0 + n], res[:])
+
+        at = turns[0]
+        c0 = times_ratio(z[0], l_pos3, q1, 0, T, "c0")
+        tb0 = [there(d0, at + k, *halves[k]) for k in range(2)]
+        c1 = times_ratio(z[1], l_pos3, q1, 0, T, "c1")
+        product(z, operands, 2, CHUNKS[3][0] // C, CHUNKS[3][1] // C, (at + 4) % 8)
+        product(z, operands, 3, CHUNKS[1][0] // C, CHUNKS[1][1] // C, (at + 7) % 8)
+        c2 = times_ratio(z[2], l_pos3, q1, 0, T, "c2")
+        bk0 = [again(tb0[k], at + 2 + k, *halves[k], f"st0{k}", 1536 * k) for k in range(2)]
+        store = added(0, 0)
         for k in range(2):
-            finish(bk0[k], 0, H * k, H)
-        tb2 = [bank_tile(2, [P, 3, P])]
-        there(c2, tb2, (0,), True, False)
-        bk1 = [again(tb1[k], 4 + k, f"st1{k}") for k in range(2)]
-        d2 = plain(z[2], l_pos4, 0, H, "d2")
-        there(d2, tb2, (0,), False, True)
-        bk2 = again(tb2[0], 3, "st2")
-        s3 = [plus(z[3], l_pos4, c3[0][:], *TAIL[0], "s30")]
-        c3.append(times_ratio(z[3], l_pos3, ratio2, *TAIL[1], "c31"))
-        finish(s3[0][:], 3, *TAIL[0])
+            finish(bk0[k], c0, 0, *halves[k])
+        store()
+        d2 = plain(z[2], l_pos4, 0, T, "d2", 3072)
+        tb2 = [there(d2, at + 5 + k, *halves[k]) for k in range(2)]
+        for k in (2, 3):
+            product(z, operands, 3, CHUNKS[k][0] // C, CHUNKS[k][1] // C, (at + k - 2) % 8)
+        bk2 = [again(tb2[k], at + 2 + k, *halves[k], f"st2{k}", 6144 + 1536 * k) for k in range(2)]
+        c3 = [times_ratio(z[3], l_pos3, q1, *halves[0], "c30")]
+        store = added(1, 3072)
         for k in range(2):
-            finish(bk1[k], 1, H * k, H)
-        s3.append(plus(z[3], l_pos4, c3[1][:], *TAIL[1], "s31b"))
-        c3.append(times_ratio(z[3], l_pos3, ratio2, *TAIL[2], "c32"))
-        finish(bk2, 2, 0, H)
-        s3.append(plus(z[3], l_pos4, c3[2][:], *TAIL[2], "s32b"))
-        for k in (1, 2):
-            finish(s3[k][:], 3, *TAIL[k])
+            finish(bk2[k], c2, 2, *halves[k])
+        store()
+        c3.append(times_ratio(z[3], l_pos3, q1, *halves[1], "c31", 7680))
+
+        def second3(k):
+            t0, n = TAIL[k]
+            d3 = plain(z[3], l_pos4, t0, n, f"d3{k}", (4608, 6144, 7168)[k])
+            return there(d3, at + (4, 7, 0)[k], 0, n)
+
+        tb3 = [second3(0), second3(1)]
+        bk3 = [again(tb3[0], at + 1, *TAIL[0], "st30")]
+        tb3.append(second3(2))
+        bk3 = bk3 + [again(tb3[k], at + 4 + k, *TAIL[k], f"st3{k}") for k in (1, 2)]
+        for k in range(3):
+            t0, n = TAIL[k]
+            finish(bk3[k], c3[t0 // H], 3, t0, n, H * (t0 // H))

@@ -25,8 +25,8 @@ COPY = mybir.ActivationFunctionType.Copy
 TINY = 2.0**-60
 BANK = 2048
 G1 = (512, 512, 384, 128)
-ORDER1 = ((0, 0, 4), (1, 0, 4), (0, 4, 4), (1, 4, 4), (0, 8, 3), (0, 11, 1), (1, 8, 4))
-ORDER1 = ORDER1 + tuple((b, e0, 4) for b in (2, 3) for e0 in (0, 4, 8))
+ORDER1 = ((0, 0, 4), (1, 0, 4), (0, 4, 4), (1, 4, 4), (2, 0, 4), (3, 0, 4), (0, 8, 3), (0, 11, 1))
+ORDER1 = ORDER1 + ((1, 8, 4), (2, 4, 4), (2, 8, 4), (3, 4, 4), (3, 8, 4))
 CHUNKS = ((0, 256), (256, 384), (896, 384), (1280, 256))
 SHARE = (640, 256)
 TAIL = ((0, 384), (384, 256), (640, 128))
@@ -66,7 +66,7 @@ def tile_moe_uni_silu_kernel(
                 bank = bank_tile(at + h, [P, 384])
                 for j in range(3):
                     nc.tensor.transpose(
-                        bank[:, j * P : (j + 1) * P], rcol[:, j, step, h : h + 1].to_broadcast([P, P]), ident[:]
+                        bank[:, j * P : (j + 1) * P], rcol[:, j, h : h + 1].to_broadcast([P, P]), ident[:]
                     )
                 nc.scalar.copy(ratio[:, 384 * h : 384 * (h + 1)], bank[:])
             return ratio
@@ -86,28 +86,28 @@ def tile_moe_uni_silu_kernel(
         l_offs = load_list(offs, "l_offs")
         for r in range(4):
             (nc.sync if r < 2 else nc.scalar).dma_start(xs[r:P:32, :].bitcast(I32), x_scales[0, r:16:4, :].bitcast(I32))
-        for step, gate in enumerate((gate1, gate2)):
+
+        def load_rows(gate, first):
             flat = gate.rearrange("r p (h t) -> (r p h) t", h=2)
-            nc.sync.dma_start(rows[4 * step : 4 * step + 4, :], flat[2 * P - 2 : 2 * P + 2, :])
+            nc.sync.dma_start(rows[first:4, :], flat[2 * P - 2 + first : 2 * P + 2, :])
+
+        load_rows(gate1, 0)
         xw = keep.tile([P, T], I32, name="xw", align_bytes=64)
         nc.sync.dma_start(xw[:], x_words[0].rearrange("p t d -> p (t d)").bitcast(I32))
 
-        def load_scales(h):
+        def load_words(e0, ne):
+            t = keep.tile([P, ne, 2 * K], U8, name=f"ww{e0}", align_bytes=64)
+            nc.sync.dma_start(t[:].bitcast(I32), w_words[e0 : e0 + ne, 0].rearrange("e p n -> p e n").bitcast(I32))
+            return [t[:, j, :] for j in range(ne)]
+
+        ww = load_words(0, 8)
+        for h in range(2):
             for r in range(4):
                 nc.sync.dma_start(
                     ws[h][r:P:32, :, :].bitcast(I32),
                     w_scales[:, 0, r:16:4, 256 * h : 256 * (h + 1)].rearrange("e q n -> q e n").bitcast(I32),
                 )
-
-        load_scales(0)
-        ww = []
-        for g in range(3):
-            t = keep.tile([P, 4, 2 * K], U8, name=f"ww{g}", align_bytes=64)
-            nc.sync.dma_start(
-                t[:].bitcast(I32), w_words[4 * g : 4 * g + 4, 0].rearrange("e p n -> p e n").bitcast(I32)
-            )
-            ww.append(t)
-        load_scales(1)
+        ww = ww + load_words(8, 4)
         l_pos1 = load_list(pos1, "l_pos1")
         l_pos2 = load_list(pos2, "l_pos2")
         l_offs2 = load_list(offs2, "l_offs2")
@@ -118,21 +118,27 @@ def tile_moe_uni_silu_kernel(
         q1 = keep.tile([P, T], F32, name="q1")
         nc.sync.dma_start(q1[:], gate2[0])
 
-        bank = bank_tile(0, [P, 3, P])
-        for j in range(3):
-            nc.tensor.transpose(bank[:, j, :], rows[:, j * P : (j + 1) * P], ident[:])
+        def gate_columns(at):
+            bank = bank_tile(at, [P, 3, P])
+            for j in range(3):
+                nc.tensor.transpose(bank[:, j, :], rows[:, j * P : (j + 1) * P], ident[:])
+            return bank[:, :, 0:4].rearrange("p j (r h) -> p j r h", r=2)
+
+        turned = gate_columns(0)
         later = early.tile([P, (5 * S - 1024) // 4], F32, name="later", align_bytes=64, offset=1024)
-        den = later[:, 0 : 2 * NB].rearrange("p (j s h) -> p j s h", j=3, s=2)
-        nc.scalar.activation(den, bank[:, :, 0:8].rearrange("p j (s r h) -> p j s r h", s=2, r=2)[:, :, :, 1, :], COPY, bias=TINY)
-        cols = keep.tile([P, 3, 2, 2, 2], F32, name="cols")
-        nc.scalar.activation(cols[:].rearrange("p j s r h -> p j (s r h)"), bank[:, :, 0:8], COPY, bias=TINY)
-        rec = keep.tile([P, 3, 2, 2], F32, name="rec")
-        nc.vector.reciprocal(rec[:].rearrange("p j s h -> p (j s h)"), later[:, 0 : 2 * NB])
-        rcol = keep.tile([P, 3, 2, 2], F32, name="rcol")
-        nc.gpsimd.tensor_tensor(rcol[:], cols[:, :, :, 0, :], rec[:], MULT)
+        den = later[:, 0:NB].rearrange("p (j h) -> p j h", j=3)
+        nc.scalar.activation(den, turned[:, :, 1, :], COPY, bias=TINY)
+        cols = keep.tile([P, 3, 2, 2], F32, name="cols")
+        cols2 = keep.tile([P, 3, 2], F32, name="cols2")
+        nc.scalar.activation(cols[:], turned, COPY, bias=TINY)
+        rec = keep.tile([P, 3, 2], F32, name="rec")
+        nc.vector.reciprocal(rec[:].rearrange("p j h -> p (j h)"), later[:, 0:NB])
+        rcol = keep.tile([P, 3, 2], F32, name="rcol")
+        nc.gpsimd.tensor_tensor(rcol[:], cols[:, :, 0, :], rec[:], MULT)
+        load_rows(gate2, 2)
 
         def factor(step, j):
-            return cols[:, j % 3, step, 1, j // 3 : j // 3 + 1]
+            return (cols2[:] if step else cols[:, :, 1, :])[:, j % 3, j // 3 : j // 3 + 1]
 
         def product(planes, operands, b, e0, ne, at):
             acc = bank_tile(at, [P, ne * C])
@@ -141,7 +147,7 @@ def tile_moe_uni_silu_kernel(
                 words, scales = operands[e]
                 nc.tensor.matmul_mx(
                     out=acc[:, j * C : (j + 1) * C],
-                    lhsT=ww[e // 4][:, e % 4, 256 * b : 256 * (b + 1)].bitcast(FP4X4),
+                    lhsT=ww[e][:, 256 * b : 256 * (b + 1)].bitcast(FP4X4),
                     lhsT_scale=ws[b // 2][:, e, P * (b % 2) : P * (b % 2 + 1)],
                     rhs=words.bitcast(FP8X4),
                     rhs_scale=scales,
@@ -191,7 +197,7 @@ def tile_moe_uni_silu_kernel(
         ratio1 = spread(rcol, 0, 1)
         y = [keep.tile([P, S], F32, name=f"y{b}") for b in range(4)]
         for i, (b, e0, ne) in enumerate(ORDER1):
-            product(y, operands, b, e0, ne, (3 + i) % 8)
+            product(y, operands, b, e0, ne, (3, 4, 5, 0, 1, 2, 6, 7, 3, 6, 4, 7, 5)[i])
 
         ct = [ring.tile([P, 2, 256], BF16, name=f"ct{j}", align_bytes=64, offset=4608 + 1024 * j) for j in range(NB)]
         cw = [keep.tile([P, T], F32, name=f"cw{u}", align_bytes=64) for u in range(2)]
@@ -222,31 +228,29 @@ def tile_moe_uni_silu_kernel(
             nc.scalar.copy(cp[u][:, :, t0 : t0 + n], backs[u][:].bitcast(BF16).rearrange("p (t e) -> p e t", e=2))
 
         (t0, n0), (t1, n1), (t2, n2) = TAIL
-        a0 = times_ratio(y[0], l_pos1, ratio1, 0, T, "a0")
-        a1 = times_ratio(y[1], l_pos1, ratio1, 0, T, "a1")
-        turn1(a1, 1, 0, T, start=True)
-        turn1(plus(y[0], l_pos2, a0[:, t0 : t0 + n0], t0, n0, "s00"), 0, t0, n0)
-        for b in (1, 2, 3):
-            if b > 1:
-                turn1(times_ratio(y[b], l_pos1, ratio1, t0, n0, f"a{b}0", 0 if b == 2 else None), b, t0, n0)
-            turn1(plain(y[b], l_pos2, t0, n0, f"b{b}0", 1536 * b if b < 3 else None), b, t0, n0, stop=b == 3)
-        turn1(plus(y[0], l_pos2, a0[:, t1 : t1 + n1], t1, n1, "s01", 0), 0, t1, n1)
-        turn1(plain(y[1], l_pos2, t1, n1, "b11"), 1, t1, n1)
-        a31 = times_ratio(y[3], l_pos1, ratio1, t1, n1, "a31")
-        turn1(plain(y[2], l_pos2, t1, n1, "b21"), 2, t1, n1)
-        turn1(times_ratio(y[2], l_pos1, ratio1, t1, n1, "a21", 1536), 2, t1, n1)
-        a32 = times_ratio(y[3], l_pos1, ratio1, t2, n2, "a32")
-        turn1(plus(y[0], l_pos2, a0[:, t2 : t2 + n2], t2, n2, "s02", 3072), 0, t2, n2)
-        turn1(times_ratio(y[2], l_pos1, ratio1, t2, n2, "a22", 3584), 2, t2, n2)
-        for b in (1, 2):
-            turn1(plain(y[b], l_pos2, t2, n2, f"b{b}2"), b, t2, n2)
+        rest = (t1, n1 + n2)
+        a = [times_ratio(y[b], l_pos1, ratio1, 0, T, f"a{b}") for b in range(2)]
+        turn1(a[0], 0, 0, T, start=True)
+        turn1(a[1], 1, 0, T)
+        turn1(plain(y[0], l_pos2, 0, T, "b0"), 0, 0, T)
+        a2 = times_ratio(y[2], l_pos1, ratio1, 0, T, "a2")
+        b1 = plain(y[1], l_pos2, 0, T, "b1")
+        turn1(a2[:, 0:n0], 2, t0, n0)
+        turn1(b1[:, 0:n0], 1, t0, n0)
+        a30 = times_ratio(y[3], l_pos1, ratio1, t0, n0, "a30")
+        turn1(plain(y[2], l_pos2, t0, n0, "b20"), 2, t0, n0)
+        turn1(plus(y[3], l_pos2, a30[:], t0, n0, "s30"), 3, t0, n0, stop=True)
+        turn1(a2[:, n0:T], 2, *rest)
+        turn1(b1[:, n0:T], 1, *rest)
+        a31 = times_ratio(y[3], l_pos1, ratio1, *rest, "a31")
+        turn1(plain(y[2], l_pos2, *rest, "b21"), 2, *rest)
         backs0 = [bank_tile(6 + u, [P, n0]) for u in range(2)]
         scale1(0, "s")
         back1(backs0, t0, 0)
-        turn1(plus(y[3], l_pos2, a31[:], t1, n1, "s31", 4608), 3, t1, n1, stop=True)
+        turn1(plus(y[3], l_pos2, a31[:, 0:n1], t1, n1, "s31"), 3, t1, n1, stop=True)
         scale1(1, "s")
         back1(backs0, t0, 1)
-        turn1(plus(y[3], l_pos2, a32[:], t2, n2, "s32", 4608 + 1024), 3, t2, n2, stop=True)
+        turn1(plus(y[3], l_pos2, a31[:, n1 : n1 + n2], t2, n2, "s32", 4608), 3, t2, n2, stop=True)
         scale1(2, "s")
         back1(backs0, t0, 2)
         backs1 = [bank_tile(u, [P, n1]) for u in range(2)]
@@ -299,6 +303,7 @@ def tile_moe_uni_silu_kernel(
         singles = mid.tile([P, SHARE[1], 4], BF16, name="singles", align_bytes=64, offset=10240)
         for t in range(4):
             nc.scalar.activation(singles[:, :, t], cp[t // 2][:, t % 2, :].indirect(part(l_offs2, *SHARE)), COPY)
+        nc.scalar.copy(cols2[:], gate_columns(5)[:, :, 1, :])
         weave(0, gather_pairs(0))
         pl = gather_pairs(1)
         quantise_woven(0)

@@ -25,8 +25,8 @@ COPY = mybir.ActivationFunctionType.Copy
 TINY = 2.0**-60
 BANK = 2048
 G1 = (512, 512, 384, 128)
-ORDER1 = ((0, 0, 4), (1, 0, 4), (0, 4, 4), (1, 4, 4), (2, 0, 4), (3, 0, 4), (0, 8, 3), (0, 11, 1))
-ORDER1 = ORDER1 + ((1, 8, 4), (2, 4, 4), (2, 8, 4), (3, 4, 4), (3, 8, 4))
+ORDER1 = ((0, 0, 4), (1, 0, 4), (0, 4, 4), (1, 4, 4), (2, 0, 4), (0, 8, 3), (0, 11, 1))
+ORDER1 = ORDER1 + ((1, 8, 4), (2, 4, 4), (2, 8, 4), (3, 0, 4), (3, 4, 4), (3, 8, 4))
 CHUNKS = ((0, 256), (256, 384), (896, 384), (1280, 256))
 SHARE = (640, 256)
 TAIL = ((0, 384), (384, 256), (640, 128))
@@ -125,7 +125,7 @@ def tile_moe_uni_silu_kernel(
             return bank[:, :, 0:4].rearrange("p j (r h) -> p j r h", r=2)
 
         turned = gate_columns(0)
-        later = early.tile([P, (5 * S - 1024) // 4], F32, name="later", align_bytes=64, offset=1024)
+        later = early.tile([P, (5 * S - 512) // 4], F32, name="later", align_bytes=64, offset=512)
         den = later[:, 0:NB].rearrange("p (j h) -> p j h", j=3)
         nc.scalar.activation(den, turned[:, :, 1, :], COPY, bias=TINY)
         cols = keep.tile([P, 3, 2, 2], F32, name="cols")
@@ -184,7 +184,7 @@ def tile_moe_uni_silu_kernel(
             early.tile([P, n], U32, name=f"gw{i}", align_bytes=64, offset=S + 4 * s0)
             for i, (s0, n) in enumerate(zip(starts(G1), G1))
         ]
-        for kind, i in (("s", 0), ("s", 1), ("w", 0), ("w", 1), ("s", 2), ("w", 2), ("w", 3)):
+        for kind, i in (("s", 0), ("w", 0), ("s", 1), ("w", 1), ("s", 2), ("w", 2), ("w", 3)):
             if kind == "s":
                 nc.vector.tensor_copy(gs[i][:], xs[:].indirect(part(l_offs, 512 * i, 512)))
             else:
@@ -197,7 +197,7 @@ def tile_moe_uni_silu_kernel(
         ratio1 = spread(rcol, 0, 1)
         y = [keep.tile([P, S], F32, name=f"y{b}") for b in range(4)]
         for i, (b, e0, ne) in enumerate(ORDER1):
-            product(y, operands, b, e0, ne, (3, 4, 5, 0, 1, 2, 6, 7, 3, 6, 4, 7, 5)[i])
+            product(y, operands, b, e0, ne, (3, 4, 5, 0, 1, 6, 7, 2, 6, 3, 7, 2, 4)[i])
 
         ct = [ring.tile([P, 2, 256], BF16, name=f"ct{j}", align_bytes=64, offset=4608 + 1024 * j) for j in range(NB)]
         cw = [keep.tile([P, T], F32, name=f"cw{u}", align_bytes=64) for u in range(2)]
@@ -235,38 +235,36 @@ def tile_moe_uni_silu_kernel(
         turn1(plain(y[0], l_pos2, 0, T, "b0"), 0, 0, T)
         a2 = times_ratio(y[2], l_pos1, ratio1, 0, T, "a2")
         b1 = plain(y[1], l_pos2, 0, T, "b1")
-        turn1(a2[:, 0:n0], 2, t0, n0)
+        turn1(plus(y[2], l_pos2, a2[:, 0:n0], t0, n0, "s20"), 2, t0, n0)
         turn1(b1[:, 0:n0], 1, t0, n0)
-        a30 = times_ratio(y[3], l_pos1, ratio1, t0, n0, "a30")
-        turn1(plain(y[2], l_pos2, t0, n0, "b20"), 2, t0, n0)
-        turn1(plus(y[3], l_pos2, a30[:], t0, n0, "s30"), 3, t0, n0, stop=True)
-        turn1(a2[:, n0:T], 2, *rest)
+        turn1(times_ratio(y[3], l_pos1, ratio1, t0, n0, "a30"), 3, t0, n0)
+        turn1(plain(y[3], l_pos2, t0, n0, "b30", 0), 3, t0, n0, stop=True)
         turn1(b1[:, n0:T], 1, *rest)
-        a31 = times_ratio(y[3], l_pos1, ratio1, *rest, "a31")
-        turn1(plain(y[2], l_pos2, *rest, "b21"), 2, *rest)
+        turn1(times_ratio(y[3], l_pos1, ratio1, *rest, "a31"), 3, *rest)
+        turn1(plain(y[3], l_pos2, *rest, "b31"), 3, *rest)
         backs0 = [bank_tile(6 + u, [P, n0]) for u in range(2)]
         scale1(0, "s")
         back1(backs0, t0, 0)
-        turn1(plus(y[3], l_pos2, a31[:, 0:n1], t1, n1, "s31"), 3, t1, n1, stop=True)
+        turn1(plus(y[2], l_pos2, a2[:, t1 : t1 + n1], t1, n1, "s21", 0), 2, t1, n1, stop=True)
         scale1(1, "s")
         back1(backs0, t0, 1)
-        turn1(plus(y[3], l_pos2, a31[:, n1 : n1 + n2], t2, n2, "s32", 4608), 3, t2, n2, stop=True)
+        turn1(plus(y[2], l_pos2, a2[:, t2:T], t2, n2, "s22", 1024), 2, t2, n2, stop=True)
         scale1(2, "s")
         back1(backs0, t0, 2)
         backs1 = [bank_tile(u, [P, n1]) for u in range(2)]
-        scale1(5, "v")
-        scale1(3, "s")
+        scale1(3, "v")
+        scale1(4, "s")
         back1(backs1, t1, 3)
-        for u in range(2):
-            words1(backs0, t0, n0, u)
-            src = cw[u][:].bitcast(BF16)[:, 0 : 2 * n0].rearrange("p (t e) -> p e t", e=2)
-            nc.gpsimd.tensor_copy(cp[u][:, :, 0:n0], src)
+        back1(backs1, t1, 4)
+        scale1(5, "v")
         backs2 = [bank_tile(2 + 3 * u, [P, n2]) for u in range(2)]
         back1(backs2, t2, 5)
-        scale1(4, "s")
-        back1(backs1, t1, 4)
         for u in range(2):
-            for piece in ((backs2, t2, n2), (backs1, t1, n1)):
+            nc.scalar.copy(cw[u][:, t0 : t0 + n0], backs0[u][:])
+            src = cw[u][:].bitcast(BF16)[:, 0 : 2 * n0].rearrange("p (t e) -> p e t", e=2)
+            nc.gpsimd.tensor_copy(cp[u][:, :, 0:n0], src)
+        for u in range(2):
+            for piece in ((backs1, t1, n1), (backs2, t2, n2)):
                 words1(*piece, u)
                 part1(*piece, u)
 

@@ -25,8 +25,8 @@ COPY = mybir.ActivationFunctionType.Copy
 TINY = 2.0**-60
 BANK = 2048
 G1 = (512, 512, 384, 128)
-ORDER1 = ((0, 0, 4), (1, 0, 4), (0, 4, 4), (1, 4, 4), (2, 0, 4), (0, 8, 3), (0, 11, 1))
-ORDER1 = ORDER1 + ((1, 8, 4), (2, 4, 4), (2, 8, 4), (3, 0, 4), (3, 4, 4), (3, 8, 4))
+ORDER1 = tuple((b, 0, 4) for b in range(4)) + tuple((b, 4, 4) for b in range(2))
+ORDER1 = ORDER1 + ((0, 8, 3), (0, 11, 1), (1, 8, 4), (2, 4, 4), (2, 8, 4), (3, 4, 4), (3, 8, 4))
 CHUNKS = ((0, 256), (256, 384), (896, 384), (1280, 256))
 SHARE = (640, 256)
 TAIL = ((0, 384), (384, 256), (640, 128))
@@ -72,10 +72,9 @@ def tile_moe_uni_silu_kernel(
             return ratio
 
         xs = keep.tile([P, T], U8, name="xs", align_bytes=64)
-        ws = [keep.tile([P, E, K // 2], U8, name=f"ws{h}", align_bytes=64) for h in range(2)]
+        ws = keep.tile([P, E, K], U8, name="ws", align_bytes=64)
         nc.gpsimd.memset(xs[:].bitcast(I32), 0)
-        for h in range(2):
-            nc.vector.memset(ws[h][:].rearrange("p e n -> p (e n)").bitcast(I32), 0)
+        nc.vector.memset(ws[:].rearrange("p e n -> p (e n)").bitcast(I32), 0)
         rows = keep.tile([P, T // 2], F32, name="rows")
         nc.gpsimd.memset(rows[:], 0.0)
         ident = keep.tile([P, P], F32, name="ident")
@@ -100,14 +99,12 @@ def tile_moe_uni_silu_kernel(
             nc.sync.dma_start(t[:].bitcast(I32), w_words[e0 : e0 + ne, 0].rearrange("e p n -> p e n").bitcast(I32))
             return [t[:, j, :] for j in range(ne)]
 
-        ww = load_words(0, 8)
-        for h in range(2):
-            for r in range(4):
-                nc.sync.dma_start(
-                    ws[h][r:P:32, :, :].bitcast(I32),
-                    w_scales[:, 0, r:16:4, 256 * h : 256 * (h + 1)].rearrange("e q n -> q e n").bitcast(I32),
-                )
-        ww = ww + load_words(8, 4)
+        ww = load_words(0, 4)
+        for r in range(4):
+            nc.sync.dma_start(
+                ws[r:P:32, :, :].bitcast(I32), w_scales[:, 0, r:16:4, :].rearrange("e q n -> q e n").bitcast(I32)
+            )
+        ww = ww + load_words(4, 4) + load_words(8, 4)
         l_pos1 = load_list(pos1, "l_pos1")
         l_pos2 = load_list(pos2, "l_pos2")
         l_offs2 = load_list(offs2, "l_offs2")
@@ -148,7 +145,7 @@ def tile_moe_uni_silu_kernel(
                 nc.tensor.matmul_mx(
                     out=acc[:, j * C : (j + 1) * C],
                     lhsT=ww[e][:, 256 * b : 256 * (b + 1)].bitcast(FP4X4),
-                    lhsT_scale=ws[b // 2][:, e, P * (b % 2) : P * (b % 2 + 1)],
+                    lhsT_scale=ws[:, e, P * b : P * (b + 1)],
                     rhs=words.bitcast(FP8X4),
                     rhs_scale=scales,
                     start=True,
@@ -197,7 +194,7 @@ def tile_moe_uni_silu_kernel(
         ratio1 = spread(rcol, 0, 1)
         y = [keep.tile([P, S], F32, name=f"y{b}") for b in range(4)]
         for i, (b, e0, ne) in enumerate(ORDER1):
-            product(y, operands, b, e0, ne, (3, 4, 5, 0, 1, 6, 7, 2, 6, 3, 7, 2, 4)[i])
+            product(y, operands, b, e0, ne, (3, 4, 5, 0, 1, 2, 6, 7, 3, 6, 4, 7, 5)[i])
 
         ct = [ring.tile([P, 2, 256], BF16, name=f"ct{j}", align_bytes=64, offset=4608 + 1024 * j) for j in range(NB)]
         cw = [keep.tile([P, T], F32, name=f"cw{u}", align_bytes=64) for u in range(2)]
@@ -323,13 +320,14 @@ def tile_moe_uni_silu_kernel(
             nc.vector.tensor_copy(woven[3][:, :, u], cw[u][:].bitcast(U32).indirect(part(l_offs2, s0, n)))
         quantise_woven(2)
         quantise_woven(3)
-        for b in range(3):
+        for b in range(2):
             product2(b, *CHUNKS[1])
         for k in (2, 3):
             product2(0, *CHUNKS[k])
         for k in (2, 3):
             product2(1, *CHUNKS[k])
         d0 = plain(z[0], l_pos4, 0, T, "d0", 3072)
+        product(z, operands, 2, CHUNKS[1][0] // C, CHUNKS[1][1] // C, (turns[0] - 3) % 8)
         product2(2, *CHUNKS[2])
 
         H = T // 2
@@ -369,7 +367,6 @@ def tile_moe_uni_silu_kernel(
         tb0 = [there(d0, at + k, *halves[k]) for k in range(2)]
         c1 = times_ratio(z[1], l_pos3, q1, 0, T, "c1")
         product(z, operands, 2, CHUNKS[3][0] // C, CHUNKS[3][1] // C, (at + 4) % 8)
-        product(z, operands, 3, CHUNKS[1][0] // C, CHUNKS[1][1] // C, (at + 7) % 8)
         c2 = times_ratio(z[2], l_pos3, q1, 0, T, "c2")
         bk0 = [again(tb0[k], at + 2 + k, *halves[k], f"st0{k}", 1536 * k) for k in range(2)]
         store = added(0, 0)
@@ -378,8 +375,8 @@ def tile_moe_uni_silu_kernel(
         store()
         d2 = plain(z[2], l_pos4, 0, T, "d2", 3072)
         tb2 = [there(d2, at + 5 + k, *halves[k]) for k in range(2)]
-        for k in (2, 3):
-            product(z, operands, 3, CHUNKS[k][0] // C, CHUNKS[k][1] // C, (at + k - 2) % 8)
+        for k in (1, 2, 3):
+            product(z, operands, 3, CHUNKS[k][0] // C, CHUNKS[k][1] // C, (at + (0, 1, 4)[k - 1]) % 8)
         bk2 = [again(tb2[k], at + 2 + k, *halves[k], f"st2{k}", 6144 + 1536 * k) for k in range(2)]
         c3 = [times_ratio(z[3], l_pos3, q1, *halves[0], "c30")]
         store = added(1, 3072)
@@ -391,7 +388,7 @@ def tile_moe_uni_silu_kernel(
         def second3(k):
             t0, n = TAIL[k]
             d3 = plain(z[3], l_pos4, t0, n, f"d3{k}", (4608, 6144, 7168)[k])
-            return there(d3, at + (4, 7, 0)[k], 0, n)
+            return there(d3, at + (7, 0, 4)[k], 0, n)
 
         tb3 = [second3(0), second3(1)]
         bk3 = [again(tb3[0], at + 1, *TAIL[0], "st30")]

@@ -25,8 +25,9 @@ COPY = mybir.ActivationFunctionType.Copy
 TINY = 2.0**-60
 BANK = 2048
 G1 = (512, 512, 384, 128)
-ORDER1 = tuple((b, 0, 4) for b in range(4)) + tuple((b, 4, 4) for b in range(2))
-ORDER1 = ORDER1 + ((0, 8, 3), (0, 11, 1), (1, 8, 4), (2, 4, 4), (2, 8, 4), (3, 4, 4), (3, 8, 4))
+ORDER1 = tuple((b, 0, 4) for b in range(4)) + ((0, 4, 4), (1, 4, 4), (0, 8, 3), (0, 11, 1), (1, 8, 4))
+ORDER1 = ORDER1 + tuple((b, e0, 4) for b in (2, 3) for e0 in (4, 8))
+SCALES = ((0, 4, 0, 512), (4, 8, 0, 256), (4, 8, 256, 256))
 CHUNKS = ((0, 256), (256, 384), (896, 384), (1280, 256))
 SHARE = (640, 256)
 TAIL = ((0, 384), (384, 256), (640, 128))
@@ -72,9 +73,10 @@ def tile_moe_uni_silu_kernel(
             return ratio
 
         xs = keep.tile([P, T], U8, name="xs", align_bytes=64)
-        ws = keep.tile([P, E, K], U8, name="ws", align_bytes=64)
+        ws = [keep.tile([P, ne, n], U8, name=f"ws{i}", align_bytes=64) for i, (e0, ne, c0, n) in enumerate(SCALES)]
         nc.gpsimd.memset(xs[:].bitcast(I32), 0)
-        nc.vector.memset(ws[:].rearrange("p e n -> p (e n)").bitcast(I32), 0)
+        for t in ws:
+            nc.vector.memset(t[:].rearrange("p e n -> p (e n)").bitcast(I32), 0)
         rows = keep.tile([P, T // 2], F32, name="rows")
         nc.gpsimd.memset(rows[:], 0.0)
         ident = keep.tile([P, P], F32, name="ident")
@@ -99,13 +101,24 @@ def tile_moe_uni_silu_kernel(
             nc.sync.dma_start(t[:].bitcast(I32), w_words[e0 : e0 + ne, 0].rearrange("e p n -> p e n").bitcast(I32))
             return [t[:, j, :] for j in range(ne)]
 
+        def load_scales(i):
+            e0, ne, c0, n = SCALES[i]
+            for r in range(4):
+                src = w_scales[e0 : e0 + ne, 0, r:16:4, c0 : c0 + n].rearrange("e q n -> q e n")
+                nc.sync.dma_start(ws[i][r:P:32, :, :].bitcast(I32), src.bitcast(I32))
+
+        def weight_scales(e, b):
+            i = 0 if e < 4 else 1 + b // 2
+            e0, ne, c0, n = SCALES[i]
+            return ws[i][:, e - e0, P * b - c0 : P * (b + 1) - c0]
+
         ww = load_words(0, 4)
-        for r in range(4):
-            nc.sync.dma_start(
-                ws[r:P:32, :, :].bitcast(I32), w_scales[:, 0, r:16:4, :].rearrange("e q n -> q e n").bitcast(I32)
-            )
-        ww = ww + load_words(4, 4) + load_words(8, 4)
+        load_scales(0)
+        ww = ww + load_words(4, 4)
+        load_scales(1)
+        ww = ww + load_words(8, 4)
         l_pos1 = load_list(pos1, "l_pos1")
+        load_scales(2)
         l_pos2 = load_list(pos2, "l_pos2")
         l_offs2 = load_list(offs2, "l_offs2")
         l_pos3 = load_list(pos3, "l_pos3")
@@ -145,7 +158,7 @@ def tile_moe_uni_silu_kernel(
                 nc.tensor.matmul_mx(
                     out=acc[:, j * C : (j + 1) * C],
                     lhsT=ww[e][:, 256 * b : 256 * (b + 1)].bitcast(FP4X4),
-                    lhsT_scale=ws[:, e, P * b : P * (b + 1)],
+                    lhsT_scale=weight_scales(e, b),
                     rhs=words.bitcast(FP8X4),
                     rhs_scale=scales,
                     start=True,
@@ -194,7 +207,7 @@ def tile_moe_uni_silu_kernel(
         ratio1 = spread(rcol, 0, 1)
         y = [keep.tile([P, S], F32, name=f"y{b}") for b in range(4)]
         for i, (b, e0, ne) in enumerate(ORDER1):
-            product(y, operands, b, e0, ne, (3, 4, 5, 0, 1, 2, 6, 7, 3, 6, 4, 7, 5)[i])
+            product(y, operands, b, e0, ne, (3, 4, 5, 0, 1, 2, 6, 7, 4, 0, 1, 2, 3)[i])
 
         ct = [ring.tile([P, 2, 256], BF16, name=f"ct{j}", align_bytes=64, offset=4608 + 1024 * j) for j in range(NB)]
         cw = [keep.tile([P, T], F32, name=f"cw{u}", align_bytes=64) for u in range(2)]
@@ -227,9 +240,13 @@ def tile_moe_uni_silu_kernel(
         (t0, n0), (t1, n1), (t2, n2) = TAIL
         rest = (t1, n1 + n2)
         a = [times_ratio(y[b], l_pos1, ratio1, 0, T, f"a{b}") for b in range(2)]
-        turn1(a[0], 0, 0, T, start=True)
-        turn1(a[1], 1, 0, T)
-        turn1(plain(y[0], l_pos2, 0, T, "b0"), 0, 0, T)
+        turn1(a[0], 0, 0, 4 * P, start=True)
+        turn1(a[1], 1, 0, 4 * P)
+        b0 = plain(y[0], l_pos2, 0, T, "b0")
+        turn1(b0, 0, 0, 4 * P)
+        turn1(b0[:, 4 * P : T], 0, 4 * P, 2 * P, start=True)
+        for b in range(2):
+            turn1(a[b][:, 4 * P : T], b, 4 * P, 2 * P)
         a2 = times_ratio(y[2], l_pos1, ratio1, 0, T, "a2")
         b1 = plain(y[1], l_pos2, 0, T, "b1")
         turn1(plus(y[2], l_pos2, a2[:, 0:n0], t0, n0, "s20"), 2, t0, n0)

@@ -19,17 +19,19 @@ FP8X4 = mybir.dt.float8_e4m3fn_x4
 FP4X4 = mybir.dt.float4_e2m1fn_x4
 MULT = mybir.AluOpType.mult
 ADD = mybir.AluOpType.add
+POW = mybir.AluOpType.pow
 SILU = mybir.ActivationFunctionType.Silu
 COPY = mybir.ActivationFunctionType.Copy
 
 TINY = 2.0**-60
 BANK = 2048
-G1 = (512, 512, 384, 128)
-ORDER1 = tuple((b, 0, 4) for b in range(4)) + ((0, 4, 4), (1, 4, 4), (0, 8, 3), (0, 11, 1), (1, 8, 4))
-ORDER1 = ORDER1 + tuple((b, e0, 4) for b in (2, 3) for e0 in (4, 8))
-SCALES = ((0, 4, 0, 512), (4, 8, 0, 256), (4, 8, 256, 256))
-CHUNKS = ((0, 256), (256, 384), (896, 384), (1280, 256))
-SHARE = (640, 256)
+WORDS1 = (256, 256, 512, 384, 128)
+BYTES1 = (256, 256, 512, 512)
+ORDER1 = ((0, 0, 2), (1, 0, 2), (2, 0, 4), (3, 0, 4), (0, 2, 2), (1, 2, 2))
+ORDER1 = ORDER1 + tuple((b, 4, 4) for b in range(4)) + ((0, 8, 3), (0, 11, 1)) + tuple((b, 8, 4) for b in (1, 2, 3))
+CHUNKS = tuple((s0, 256) for s0 in range(0, S, 256))
+SHARED = 160
+SUMMED = 256
 TAIL = ((0, 384), (384, 256), (640, 128))
 
 
@@ -69,16 +71,17 @@ def tile_moe_uni_silu_kernel(
                     nc.tensor.transpose(
                         bank[:, j * P : (j + 1) * P], rcol[:, j, h : h + 1].to_broadcast([P, P]), ident[:]
                     )
-                nc.scalar.copy(ratio[:, 384 * h : 384 * (h + 1)], bank[:])
+                nc.vector.tensor_copy(ratio[:, 384 * h : 384 * (h + 1)], bank[:])
             return ratio
 
         xs = keep.tile([P, T], U8, name="xs", align_bytes=64)
-        ws = [keep.tile([P, ne, n], U8, name=f"ws{i}", align_bytes=64) for i, (e0, ne, c0, n) in enumerate(SCALES)]
+        ws = [keep.tile([P, 4, K], U8, name=f"ws{i}", align_bytes=64) for i in range(3)]
         nc.gpsimd.memset(xs[:].bitcast(I32), 0)
         for t in ws:
             nc.vector.memset(t[:].rearrange("p e n -> p (e n)").bitcast(I32), 0)
-        rows = keep.tile([P, T // 2], F32, name="rows")
-        nc.gpsimd.memset(rows[:], 0.0)
+        room = early.tile([P, (5 * S - BYTES1[0]) // 4], F32, name="room", align_bytes=64, offset=BYTES1[0])
+        rows1 = room[:, 0 : T // 2]
+        nc.gpsimd.memset(rows1, 0.0)
         ident = keep.tile([P, P], F32, name="ident")
         make_identity(nc, ident[:])
 
@@ -88,11 +91,11 @@ def tile_moe_uni_silu_kernel(
         for r in range(4):
             (nc.sync if r < 2 else nc.scalar).dma_start(xs[r:P:32, :].bitcast(I32), x_scales[0, r:16:4, :].bitcast(I32))
 
-        def load_rows(gate, first):
+        def load_rows(rows, gate, first):
             flat = gate.rearrange("r p (h t) -> (r p h) t", h=2)
             nc.sync.dma_start(rows[first:4, :], flat[2 * P - 2 + first : 2 * P + 2, :])
 
-        load_rows(gate1, 0)
+        load_rows(rows1, gate1, 0)
         xw = keep.tile([P, T], I32, name="xw", align_bytes=64)
         nc.sync.dma_start(xw[:], x_words[0].rearrange("p t d -> p (t d)").bitcast(I32))
 
@@ -102,23 +105,18 @@ def tile_moe_uni_silu_kernel(
             return [t[:, j, :] for j in range(ne)]
 
         def load_scales(i):
-            e0, ne, c0, n = SCALES[i]
             for r in range(4):
-                src = w_scales[e0 : e0 + ne, 0, r:16:4, c0 : c0 + n].rearrange("e q n -> q e n")
+                src = w_scales[4 * i : 4 * i + 4, 0, r:16:4, :].rearrange("e q n -> q e n")
                 nc.sync.dma_start(ws[i][r:P:32, :, :].bitcast(I32), src.bitcast(I32))
 
         def weight_scales(e, b):
-            i = 0 if e < 4 else 1 + b // 2
-            e0, ne, c0, n = SCALES[i]
-            return ws[i][:, e - e0, P * b - c0 : P * (b + 1) - c0]
+            return ws[e // 4][:, e % 4, P * b : P * (b + 1)]
 
-        ww = load_words(0, 4)
-        load_scales(0)
-        ww = ww + load_words(4, 4)
-        load_scales(1)
-        ww = ww + load_words(8, 4)
+        ww = []
+        for i in range(3):
+            ww = ww + load_words(4 * i, 4)
+            load_scales(i)
         l_pos1 = load_list(pos1, "l_pos1")
-        load_scales(2)
         l_pos2 = load_list(pos2, "l_pos2")
         l_offs2 = load_list(offs2, "l_offs2")
         l_pos3 = load_list(pos3, "l_pos3")
@@ -128,24 +126,25 @@ def tile_moe_uni_silu_kernel(
         q1 = keep.tile([P, T], F32, name="q1")
         nc.sync.dma_start(q1[:], gate2[0])
 
-        def gate_columns(at):
+        def gate_columns(rows, at):
             bank = bank_tile(at, [P, 3, P])
             for j in range(3):
                 nc.tensor.transpose(bank[:, j, :], rows[:, j * P : (j + 1) * P], ident[:])
             return bank[:, :, 0:4].rearrange("p j (r h) -> p j r h", r=2)
 
-        turned = gate_columns(0)
-        later = early.tile([P, (5 * S - 512) // 4], F32, name="later", align_bytes=64, offset=512)
-        den = later[:, 0:NB].rearrange("p (j h) -> p j h", j=3)
-        nc.scalar.activation(den, turned[:, :, 1, :], COPY, bias=TINY)
+        turned = gate_columns(rows1, 0)
         cols = keep.tile([P, 3, 2, 2], F32, name="cols")
         cols2 = keep.tile([P, 3, 2], F32, name="cols2")
         nc.scalar.activation(cols[:], turned, COPY, bias=TINY)
         rec = keep.tile([P, 3, 2], F32, name="rec")
-        nc.vector.reciprocal(rec[:].rearrange("p j h -> p (j h)"), later[:, 0:NB])
+        minus = keep.tile([P, 3, 2], F32, name="minus")
+        nc.gpsimd.memset(minus[:], -1.0)
+        nc.gpsimd.tensor_tensor(rec[:], cols[:, :, 1, :], minus[:], POW)
         rcol = keep.tile([P, 3, 2], F32, name="rcol")
         nc.gpsimd.tensor_tensor(rcol[:], cols[:, :, 0, :], rec[:], MULT)
-        load_rows(gate2, 2)
+        rows2 = keep.tile([P, T // 2], F32, name="rows2")
+        nc.gpsimd.memset(rows2[:], 0.0)
+        load_rows(rows2, gate2, 2)
 
         def factor(step, j):
             return (cols2[:] if step else cols[:, :, 1, :])[:, j % 3, j // 3 : j // 3 + 1]
@@ -189,120 +188,108 @@ def tile_moe_uni_silu_kernel(
         def turn(dst, src, start, stop):
             nc.tensor.matmul(dst, src, ident[:], start=start, stop=stop, is_transpose=True)
 
-        gs = [early.tile([P, 512], U8, name=f"gs{i}", align_bytes=64, offset=512 * i) for i in range(3)]
+        gs = [
+            early.tile([P, n], U8, name=f"gs{i}", align_bytes=64, offset=s0)
+            for i, (s0, n) in enumerate(zip(starts(BYTES1), BYTES1))
+        ]
         gw = [
             early.tile([P, n], U32, name=f"gw{i}", align_bytes=64, offset=S + 4 * s0)
-            for i, (s0, n) in enumerate(zip(starts(G1), G1))
+            for i, (s0, n) in enumerate(zip(starts(WORDS1), WORDS1))
         ]
-        for kind, i in (("s", 0), ("w", 0), ("s", 1), ("w", 1), ("s", 2), ("w", 2), ("w", 3)):
-            if kind == "s":
-                nc.vector.tensor_copy(gs[i][:], xs[:].indirect(part(l_offs, 512 * i, 512)))
-            else:
-                nc.vector.tensor_copy(gw[i][:], xw[:].bitcast(U32).indirect(part(l_offs, starts(G1)[i], G1[i])))
-        operands = [
-            (gw[i][:, j : j + C], gs[(s0 + j) // 512][:, (s0 + j) % 512 : (s0 + j) % 512 + C])
-            for i, (s0, n) in enumerate(zip(starts(G1), G1))
-            for j in range(0, n, C)
-        ]
-        ratio1 = spread(rcol, 0, 1)
+        for i, n in enumerate(WORDS1):
+            if i < len(BYTES1):
+                nc.vector.tensor_copy(gs[i][:], xs[:].indirect(part(l_offs, starts(BYTES1)[i], BYTES1[i])))
+            nc.vector.tensor_copy(gw[i][:], xw[:].bitcast(U32).indirect(part(l_offs, starts(WORDS1)[i], n)))
+
+        def by_expert(tiles, widths):
+            return [t[:, j : j + C] for t, n in zip(tiles, widths) for j in range(0, n, C)]
+
+        operands = list(zip(by_expert(gw, WORDS1), by_expert(gs, BYTES1)))
         y = [keep.tile([P, S], F32, name=f"y{b}") for b in range(4)]
         for i, (b, e0, ne) in enumerate(ORDER1):
-            product(y, operands, b, e0, ne, (3, 4, 5, 0, 1, 2, 6, 7, 4, 0, 1, 2, 3)[i])
+            product(y, operands, b, e0, ne, (1, 2, 3, 4, 6, 7)[i] if i < 6 else (i - 1) % 6)
+            if i == 5:
+                ratio1 = spread(rcol, 0, 6)
 
-        ct = [ring.tile([P, 2, 256], BF16, name=f"ct{j}", align_bytes=64, offset=4608 + 1024 * j) for j in range(NB)]
+        ct = {}
         cw = [keep.tile([P, T], F32, name=f"cw{u}", align_bytes=64) for u in range(2)]
-        cp = [keep.tile([P, 2, T], BF16, name=f"cp{u}", align_bytes=64) for u in range(2)]
         tok = [bank_tile(j, [P, 4, P]) for j in range(NB)]
 
         def turn1(src, b, t0, n, start=False, stop=False):
             for m in range(n // P):
                 turn(tok[t0 // P + m][:, b, :], src[:, m * P : (m + 1) * P], start, stop)
 
-        def scale1(j, eng):
-            dst = ct[j][:].rearrange("p u (m e) -> p u m e", e=2)
-            src = tok[j][:].rearrange("p h (m u e) -> p u (h m) e", u=2, e=2)
+        def round1(u, j, eng, at=None):
+            at = 4608 + 1024 * j + 512 * u if at is None else at
+            ct[u, j] = ring.tile([P, 256], BF16, name=f"ct{u}{j}", align_bytes=64, offset=at)
+            dst = ct[u, j][:].rearrange("p (m e) -> p m e", e=2)
+            src = tok[j][:].rearrange("p h (m u e) -> p u (h m) e", u=2, e=2)[:, u]
             if eng == "v":
                 nc.vector.tensor_scalar(dst, src, factor(0, j), None, MULT)
             else:
                 nc.scalar.activation(dst, src, COPY, scale=factor(0, j))
 
-        def back1(backs, t0, j):
-            for u in range(2):
-                m = j - t0 // P
-                nc.tensor.transpose(backs[u][:, m * P : (m + 1) * P], ct[j][:].bitcast(F32)[:, u, :], ident[:])
+        def back1(bank, t0, u, j):
+            m = j - t0 // P
+            nc.tensor.transpose(bank[:, m * P : (m + 1) * P], ct[u, j][:].bitcast(F32), ident[:])
 
-        def words1(backs, t0, n, u):
-            nc.vector.tensor_copy(cw[u][:, t0 : t0 + n], backs[u][:])
-
-        def part1(backs, t0, n, u):
-            nc.scalar.copy(cp[u][:, :, t0 : t0 + n], backs[u][:].bitcast(BF16).rearrange("p (t e) -> p e t", e=2))
+        def words1(bank, t0, n, u, eng):
+            if eng == "v":
+                nc.vector.tensor_copy(cw[u][:, t0 : t0 + n], bank[:])
+            else:
+                nc.scalar.copy(cw[u][:, t0 : t0 + n], bank[:])
 
         (t0, n0), (t1, n1), (t2, n2) = TAIL
         rest = (t1, n1 + n2)
-        a = [times_ratio(y[b], l_pos1, ratio1, 0, T, f"a{b}") for b in range(2)]
-        turn1(a[0], 0, 0, 4 * P, start=True)
-        turn1(a[1], 1, 0, 4 * P)
-        b0 = plain(y[0], l_pos2, 0, T, "b0")
-        turn1(b0, 0, 0, 4 * P)
-        turn1(b0[:, 4 * P : T], 0, 4 * P, 2 * P, start=True)
         for b in range(2):
-            turn1(a[b][:, 4 * P : T], b, 4 * P, 2 * P)
+            turn1(times_ratio(y[b], l_pos1, ratio1, 0, T, f"a{b}"), b, 0, T, start=b == 0)
+            turn1(plain(y[b], l_pos2, 0, T, f"b{b}"), b, 0, T)
         a2 = times_ratio(y[2], l_pos1, ratio1, 0, T, "a2")
-        b1 = plain(y[1], l_pos2, 0, T, "b1")
-        turn1(plus(y[2], l_pos2, a2[:, 0:n0], t0, n0, "s20"), 2, t0, n0)
-        turn1(b1[:, 0:n0], 1, t0, n0)
-        turn1(times_ratio(y[3], l_pos1, ratio1, t0, n0, "a30"), 3, t0, n0)
-        turn1(plain(y[3], l_pos2, t0, n0, "b30", 0), 3, t0, n0, stop=True)
-        turn1(b1[:, n0:T], 1, *rest)
-        turn1(times_ratio(y[3], l_pos1, ratio1, *rest, "a31"), 3, *rest)
+        turn1(a2[:, SUMMED:T], 2, SUMMED, T - SUMMED)
+        turn1(plain(y[2], l_pos2, SUMMED, T - SUMMED, "b2"), 2, SUMMED, T - SUMMED)
+        turn1(plus(y[2], l_pos2, a2[:, 0:SUMMED], 0, SUMMED, "s2"), 2, 0, SUMMED)
+        turn1(plain(y[3], l_pos2, t0, n0, "b30"), 3, t0, n0)
+        turn1(times_ratio(y[3], l_pos1, ratio1, t0, n0, "a30"), 3, t0, n0, stop=True)
         turn1(plain(y[3], l_pos2, *rest, "b31"), 3, *rest)
-        backs0 = [bank_tile(6 + u, [P, n0]) for u in range(2)]
-        scale1(0, "s")
-        back1(backs0, t0, 0)
-        turn1(plus(y[2], l_pos2, a2[:, t1 : t1 + n1], t1, n1, "s21", 0), 2, t1, n1, stop=True)
-        scale1(1, "s")
-        back1(backs0, t0, 1)
-        turn1(plus(y[2], l_pos2, a2[:, t2:T], t2, n2, "s22", 1024), 2, t2, n2, stop=True)
-        scale1(2, "s")
-        back1(backs0, t0, 2)
-        backs1 = [bank_tile(u, [P, n1]) for u in range(2)]
-        scale1(3, "v")
-        scale1(4, "s")
-        back1(backs1, t1, 3)
-        back1(backs1, t1, 4)
-        scale1(5, "v")
-        backs2 = [bank_tile(2 + 3 * u, [P, n2]) for u in range(2)]
-        back1(backs2, t2, 5)
-        for u in range(2):
-            nc.scalar.copy(cw[u][:, t0 : t0 + n0], backs0[u][:])
-            src = cw[u][:].bitcast(BF16)[:, 0 : 2 * n0].rearrange("p (t e) -> p e t", e=2)
-            nc.gpsimd.tensor_copy(cp[u][:, :, 0:n0], src)
-        for u in range(2):
-            for piece in ((backs1, t1, n1), (backs2, t2, n2)):
-                words1(*piece, u)
-                part1(*piece, u)
+        turn1(times_ratio(y[3], l_pos1, ratio1, t1, n1, "a31", 0), 3, t1, n1, stop=True)
+        first0 = bank_tile(6, [P, n0])
+        first1 = bank_tile(7, [P, n1 + n2])
+        round1(0, 0, "s")
+        back1(first0, t0, 0, 0)
+        turn1(times_ratio(y[3], l_pos1, ratio1, t2, n2, "a32", 1280), 3, t2, n2, stop=True)
+        for j, eng in ((1, "s"), (3, "v"), (2, "s"), (5, "v"), (4, "s")):
+            round1(0, j, eng)
+            back1(first0 if j < 3 else first1, t0 if j < 3 else t1, 0, j)
+        round1(1, 0, "s", 0)
+        round1(1, 1, "v", 1024)
+        round1(1, 2, "v", 1536)
+        words1(first0, t0, n0, 0, "s")
+        words1(first1, *rest, 0, "v")
+        second0 = bank_tile(0, [P, n0])
+        second1 = bank_tile(1, [P, n1 + n2])
+        for j in range(NB):
+            if j > 2:
+                round1(1, j, "s")
+            back1(second0 if j < 3 else second1, t0 if j < 3 else t1, 1, j)
+        words1(second0, t0, n0, 1, "s")
+        words1(second1, *rest, 1, "s")
 
         qw = keep.tile([P, S], U32, name="qw", align_bytes=64)
         qs = keep.tile([P, S], U8, name="qs", align_bytes=64)
-        woven = {}
 
-        def gather_pairs(k):
+        def pairs(dst, u, s0, n):
+            nc.vector.tensor_copy(dst, cw[u][:].bitcast(U32).indirect(part(l_offs2, s0, n)))
+
+        def planes_tile(name, n, at):
+            return mid.tile([P, 2, n], U32, name=name, align_bytes=64, offset=at)
+
+        def woven_tile(name, n, at):
+            return mid.tile([P, n, 2], U32, name=name, align_bytes=64, offset=at)
+
+        def quantise(woven, k):
             s0, n = CHUNKS[k]
-            pl = mid.tile([P, 2, n], U32, name=f"pl{k}", align_bytes=64, offset=3072 * (k % 2))
-            for u in range(2):
-                nc.vector.tensor_copy(pl[:, u, :], cw[u][:].bitcast(U32).indirect(part(l_offs2, s0, n)))
-            return pl
-
-        def weave(k, pl):
-            woven[k] = mid.tile([P, CHUNKS[k][1], 2], U32, name=f"woven{k}", align_bytes=64, offset=6144 if k else 8192)
-            nc.gpsimd.tensor_copy(woven[k][:], pl[:].rearrange("p u n -> p n u"))
-
-        def quantise(src, s0, n, words=None):
-            words = qw[:, s0 : s0 + n] if words is None else words
-            nc.vector.quantize_mx(out=words.bitcast(FP8X4), scales=qs[:, s0 : s0 + n], in_=src)
-
-        def quantise_woven(k):
-            quantise(woven[k][:].rearrange("p n u -> p (n u)").bitcast(BF16), *CHUNKS[k])
+            src = woven[:].rearrange("p n u -> p (n u)").bitcast(BF16)
+            nc.vector.quantize_mx(out=qw[:, s0 : s0 + n].bitcast(FP8X4), scales=qs[:, s0 : s0 + n], in_=src)
 
         operands = [(qw[:, e * C : (e + 1) * C], qs[:, e * C : (e + 1) * C]) for e in range(E)]
         z = [keep.tile([P, S], F32, name=f"z{b}") for b in range(4)]
@@ -312,40 +299,58 @@ def tile_moe_uni_silu_kernel(
             product(z, operands, b, s0 // C, n // C, turns[0] % 8)
             turns[0] = turns[0] + 1
 
-        singles = mid.tile([P, SHARE[1], 4], BF16, name="singles", align_bytes=64, offset=10240)
-        for t in range(4):
-            nc.scalar.activation(singles[:, :, t], cp[t // 2][:, t % 2, :].indirect(part(l_offs2, *SHARE)), COPY)
-        nc.scalar.copy(cols2[:], gate_columns(5)[:, :, 1, :])
-        weave(0, gather_pairs(0))
-        pl = gather_pairs(1)
-        quantise_woven(0)
-        weave(1, pl)
+        places = (6144, 8192, 9216, 11200, 13184, 0)
+        woven = []
+
+        def weave(k, planes, shared):
+            woven.append(woven_tile(f"woven{k}", 256, places[k]))
+            src = planes.rearrange("p u n -> p n u")
+            if shared:
+                nc.gpsimd.tensor_copy(woven[k][:, 0:shared, :], src[:, 0:shared, :])
+            nc.scalar.copy(woven[k][:, shared:256, :], src[:, shared:256, :])
+
+        def both(k, at):
+            pl = planes_tile(f"pl{k}", 256, at)
+            for u in range(2):
+                pairs(pl[:, u, :], u, *CHUNKS[k])
+            return pl[:]
+
+        lead = planes_tile("lead", 512, 0)
+        pairs(lead[:, 0, :], 0, 0, 512)
+        pl = planes_tile("pl2", 256, 4096)
+        pairs(pl[:, 0, :], 0, *CHUNKS[2])
+        for k in range(2):
+            s0, n = CHUNKS[k]
+            pairs(lead[:, 1, s0 : s0 + n], 1, s0, n)
+            weave(k, lead[:, :, s0 : s0 + n], 0)
+        nc.scalar.copy(cols2[:], gate_columns(rows2, 1)[:, :, 1, :])
+        pairs(pl[:, 1, :], 1, *CHUNKS[2])
+        quantise(woven[0], 0)
+        quantise(woven[1], 1)
+        weave(2, pl[:], SHARED)
         for b in range(4):
             product2(b, *CHUNKS[0])
-        pl = gather_pairs(2)
-        qw2 = mid.tile([P, SHARE[1]], U32, name="qw2", align_bytes=64, offset=9216)
-        quantise(singles[:].rearrange("p n t -> p (n t)"), *SHARE, qw2[:])
-        for j in range(0, SHARE[1], C):
-            operands[(SHARE[0] + j) // C] = (qw2[:, j : j + C], qs[:, SHARE[0] + j : SHARE[0] + j + C])
-        quantise_woven(1)
-        weave(2, pl)
+        pl = both(3, 2048)
+        quantise(woven[2], 2)
+        weave(3, pl, SHARED)
         for b in range(4):
-            product2(b, *SHARE)
-        s0, n = CHUNKS[3]
-        woven[3] = mid.tile([P, n, 2], U32, name="woven3", align_bytes=64, offset=3072)
-        for u in range(2):
-            nc.vector.tensor_copy(woven[3][:, :, u], cw[u][:].bitcast(U32).indirect(part(l_offs2, s0, n)))
-        quantise_woven(2)
-        quantise_woven(3)
-        for b in range(2):
             product2(b, *CHUNKS[1])
-        for k in (2, 3):
+        pl = both(4, 4096)
+        quantise(woven[3], 3)
+        weave(4, pl, SHARED)
+        for b in range(4):
+            product2(b, *CHUNKS[2])
+        woven.append(woven_tile("woven5", 256, 2048))
+        for u in range(2):
+            pairs(woven[5][:, :, u], u, *CHUNKS[5])
+        quantise(woven[4], 4)
+        quantise(woven[5], 5)
+        for b in range(3):
+            product2(b, *CHUNKS[3])
+        for k in (4, 5):
             product2(0, *CHUNKS[k])
-        for k in (2, 3):
-            product2(1, *CHUNKS[k])
+        product2(1, 1024, 512)
         d0 = plain(z[0], l_pos4, 0, T, "d0", 3072)
-        product(z, operands, 2, CHUNKS[1][0] // C, CHUNKS[1][1] // C, (turns[0] - 3) % 8)
-        product2(2, *CHUNKS[2])
 
         H = T // 2
         halves = ((0, H), (H, H))
@@ -383,7 +388,7 @@ def tile_moe_uni_silu_kernel(
         c0 = times_ratio(z[0], l_pos3, q1, 0, T, "c0")
         tb0 = [there(d0, at + k, *halves[k]) for k in range(2)]
         c1 = times_ratio(z[1], l_pos3, q1, 0, T, "c1")
-        product(z, operands, 2, CHUNKS[3][0] // C, CHUNKS[3][1] // C, (at + 4) % 8)
+        product(z, operands, 2, 8, 4, (at + 4) % 8)
         c2 = times_ratio(z[2], l_pos3, q1, 0, T, "c2")
         bk0 = [again(tb0[k], at + 2 + k, *halves[k], f"st0{k}", 1536 * k) for k in range(2)]
         store = added(0, 0)
@@ -392,8 +397,8 @@ def tile_moe_uni_silu_kernel(
         store()
         d2 = plain(z[2], l_pos4, 0, T, "d2", 3072)
         tb2 = [there(d2, at + 5 + k, *halves[k]) for k in range(2)]
-        for k in (1, 2, 3):
-            product(z, operands, 3, CHUNKS[k][0] // C, CHUNKS[k][1] // C, (at + (0, 1, 4)[k - 1]) % 8)
+        product(z, operands, 3, 6, 2, at % 8)
+        product(z, operands, 3, 8, 4, (at + 1) % 8)
         bk2 = [again(tb2[k], at + 2 + k, *halves[k], f"st2{k}", 6144 + 1536 * k) for k in range(2)]
         c3 = [times_ratio(z[3], l_pos3, q1, *halves[0], "c30")]
         store = added(1, 3072)

@@ -26,12 +26,12 @@ COPY = mybir.ActivationFunctionType.Copy
 TINY = 2.0**-60
 BANK = 2048
 WORDS1 = (256, 256, 512, 384, 128)
-BYTES1 = (256, 256, 512, 512)
+BYTES1 = (512, 512, 512)
 ORDER1 = ((0, 0, 2), (1, 0, 2), (2, 0, 4), (3, 0, 4), (0, 2, 2), (1, 2, 2))
 ORDER1 = ORDER1 + tuple((b, 4, 4) for b in range(4)) + ((0, 8, 3), (0, 11, 1)) + tuple((b, 8, 4) for b in (1, 2, 3))
 CHUNKS = tuple((s0, 256) for s0 in range(0, S, 256))
 SHARED = 160
-SUMMED = 256
+SUMMED = 128
 TAIL = ((0, 384), (384, 256), (640, 128))
 
 
@@ -196,10 +196,10 @@ def tile_moe_uni_silu_kernel(
             early.tile([P, n], U32, name=f"gw{i}", align_bytes=64, offset=S + 4 * s0)
             for i, (s0, n) in enumerate(zip(starts(WORDS1), WORDS1))
         ]
-        for i, n in enumerate(WORDS1):
-            if i < len(BYTES1):
-                nc.vector.tensor_copy(gs[i][:], xs[:].indirect(part(l_offs, starts(BYTES1)[i], BYTES1[i])))
-            nc.vector.tensor_copy(gw[i][:], xw[:].bitcast(U32).indirect(part(l_offs, starts(WORDS1)[i], n)))
+        for i, (s0, n) in enumerate(zip(starts(WORDS1), WORDS1)):
+            if s0 % 512 == 0:
+                nc.vector.tensor_copy(gs[s0 // 512][:], xs[:].indirect(part(l_offs, s0, 512)))
+            nc.vector.tensor_copy(gw[i][:], xw[:].bitcast(U32).indirect(part(l_offs, s0, n)))
 
         def by_expert(tiles, widths):
             return [t[:, j : j + C] for t, n in zip(tiles, widths) for j in range(0, n, C)]
@@ -246,26 +246,26 @@ def tile_moe_uni_silu_kernel(
             turn1(plain(y[b], l_pos2, 0, T, f"b{b}"), b, 0, T)
         a2 = times_ratio(y[2], l_pos1, ratio1, 0, T, "a2")
         turn1(a2[:, SUMMED:T], 2, SUMMED, T - SUMMED)
-        turn1(plain(y[2], l_pos2, SUMMED, T - SUMMED, "b2"), 2, SUMMED, T - SUMMED)
         turn1(plus(y[2], l_pos2, a2[:, 0:SUMMED], 0, SUMMED, "s2"), 2, 0, SUMMED)
-        turn1(plain(y[3], l_pos2, t0, n0, "b30"), 3, t0, n0)
-        turn1(times_ratio(y[3], l_pos1, ratio1, t0, n0, "a30"), 3, t0, n0, stop=True)
-        turn1(plain(y[3], l_pos2, *rest, "b31"), 3, *rest)
-        turn1(times_ratio(y[3], l_pos1, ratio1, t1, n1, "a31", 0), 3, t1, n1, stop=True)
-        first0 = bank_tile(6, [P, n0])
-        first1 = bank_tile(7, [P, n1 + n2])
-        round1(0, 0, "s")
-        back1(first0, t0, 0, 0)
-        turn1(times_ratio(y[3], l_pos1, ratio1, t2, n2, "a32", 1280), 3, t2, n2, stop=True)
-        for j, eng in ((1, "s"), (3, "v"), (2, "s"), (5, "v"), (4, "s")):
+        turn1(plain(y[2], l_pos2, SUMMED, T - SUMMED, "b2"), 2, SUMMED, T - SUMMED)
+        for k, (t, n) in enumerate(TAIL):
+            turn1(times_ratio(y[3], l_pos1, ratio1, t, n, f"a3{k}"), 3, t, n)
+            turn1(plain(y[3], l_pos2, t, n, f"b3{k}", (None, 0, 1280)[k]), 3, t, n, stop=True)
+        first = [bank_tile(6, [P, n0]), bank_tile(7, [P, n1])]
+        for j, eng in enumerate("vsvs"):
             round1(0, j, eng)
-            back1(first0 if j < 3 else first1, t0 if j < 3 else t1, 0, j)
-        round1(1, 0, "s", 0)
-        round1(1, 1, "v", 1024)
-        round1(1, 2, "v", 1536)
-        words1(first0, t0, n0, 0, "s")
-        words1(first1, *rest, 0, "v")
-        second0 = bank_tile(0, [P, n0])
+            back1(first[j // 3], TAIL[j // 3][0], 0, j)
+        round1(0, 5, "v")
+        round1(0, 4, "s")
+        round1(1, 0, "v", 1024)
+        first.append(bank_tile(0, [P, n2]))
+        back1(first[1], t1, 0, 4)
+        back1(first[2], t2, 0, 5)
+        round1(1, 2, "s", 0)
+        round1(1, 1, "v", 1536)
+        for k, eng in enumerate("ssv"):
+            words1(first[k], *TAIL[k], 0, eng)
+        second0 = bank_tile(2, [P, n0])
         second1 = bank_tile(1, [P, n1 + n2])
         for j in range(NB):
             if j > 2:

@@ -28,7 +28,9 @@ BANK = 2048
 WORDS1 = (256, 256, 512, 384, 128)
 BYTES1 = (512, 512, 512)
 ORDER1 = ((0, 0, 2), (1, 0, 2), (2, 0, 4), (3, 0, 4), (0, 2, 2), (1, 2, 2))
-ORDER1 = ORDER1 + tuple((b, 4, 4) for b in range(4)) + ((0, 8, 3), (0, 11, 1)) + tuple((b, 8, 4) for b in (1, 2, 3))
+ORDER1 = ORDER1 + tuple((b, 4, 4) for b in range(4)) + ((0, 8, 3), (0, 11, 1), (1, 8, 4))
+ORDER1 = ORDER1 + tuple((b, e0, 2) for b in (2, 3) for e0 in (8, 10))
+SCALES = ((0, 0, 512), (4, 0, 512), (8, 0, 256), (8, 256, 256))
 CHUNKS = tuple((s0, 256) for s0 in range(0, S, 256))
 SHARED = 160
 SUMMED = 128
@@ -75,7 +77,7 @@ def tile_moe_uni_silu_kernel(
             return ratio
 
         xs = keep.tile([P, T], U8, name="xs", align_bytes=64)
-        ws = [keep.tile([P, 4, K], U8, name=f"ws{i}", align_bytes=64) for i in range(3)]
+        ws = [keep.tile([P, 4, n], U8, name=f"ws{i}", align_bytes=64) for i, (e0, c0, n) in enumerate(SCALES)]
         nc.gpsimd.memset(xs[:].bitcast(I32), 0)
         for t in ws:
             nc.vector.memset(t[:].rearrange("p e n -> p (e n)").bitcast(I32), 0)
@@ -105,18 +107,22 @@ def tile_moe_uni_silu_kernel(
             return [t[:, j, :] for j in range(ne)]
 
         def load_scales(i):
+            e0, c0, n = SCALES[i]
             for r in range(4):
-                src = w_scales[4 * i : 4 * i + 4, 0, r:16:4, :].rearrange("e q n -> q e n")
+                src = w_scales[e0 : e0 + 4, 0, r:16:4, c0 : c0 + n].rearrange("e q n -> q e n")
                 nc.sync.dma_start(ws[i][r:P:32, :, :].bitcast(I32), src.bitcast(I32))
 
         def weight_scales(e, b):
-            return ws[e // 4][:, e % 4, P * b : P * (b + 1)]
+            i = e // 4 if e < 8 else 2 + b // 2
+            c0 = SCALES[i][1]
+            return ws[i][:, e % 4, P * b - c0 : P * (b + 1) - c0]
 
         ww = []
         for i in range(3):
             ww = ww + load_words(4 * i, 4)
             load_scales(i)
         l_pos1 = load_list(pos1, "l_pos1")
+        load_scales(3)
         l_pos2 = load_list(pos2, "l_pos2")
         l_offs2 = load_list(offs2, "l_offs2")
         l_pos3 = load_list(pos3, "l_pos3")
@@ -207,7 +213,7 @@ def tile_moe_uni_silu_kernel(
         operands = list(zip(by_expert(gw, WORDS1), by_expert(gs, BYTES1)))
         y = [keep.tile([P, S], F32, name=f"y{b}") for b in range(4)]
         for i, (b, e0, ne) in enumerate(ORDER1):
-            product(y, operands, b, e0, ne, (1, 2, 3, 4, 6, 7)[i] if i < 6 else (i - 1) % 6)
+            product(y, operands, b, e0, ne, (1, 2, 3, 4, 6, 7, 5, 0, 1, 2, 3, 4, 5, 0, 1, 2, 3)[i])
             if i == 5:
                 ratio1 = spread(rcol, 0, 6)
 
@@ -241,9 +247,14 @@ def tile_moe_uni_silu_kernel(
 
         (t0, n0), (t1, n1), (t2, n2) = TAIL
         rest = (t1, n1 + n2)
-        for b in range(2):
-            turn1(times_ratio(y[b], l_pos1, ratio1, 0, T, f"a{b}"), b, 0, T, start=b == 0)
-            turn1(plain(y[b], l_pos2, 0, T, f"b{b}"), b, 0, T)
+        a0 = times_ratio(y[0], l_pos1, ratio1, 0, T, "a0")
+        turn1(a0, 0, 0, 4 * P, start=True)
+        b0 = plain(y[0], l_pos2, 0, T, "b0")
+        turn1(b0[:, 4 * P : T], 0, 4 * P, 2 * P, start=True)
+        turn1(a0[:, 4 * P : T], 0, 4 * P, 2 * P)
+        turn1(b0, 0, 0, 4 * P)
+        turn1(times_ratio(y[1], l_pos1, ratio1, 0, T, "a1"), 1, 0, T)
+        turn1(plain(y[1], l_pos2, 0, T, "b1"), 1, 0, T)
         a2 = times_ratio(y[2], l_pos1, ratio1, 0, T, "a2")
         turn1(a2[:, SUMMED:T], 2, SUMMED, T - SUMMED)
         turn1(plus(y[2], l_pos2, a2[:, 0:SUMMED], 0, SUMMED, "s2"), 2, 0, SUMMED)
@@ -299,7 +310,7 @@ def tile_moe_uni_silu_kernel(
             product(z, operands, b, s0 // C, n // C, turns[0] % 8)
             turns[0] = turns[0] + 1
 
-        places = (6144, 8192, 9216, 11200, 13184, 0)
+        places = (6144, 8192, 10240, 12224, 14208, 0)
         woven = []
 
         def weave(k, planes, shared):
@@ -323,11 +334,11 @@ def tile_moe_uni_silu_kernel(
             s0, n = CHUNKS[k]
             pairs(lead[:, 1, s0 : s0 + n], 1, s0, n)
             weave(k, lead[:, :, s0 : s0 + n], 0)
-        nc.scalar.copy(cols2[:], gate_columns(rows2, 1)[:, :, 1, :])
         pairs(pl[:, 1, :], 1, *CHUNKS[2])
+        weave(2, pl[:], 0)
+        nc.scalar.copy(cols2[:], gate_columns(rows2, 1)[:, :, 1, :])
         quantise(woven[0], 0)
         quantise(woven[1], 1)
-        weave(2, pl[:], SHARED)
         for b in range(4):
             product2(b, *CHUNKS[0])
         pl = both(3, 2048)

@@ -28,10 +28,8 @@ BANK = 2048
 WORDS1 = (256, 256, 512, 384, 128)
 BYTES1 = (512, 512, 512)
 ORDER1 = ((0, 0, 2), (1, 0, 2), (2, 0, 4), (3, 0, 4), (0, 2, 2), (1, 2, 2))
-ORDER1 = ORDER1 + tuple((b, 4, 4) for b in range(4)) + ((0, 8, 3), (0, 11, 1), (1, 8, 4))
-ORDER1 = ORDER1 + tuple((b, e0, 2) for b in (2, 3) for e0 in (8, 10))
-SCALES = ((0, 0, 512), (4, 0, 512), (8, 0, 256), (8, 256, 256))
-CHUNKS = tuple((s0, 256) for s0 in range(0, S, 256))
+ORDER1 = ORDER1 + tuple((b, 4, 4) for b in range(4)) + ((0, 8, 3), (0, 11, 1)) + tuple((b, 8, 4) for b in (1, 2, 3))
+CHUNKS = ((0, 256), (256, 512), (768, 256), (1024, 256), (1280, 256))
 SHARED = 160
 SUMMED = 128
 TAIL = ((0, 384), (384, 256), (640, 128))
@@ -77,7 +75,7 @@ def tile_moe_uni_silu_kernel(
             return ratio
 
         xs = keep.tile([P, T], U8, name="xs", align_bytes=64)
-        ws = [keep.tile([P, 4, n], U8, name=f"ws{i}", align_bytes=64) for i, (e0, c0, n) in enumerate(SCALES)]
+        ws = [keep.tile([P, 4, K], U8, name=f"ws{i}", align_bytes=64) for i in range(3)]
         nc.gpsimd.memset(xs[:].bitcast(I32), 0)
         for t in ws:
             nc.vector.memset(t[:].rearrange("p e n -> p (e n)").bitcast(I32), 0)
@@ -107,22 +105,18 @@ def tile_moe_uni_silu_kernel(
             return [t[:, j, :] for j in range(ne)]
 
         def load_scales(i):
-            e0, c0, n = SCALES[i]
             for r in range(4):
-                src = w_scales[e0 : e0 + 4, 0, r:16:4, c0 : c0 + n].rearrange("e q n -> q e n")
+                src = w_scales[4 * i : 4 * i + 4, 0, r:16:4, :].rearrange("e q n -> q e n")
                 nc.sync.dma_start(ws[i][r:P:32, :, :].bitcast(I32), src.bitcast(I32))
 
         def weight_scales(e, b):
-            i = e // 4 if e < 8 else 2 + b // 2
-            c0 = SCALES[i][1]
-            return ws[i][:, e % 4, P * b - c0 : P * (b + 1) - c0]
+            return ws[e // 4][:, e % 4, P * b : P * (b + 1)]
 
         ww = []
         for i in range(3):
             ww = ww + load_words(4 * i, 4)
             load_scales(i)
         l_pos1 = load_list(pos1, "l_pos1")
-        load_scales(3)
         l_pos2 = load_list(pos2, "l_pos2")
         l_offs2 = load_list(offs2, "l_offs2")
         l_pos3 = load_list(pos3, "l_pos3")
@@ -213,7 +207,7 @@ def tile_moe_uni_silu_kernel(
         operands = list(zip(by_expert(gw, WORDS1), by_expert(gs, BYTES1)))
         y = [keep.tile([P, S], F32, name=f"y{b}") for b in range(4)]
         for i, (b, e0, ne) in enumerate(ORDER1):
-            product(y, operands, b, e0, ne, (1, 2, 3, 4, 6, 7, 5, 0, 1, 2, 3, 4, 5, 0, 1, 2, 3)[i])
+            product(y, operands, b, e0, ne, (1, 2, 3, 4, 6, 7)[i] if i < 6 else (i - 1) % 6)
             if i == 5:
                 ratio1 = spread(rcol, 0, 6)
 
@@ -247,14 +241,9 @@ def tile_moe_uni_silu_kernel(
 
         (t0, n0), (t1, n1), (t2, n2) = TAIL
         rest = (t1, n1 + n2)
-        a0 = times_ratio(y[0], l_pos1, ratio1, 0, T, "a0")
-        turn1(a0, 0, 0, 4 * P, start=True)
-        b0 = plain(y[0], l_pos2, 0, T, "b0")
-        turn1(b0[:, 4 * P : T], 0, 4 * P, 2 * P, start=True)
-        turn1(a0[:, 4 * P : T], 0, 4 * P, 2 * P)
-        turn1(b0, 0, 0, 4 * P)
-        turn1(times_ratio(y[1], l_pos1, ratio1, 0, T, "a1"), 1, 0, T)
-        turn1(plain(y[1], l_pos2, 0, T, "b1"), 1, 0, T)
+        for b in range(2):
+            turn1(times_ratio(y[b], l_pos1, ratio1, 0, T, f"a{b}"), b, 0, T, start=b == 0)
+            turn1(plain(y[b], l_pos2, 0, T, f"b{b}"), b, 0, T)
         a2 = times_ratio(y[2], l_pos1, ratio1, 0, T, "a2")
         turn1(a2[:, SUMMED:T], 2, SUMMED, T - SUMMED)
         turn1(plus(y[2], l_pos2, a2[:, 0:SUMMED], 0, SUMMED, "s2"), 2, 0, SUMMED)
@@ -310,55 +299,50 @@ def tile_moe_uni_silu_kernel(
             product(z, operands, b, s0 // C, n // C, turns[0] % 8)
             turns[0] = turns[0] + 1
 
-        places = (6144, 8192, 10240, 12224, 14208, 0)
+        planes_at = (0, 2048, 0, 2048)
+        woven_at = (6144, 8192, 11264, 12288, 0)
         woven = []
 
         def weave(k, planes, shared):
-            woven.append(woven_tile(f"woven{k}", 256, places[k]))
-            src = planes.rearrange("p u n -> p n u")
+            n = CHUNKS[k][1]
+            woven.append(woven_tile(f"woven{k}", n, woven_at[k]))
+            src = planes[:].rearrange("p u n -> p n u")
             if shared:
                 nc.gpsimd.tensor_copy(woven[k][:, 0:shared, :], src[:, 0:shared, :])
-            nc.scalar.copy(woven[k][:, shared:256, :], src[:, shared:256, :])
+            nc.scalar.copy(woven[k][:, shared:n, :], src[:, shared:n, :])
 
-        def both(k, at):
-            pl = planes_tile(f"pl{k}", 256, at)
+        def both(k):
+            pl = planes_tile(f"pl{k}", CHUNKS[k][1], planes_at[k])
             for u in range(2):
                 pairs(pl[:, u, :], u, *CHUNKS[k])
-            return pl[:]
+            return pl
 
-        lead = planes_tile("lead", 512, 0)
-        pairs(lead[:, 0, :], 0, 0, 512)
-        pl = planes_tile("pl2", 256, 4096)
-        pairs(pl[:, 0, :], 0, *CHUNKS[2])
+        lead = [planes_tile(f"pl{k}", CHUNKS[k][1], planes_at[k]) for k in range(2)]
         for k in range(2):
-            s0, n = CHUNKS[k]
-            pairs(lead[:, 1, s0 : s0 + n], 1, s0, n)
-            weave(k, lead[:, :, s0 : s0 + n], 0)
-        pairs(pl[:, 1, :], 1, *CHUNKS[2])
-        weave(2, pl[:], 0)
+            pairs(lead[k][:, 0, :], 0, *CHUNKS[k])
+        for k in range(2):
+            pairs(lead[k][:, 1, :], 1, *CHUNKS[k])
+            weave(k, lead[k], 0)
         nc.scalar.copy(cols2[:], gate_columns(rows2, 1)[:, :, 1, :])
         quantise(woven[0], 0)
+        pl = both(2)
         quantise(woven[1], 1)
+        weave(2, pl, SHARED)
         for b in range(4):
             product2(b, *CHUNKS[0])
-        pl = both(3, 2048)
+        pl = both(3)
         quantise(woven[2], 2)
         weave(3, pl, SHARED)
         for b in range(4):
             product2(b, *CHUNKS[1])
-        pl = both(4, 4096)
-        quantise(woven[3], 3)
-        weave(4, pl, SHARED)
-        for b in range(4):
-            product2(b, *CHUNKS[2])
-        woven.append(woven_tile("woven5", 256, 2048))
+        woven.append(woven_tile("woven4", 256, woven_at[4]))
         for u in range(2):
-            pairs(woven[5][:, :, u], u, *CHUNKS[5])
+            pairs(woven[4][:, :, u], u, *CHUNKS[4])
+        quantise(woven[3], 3)
         quantise(woven[4], 4)
-        quantise(woven[5], 5)
         for b in range(3):
-            product2(b, *CHUNKS[3])
-        for k in (4, 5):
+            product2(b, *CHUNKS[2])
+        for k in (3, 4):
             product2(0, *CHUNKS[k])
         product2(1, 1024, 512)
         d0 = plain(z[0], l_pos4, 0, T, "d0", 3072)

from contextlib import ExitStack

import concourse.mybir as mybir
from concourse.masks import make_identity

K, T, E, C = 512, 768, 12, 128
S = E * C
P = 128
NB = T // P
FLOPS = 2 * 2 * K * K * S

F32 = mybir.dt.float32
BF16 = mybir.dt.bfloat16
I32 = mybir.dt.int32
U32 = mybir.dt.uint32
U16 = mybir.dt.uint16
U8 = mybir.dt.uint8
FP8X4 = mybir.dt.float8_e4m3fn_x4
FP4X4 = mybir.dt.float4_e2m1fn_x4
MULT = mybir.AluOpType.mult
ADD = mybir.AluOpType.add
POW = mybir.AluOpType.pow
SILU = mybir.ActivationFunctionType.Silu
COPY = mybir.ActivationFunctionType.Copy

TINY = 2.0**-60
BANK = 2048
WORDS1 = (256, 256, 512, 384, 128)
BYTES1 = (512, 512, 512)
ORDER1 = ((0, 0, 2), (1, 0, 2), (2, 0, 4), (3, 0, 4), (0, 2, 2), (1, 2, 2))
ORDER1 = ORDER1 + tuple((b, 4, 4) for b in range(4)) + ((0, 8, 3), (0, 11, 1)) + tuple((b, 8, 4) for b in (1, 2, 3))
CHUNKS = ((0, 256), (256, 512), (768, 256), (1024, 256), (1280, 256))
SHARED = 160
SUMMED = 128
TAIL = ((0, 384), (384, 256), (640, 128))


def starts(widths):
    return [sum(widths[:i]) for i in range(len(widths))]


def tile_moe_uni_silu_kernel(
    tc, x_words, x_scales, w_words, w_scales, gate1, gate2, offs, pos1, pos2, offs2, pos3, pos4, out
):
    nc = tc.nc
    with ExitStack() as ctx:
        keep = ctx.enter_context(tc.tile_pool(name="keep", bufs=1))
        early = ctx.enter_context(tc.tile_pool(name="early", bufs=1))
        mid = ctx.enter_context(tc.tile_pool(name="mid", bufs=1))
        ring = ctx.enter_context(tc.tile_pool(name="ring", bufs=1))
        psum = ctx.enter_context(tc.psum_pool(name="psum", bufs=1))
        made = []

        def bank_tile(k, shape):
            made.append(k)
            return psum.tile(shape, F32, name=f"bank{len(made)}", offset=BANK * k)

        def load_list(src, name):
            t = keep.tile([P, src.shape[1]], U16, name=name)
            nc.sync.dma_start(t[:], src)
            return t

        def part(lst, a, n):
            return lst[:, a // 16 : (a + n) // 16]

        def spread(rcol, step, at):
            ratio = keep.tile([P, T], F32, name=f"ratio{step}")
            for h in range(2):
                bank = bank_tile(at + h, [P, 384])
                for j in range(3):
                    nc.tensor.transpose(
                        bank[:, j * P : (j + 1) * P], rcol[:, j, h : h + 1].to_broadcast([P, P]), ident[:]
                    )
                nc.vector.tensor_copy(ratio[:, 384 * h : 384 * (h + 1)], bank[:])
            return ratio

        xs = keep.tile([P, T], U8, name="xs", align_bytes=64)
        ws = [keep.tile([P, 4, K], U8, name=f"ws{i}", align_bytes=64) for i in range(3)]
        nc.gpsimd.memset(xs[:].bitcast(I32), 0)
        for t in ws:
            nc.vector.memset(t[:].rearrange("p e n -> p (e n)").bitcast(I32), 0)
        room = early.tile([P, (5 * S - BYTES1[0]) // 4], F32, name="room", align_bytes=64, offset=BYTES1[0])
        rows1 = room[:, 0 : T // 2]
        nc.gpsimd.memset(rows1, 0.0)
        ident = keep.tile([P, P], F32, name="ident")
        make_identity(nc, ident[:])

        warm = keep.tile([P, 1], F32, name="warm")
        nc.scalar.activation(warm[:], ident[:, 0:1], SILU)
        l_offs = load_list(offs, "l_offs")
        for r in range(4):
            (nc.sync if r < 2 else nc.scalar).dma_start(xs[r:P:32, :].bitcast(I32), x_scales[0, r:16:4, :].bitcast(I32))

        def load_rows(rows, gate, first):
            flat = gate.rearrange("r p (h t) -> (r p h) t", h=2)
            nc.sync.dma_start(rows[first:4, :], flat[2 * P - 2 + first : 2 * P + 2, :])

        load_rows(rows1, gate1, 0)
        xw = keep.tile([P, T], I32, name="xw", align_bytes=64)
        nc.sync.dma_start(xw[:], x_words[0].rearrange("p t d -> p (t d)").bitcast(I32))

        def load_words(e0, ne):
            t = keep.tile([P, ne, 2 * K], U8, name=f"ww{e0}", align_bytes=64)
            nc.sync.dma_start(t[:].bitcast(I32), w_words[e0 : e0 + ne, 0].rearrange("e p n -> p e n").bitcast(I32))
            return [t[:, j, :] for j in range(ne)]

        def load_scales(i):
            for r in range(4):
                src = w_scales[4 * i : 4 * i + 4, 0, r:16:4, :].rearrange("e q n -> q e n")
                nc.sync.dma_start(ws[i][r:P:32, :, :].bitcast(I32), src.bitcast(I32))

        def weight_scales(e, b):
            return ws[e // 4][:, e % 4, P * b : P * (b + 1)]

        ww = []
        for i in range(3):
            ww = ww + load_words(4 * i, 4)
            load_scales(i)
        l_pos1 = load_list(pos1, "l_pos1")
        l_pos2 = load_list(pos2, "l_pos2")
        l_offs2 = load_list(offs2, "l_offs2")
        l_pos3 = load_list(pos3, "l_pos3")
        l_pos4 = load_list(pos4, "l_pos4")
        q2 = keep.tile([P, T], F32, name="q2")
        nc.sync.dma_start(q2[:], gate2[1])
        q1 = keep.tile([P, T], F32, name="q1")
        nc.sync.dma_start(q1[:], gate2[0])

        def gate_columns(rows, at):
            bank = bank_tile(at, [P, 3, P])
            for j in range(3):
                nc.tensor.transpose(bank[:, j, :], rows[:, j * P : (j + 1) * P], ident[:])
            return bank[:, :, 0:4].rearrange("p j (r h) -> p j r h", r=2)

        turned = gate_columns(rows1, 0)
        cols = keep.tile([P, 3, 2, 2], F32, name="cols")
        cols2 = keep.tile([P, 3, 2], F32, name="cols2")
        nc.scalar.activation(cols[:], turned, COPY, bias=TINY)
        rec = keep.tile([P, 3, 2], F32, name="rec")
        minus = keep.tile([P, 3, 2], F32, name="minus")
        nc.gpsimd.memset(minus[:], -1.0)
        nc.gpsimd.tensor_tensor(rec[:], cols[:, :, 1, :], minus[:], POW)
        rcol = keep.tile([P, 3, 2], F32, name="rcol")
        nc.gpsimd.tensor_tensor(rcol[:], cols[:, :, 0, :], rec[:], MULT)
        rows2 = keep.tile([P, T // 2], F32, name="rows2")
        nc.gpsimd.memset(rows2[:], 0.0)
        load_rows(rows2, gate2, 2)

        def factor(step, j):
            return (cols2[:] if step else cols[:, :, 1, :])[:, j % 3, j // 3 : j // 3 + 1]

        def product(planes, operands, b, e0, ne, at):
            acc = bank_tile(at, [P, ne * C])
            for j in range(ne):
                e = e0 + j
                words, scales = operands[e]
                nc.tensor.matmul_mx(
                    out=acc[:, j * C : (j + 1) * C],
                    lhsT=ww[e][:, 256 * b : 256 * (b + 1)].bitcast(FP4X4),
                    lhsT_scale=weight_scales(e, b),
                    rhs=words.bitcast(FP8X4),
                    rhs_scale=scales,
                    start=True,
                    stop=True,
                )
            nc.scalar.activation(planes[b][:, e0 * C : (e0 + ne) * C], acc[:], SILU)

        def gathered(name, n, at):
            if at is None:
                return keep.tile([P, n], F32, name=name)
            return ring.tile([P, n], F32, name=name, align_bytes=64, offset=at)

        def times_ratio(y, lst, ratio, t0, n, name, at=None):
            a = gathered(name, n, at)
            nc.vector.tensor_tensor(a[:], y[:].indirect(part(lst, t0, n)), ratio[:, t0 : t0 + n], MULT)
            return a

        def plus(y, lst, a, t0, n, name, at=None):
            s = gathered(name, n, at)
            nc.vector.tensor_tensor(s[:], y[:].indirect(part(lst, t0, n)), a, ADD)
            return s

        def plain(y, lst, t0, n, name, at=None):
            b = gathered(name, n, at)
            nc.scalar.activation(b[:], y[:].indirect(part(lst, t0, n)), COPY)
            return b

        def turn(dst, src, start, stop):
            nc.tensor.matmul(dst, src, ident[:], start=start, stop=stop, is_transpose=True)

        gs = [
            early.tile([P, n], U8, name=f"gs{i}", align_bytes=64, offset=s0)
            for i, (s0, n) in enumerate(zip(starts(BYTES1), BYTES1))
        ]
        gw = [
            early.tile([P, n], U32, name=f"gw{i}", align_bytes=64, offset=S + 4 * s0)
            for i, (s0, n) in enumerate(zip(starts(WORDS1), WORDS1))
        ]
        for i, (s0, n) in enumerate(zip(starts(WORDS1), WORDS1)):
            if s0 % 512 == 0:
                nc.vector.tensor_copy(gs[s0 // 512][:], xs[:].indirect(part(l_offs, s0, 512)))
            nc.vector.tensor_copy(gw[i][:], xw[:].bitcast(U32).indirect(part(l_offs, s0, n)))

        def by_expert(tiles, widths):
            return [t[:, j : j + C] for t, n in zip(tiles, widths) for j in range(0, n, C)]

        operands = list(zip(by_expert(gw, WORDS1), by_expert(gs, BYTES1)))
        y = [keep.tile([P, S], F32, name=f"y{b}") for b in range(4)]
        for i, (b, e0, ne) in enumerate(ORDER1):
            product(y, operands, b, e0, ne, (1, 2, 3, 4, 6, 7)[i] if i < 6 else (i - 1) % 6)
            if i == 5:
                ratio1 = spread(rcol, 0, 6)

        ct = {}
        cw = [keep.tile([P, T], F32, name=f"cw{u}", align_bytes=64) for u in range(2)]
        tok = [bank_tile(j, [P, 4, P]) for j in range(NB)]

        def turn1(src, b, t0, n, start=False, stop=False):
            for m in range(n // P):
                turn(tok[t0 // P + m][:, b, :], src[:, m * P : (m + 1) * P], start, stop)

        def round1(u, j, eng, at=None):
            at = 4608 + 1024 * j + 512 * u if at is None else at
            ct[u, j] = ring.tile([P, 256], BF16, name=f"ct{u}{j}", align_bytes=64, offset=at)
            dst = ct[u, j][:].rearrange("p (m e) -> p m e", e=2)
            src = tok[j][:].rearrange("p h (m u e) -> p u (h m) e", u=2, e=2)[:, u]
            if eng == "v":
                nc.vector.tensor_scalar(dst, src, factor(0, j), None, MULT)
            else:
                nc.scalar.activation(dst, src, COPY, scale=factor(0, j))

        def back1(bank, t0, u, j):
            m = j - t0 // P
            nc.tensor.transpose(bank[:, m * P : (m + 1) * P], ct[u, j][:].bitcast(F32), ident[:])

        def words1(bank, t0, n, u, eng):
            if eng == "v":
                nc.vector.tensor_copy(cw[u][:, t0 : t0 + n], bank[:])
            else:
                nc.scalar.copy(cw[u][:, t0 : t0 + n], bank[:])

        (t0, n0), (t1, n1), (t2, n2) = TAIL
        rest = (t1, n1 + n2)
        for b in range(2):
            turn1(times_ratio(y[b], l_pos1, ratio1, 0, T, f"a{b}"), b, 0, T, start=b == 0)
            turn1(plain(y[b], l_pos2, 0, T, f"b{b}"), b, 0, T)
        a2 = times_ratio(y[2], l_pos1, ratio1, 0, T, "a2")
        turn1(a2[:, SUMMED:T], 2, SUMMED, T - SUMMED)
        turn1(plus(y[2], l_pos2, a2[:, 0:SUMMED], 0, SUMMED, "s2"), 2, 0, SUMMED)
        turn1(plain(y[2], l_pos2, SUMMED, T - SUMMED, "b2"), 2, SUMMED, T - SUMMED)
        for k, (t, n) in enumerate(TAIL):
            turn1(times_ratio(y[3], l_pos1, ratio1, t, n, f"a3{k}"), 3, t, n)
            turn1(plain(y[3], l_pos2, t, n, f"b3{k}", (None, 0, 1280)[k]), 3, t, n, stop=True)
        first = [bank_tile(6, [P, n0]), bank_tile(7, [P, n1])]
        for j, eng in enumerate("vsvs"):
            round1(0, j, eng)
            back1(first[j // 3], TAIL[j // 3][0], 0, j)
        round1(0, 5, "v")
        round1(0, 4, "s")
        round1(1, 0, "v", 1024)
        first.append(bank_tile(0, [P, n2]))
        back1(first[1], t1, 0, 4)
        back1(first[2], t2, 0, 5)
        round1(1, 2, "s", 0)
        round1(1, 1, "v", 1536)
        for k, eng in enumerate("ssv"):
            words1(first[k], *TAIL[k], 0, eng)
        second0 = bank_tile(2, [P, n0])
        second1 = bank_tile(1, [P, n1 + n2])
        for j in range(NB):
            if j > 2:
                round1(1, j, "s")
            back1(second0 if j < 3 else second1, t0 if j < 3 else t1, 1, j)
        words1(second0, t0, n0, 1, "s")
        words1(second1, *rest, 1, "s")

        qw = keep.tile([P, S], U32, name="qw", align_bytes=64)
        qs = keep.tile([P, S], U8, name="qs", align_bytes=64)

        def pairs(dst, u, s0, n):
            nc.vector.tensor_copy(dst, cw[u][:].bitcast(U32).indirect(part(l_offs2, s0, n)))

        def planes_tile(name, n, at):
            return mid.tile([P, 2, n], U32, name=name, align_bytes=64, offset=at)

        def woven_tile(name, n, at):
            return mid.tile([P, n, 2], U32, name=name, align_bytes=64, offset=at)

        def quantise(woven, k):
            s0, n = CHUNKS[k]
            src = woven[:].rearrange("p n u -> p (n u)").bitcast(BF16)
            nc.vector.quantize_mx(out=qw[:, s0 : s0 + n].bitcast(FP8X4), scales=qs[:, s0 : s0 + n], in_=src)

        operands = [(qw[:, e * C : (e + 1) * C], qs[:, e * C : (e + 1) * C]) for e in range(E)]
        z = [keep.tile([P, S], F32, name=f"z{b}") for b in range(4)]
        turns = [3]

        def product2(b, s0, n):
            product(z, operands, b, s0 // C, n // C, turns[0] % 8)
            turns[0] = turns[0] + 1

        planes_at = (0, 2048, 0, 2048)
        woven_at = (6144, 8192, 11264, 12288, 0)
        woven = []

        def weave(k, planes, shared):
            n = CHUNKS[k][1]
            woven.append(woven_tile(f"woven{k}", n, woven_at[k]))
            src = planes[:].rearrange("p u n -> p n u")
            if shared:
                nc.gpsimd.tensor_copy(woven[k][:, 0:shared, :], src[:, 0:shared, :])
            nc.scalar.copy(woven[k][:, shared:n, :], src[:, shared:n, :])

        def both(k):
            pl = planes_tile(f"pl{k}", CHUNKS[k][1], planes_at[k])
            for u in range(2):
                pairs(pl[:, u, :], u, *CHUNKS[k])
            return pl

        lead = [planes_tile(f"pl{k}", CHUNKS[k][1], planes_at[k]) for k in range(2)]
        for k in range(2):
            pairs(lead[k][:, 0, :], 0, *CHUNKS[k])
        for k in range(2):
            pairs(lead[k][:, 1, :], 1, *CHUNKS[k])
            weave(k, lead[k], 0)
        nc.scalar.copy(cols2[:], gate_columns(rows2, 1)[:, :, 1, :])
        quantise(woven[0], 0)
        pl = both(2)
        quantise(woven[1], 1)
        weave(2, pl, SHARED)
        for b in range(4):
            product2(b, *CHUNKS[0])
        pl = both(3)
        quantise(woven[2], 2)
        weave(3, pl, SHARED)
        for b in range(4):
            product2(b, *CHUNKS[1])
        woven.append(woven_tile("woven4", 256, woven_at[4]))
        for u in range(2):
            pairs(woven[4][:, :, u], u, *CHUNKS[4])
        quantise(woven[3], 3)
        quantise(woven[4], 4)
        for b in range(3):
            product2(b, *CHUNKS[2])
        for k in (3, 4):
            product2(0, *CHUNKS[k])
        product2(1, 1024, 512)
        d0 = plain(z[0], l_pos4, 0, T, "d0", 3072)

        H = T // 2
        halves = ((0, H), (H, H))

        def there(src, at, t0, n):
            bank = bank_tile(at % 8, [P, n])
            for m in range(n // P):
                nc.tensor.transpose(bank[:, m * P : (m + 1) * P], src[:, t0 + m * P : t0 + (m + 1) * P], ident[:])
            return bank

        def again(bank, at, t0, n, name, place=None):
            st = gathered(name, n, place)
            back = bank_tile(at % 8, [P, n])
            for m in range(n // P):
                cut = slice(m * P, (m + 1) * P)
                nc.scalar.activation(st[:, cut], bank[:, cut], COPY, scale=factor(1, t0 // P + m))
            for m in range(n // P):
                cut = slice(m * P, (m + 1) * P)
                nc.tensor.transpose(back[:, cut], st[:, cut], ident[:])
            return back

        def finish(back, first, b, t0, n, origin=0):
            res = keep.tile([P, n], F32, name=f"res{b}_{t0}")
            nc.vector.tensor_tensor(res[:], back[:], first[:, t0 - origin : t0 - origin + n], ADD)
            nc.sync.dma_start(out[b * P : (b + 1) * P, t0 : t0 + n], res[:])

        def added(k, place):
            t0, n = halves[k]
            e = times_ratio(z[1], l_pos4, q2, t0, n, f"e1{k}", place)
            res = keep.tile([P, n], F32, name=f"res1{k}")
            nc.gpsimd.tensor_tensor(res[:], c1[:, t0 : t0 + n], e[:], ADD)
            return lambda: nc.sync.dma_start(out[P : 2 * P, t0 : t0 + n], res[:])

        at = turns[0]
        c0 = times_ratio(z[0], l_pos3, q1, 0, T, "c0")
        tb0 = [there(d0, at + k, *halves[k]) for k in range(2)]
        c1 = times_ratio(z[1], l_pos3, q1, 0, T, "c1")
        product(z, operands, 2, 8, 4, (at + 4) % 8)
        c2 = times_ratio(z[2], l_pos3, q1, 0, T, "c2")
        bk0 = [again(tb0[k], at + 2 + k, *halves[k], f"st0{k}", 1536 * k) for k in range(2)]
        store = added(0, 0)
        for k in range(2):
            finish(bk0[k], c0, 0, *halves[k])
        store()
        d2 = plain(z[2], l_pos4, 0, T, "d2", 3072)
        tb2 = [there(d2, at + 5 + k, *halves[k]) for k in range(2)]
        product(z, operands, 3, 6, 2, at % 8)
        product(z, operands, 3, 8, 4, (at + 1) % 8)
        bk2 = [again(tb2[k], at + 2 + k, *halves[k], f"st2{k}", 6144 + 1536 * k) for k in range(2)]
        c3 = [times_ratio(z[3], l_pos3, q1, *halves[0], "c30")]
        store = added(1, 3072)
        for k in range(2):
            finish(bk2[k], c2, 2, *halves[k])
        store()
        c3.append(times_ratio(z[3], l_pos3, q1, *halves[1], "c31", 7680))

        def second3(k):
            t0, n = TAIL[k]
            d3 = plain(z[3], l_pos4, t0, n, f"d3{k}", (4608, 6144, 7168)[k])
            return there(d3, at + (7, 0, 4)[k], 0, n)

        tb3 = [second3(0), second3(1)]
        bk3 = [again(tb3[0], at + 1, *TAIL[0], "st30")]
        tb3.append(second3(2))
        bk3 = bk3 + [again(tb3[k], at + 4 + k, *TAIL[k], f"st3{k}") for k in (1, 2)]
        for k in range(3):
            t0, n = TAIL[k]
            finish(bk3[k], c3[t0 // H], 3, t0, n, H * (t0 // H))
